import numpy as np
import ml_dtypes


def mxq(x, axis, fmt="e4m3"):
    dtype, down = {"e4m3": (ml_dtypes.float8_e4m3fn, 7), "e5m2": (ml_dtypes.float8_e5m2, 14)}[fmt]
    v = np.moveaxis(np.asarray(x, np.float32).astype(ml_dtypes.bfloat16).astype(np.float64), axis, -1)
    blocks = v.reshape(v.shape[:-1] + (-1, 32))
    amax = np.abs(blocks).max(-1, keepdims=True)
    byte = np.maximum(np.where(amax > 0, np.frexp(amax)[1] - 1 + 127, 0) - down, 1)
    scale = np.exp2(byte - 127.0)
    codes = (blocks / scale).astype(np.float32).astype(dtype).astype(np.float64)
    return np.moveaxis((codes * scale).reshape(v.shape), -1, axis)


WIDE = False


def mx_kscale(k):
    if not WIDE:
        return np.ones(k)
    levels = np.array([18, -18])
    if k % 512:
        return np.exp2(np.random.permutation(np.resize(levels, k // 32))).repeat(32)
    a = np.empty((k // 512, 16))
    for p in range(k // 512):
        a[p, :8] = np.random.permutation(np.resize(levels, 8))
        for g in range(8):
            far = levels[np.abs(levels - a[p, g]) >= 10]
            a[p, g + 8] = far[np.random.randint(len(far))]
    return np.exp2(a.ravel()).repeat(32)


def f64(x):
    return np.asarray(x).astype(np.float64)


def striped(idx):
    return np.tile(np.asarray(idx).reshape(-1, 16).T, (8, 1)).astype(np.uint16)


def unstriped(offs):
    return offs[:16].T.reshape(-1).astype(np.int64)


E2M1 = np.array([0.0, 0.5, 1.0, 1.5, 2.0, 3.0, 4.0, 6.0, -0.0, -0.5, -1.0, -1.5, -2.0, -3.0, -4.0, -6.0])


def pack_weight(w, fmt):
    k, n = w.shape
    w = f64(np.asarray(w, np.float32).astype(ml_dtypes.bfloat16)).reshape(k // 32, 32, n)
    amax = np.abs(w).max(1)
    if fmt == "e4m3":
        byte = np.frexp(amax)[1] - 1 + 127 - 7
    else:
        mant, ex = np.frexp(amax / 6.0)
        byte = np.where(mant > 0.5, ex, ex - 1) + 127
    byte = np.clip(np.where(amax > 0, byte, 1), 1, 254)
    scaled = (w * np.exp2(127.0 - byte)[:, None, :]).reshape(k, n).astype(np.float32)
    by_word = np.ascontiguousarray(scaled.reshape(k // 512, 128, 4, n).transpose(0, 1, 3, 2))
    if fmt == "e4m3":
        words = by_word.astype(ml_dtypes.float8_e4m3fn).view(np.uint8)
    else:
        c = by_word.astype(ml_dtypes.float4_e2m1fn).view(np.uint8) & 0xF
        words = (c[..., 0::2] | (c[..., 1::2] << 4)).reshape(k // 512, 128, 2 * n)
    return np.ascontiguousarray(words), np.ascontiguousarray(byte.astype(np.uint8).reshape(k // 512, 16, n))


def unpack_weight(words, scales, fmt):
    g, _, n = scales.shape
    words = np.ascontiguousarray(words).reshape(g, 128, n, -1)
    if fmt == "e4m3":
        vals = words.view(ml_dtypes.float8_e4m3fn).astype(np.float64)
    else:
        nib = np.empty((g, 128, n, 4), np.uint8)
        nib[..., 0::2] = words & 0xF
        nib[..., 1::2] = words >> 4
        vals = E2M1[nib]
    vals = vals * np.repeat(np.exp2(scales.astype(np.float64) - 127.0), 8, axis=1)[..., None]
    return vals.transpose(0, 1, 3, 2).reshape(g * 512, n)


B, N, T, D, R = 1, 512, 2048, 512, 1024


def setup_inputs():
    n = np.random.standard_normal
    idx = np.random.permutation(T)[:B * N]
    s = mx_kscale(D)[:, None]
    z = mx_kscale(R)[:, None]
    x = n((B, D, R))
    wp = pack_weight(n((D, T)) * (0.50 / np.sqrt(D)) / s, "e4m3")
    return {
        "xT": (x * s).astype(np.float32),
        "w_words": wp[0],
        "w_scales": wp[1],
        "y": np.exp(n((B, R, N))).astype(np.float32),
        "wt": (np.random.uniform(0.5, 1.5, (B, R, 1)) * 1.0 / np.sqrt(R) * z).astype(np.float32),
        "xm": (x.transpose(0, 2, 1) / z).astype(np.float32),
        "offs": striped(idx),
    }


def reference(xT, w_words, w_scales, y, wt, xm, offs):
    idx = unstriped(offs)
    w = unpack_weight(w_words, w_scales, "e4m3")
    pick = lambda x: x[:, idx].reshape(x.shape[0], B, N).transpose(1, 0, 2)
    a = mxq(f64(xT), 1, "e4m3").transpose(0, 2, 1) @ pick(w)
    g = f64(wt) * (np.exp(a) - f64(y))
    dw = mxq(f64(xm), 1, "e4m3").transpose(0, 2, 1) @ mxq(g, 1, "e5m2")
    gw = np.zeros((D, T))
    gw[:, idx] = dw.transpose(1, 0, 2).reshape(D, B * N)
    return gw

@@ -1,0 +1,230 @@
+from contextlib import ExitStack
+
+import concourse.mybir as mybir
+
+D, R, N, T = 512, 1024, 512, 2048
+FLOPS = 2 * 2 * D * R * N
+
+F32 = mybir.dt.float32
+BF16 = mybir.dt.bfloat16
+I32 = mybir.dt.int32
+U32 = mybir.dt.uint32
+U16 = mybir.dt.uint16
+U8 = mybir.dt.uint8
+E4M3 = mybir.dt.float8_e4m3fn_x4
+E5M2 = mybir.dt.float8_e5m2_x4
+EXP = mybir.ActivationFunctionType.Exp
+SUB = mybir.AluOpType.subtract
+MUL = mybir.AluOpType.mult
+
+P = 128
+PACK = 4
+K_PASS = P * PACK
+PASSES = R // K_PASS
+SLOT_BLOCK = 128
+SLOT_BLOCKS = N // SLOT_BLOCK
+D_BLOCKS = D // P
+HALF = 256
+
+
+def tile_attend_gpoi_w_kernel(tc, xT, w_words, w_scales, y, wt, xm, offs, out):
+    nc = tc.nc
+    with ExitStack() as ctx:
+        keep = ctx.enter_context(tc.tile_pool(name="keep", bufs=1))
+        ring = ctx.enter_context(tc.tile_pool(name="ring", bufs=3))
+        psum_a = ctx.enter_context(tc.psum_pool(name="psum_a", bufs=4))
+        psum_dw = ctx.enter_context(tc.psum_pool(name="psum_dw", bufs=4))
+
+        offsets = keep.tile([P, N // 16], U16)
+        table_words = keep.tile([P, T], I32, align_bytes=64)
+        table_scales = keep.tile([P, T // 4], I32, align_bytes=64)
+        wt_sb = keep.tile([P, PASSES, PACK], F32)
+        xT_raw = [[keep.tile([P, PACK, HALF], F32, name=f"xT_raw{o}{h}") for h in range(2)] for o in range(PASSES)]
+        y_sb = [[keep.tile([P, PACK, HALF], F32, name=f"y_sb{o}{h}") for h in range(2)] for o in range(PASSES)]
+        xm_raw = [[keep.tile([P, PACK, HALF], F32, name=f"xm_raw{o}{h}") for h in range(2)] for o in range(PASSES)]
+        windows = [keep.tile([P, T], F32, name=f"window{c}") for c in range(D_BLOCKS)]
+
+        xT_v = xT[0].rearrange("(p j) r -> p j r", j=PACK)
+        y_v = y[0].rearrange("(o p t) i -> o p t i", o=PASSES, t=PACK)
+        xm_v = xm[0].rearrange("(o p t) d -> o p t d", o=PASSES, t=PACK)
+
+        def load_xT(o, h):
+            r0 = o * K_PASS + h * HALF
+            nc.sync.dma_start(out=xT_raw[o][h][:], in_=xT_v[:, :, r0 : r0 + HALF])
+
+        def load_y(o, h):
+            nc.sync.dma_start(out=y_sb[o][h][:], in_=y_v[o, :, :, h * HALF : (h + 1) * HALF])
+
+        def load_xm(o, h):
+            nc.sync.dma_start(out=xm_raw[o][h][:], in_=xm_v[o, :, :, h * HALF : (h + 1) * HALF])
+
+        nc.vector.memset(table_scales[:], 0)
+        nc.sync.dma_start(offsets[:], offs)
+        load_xT(0, 0)
+        scale_rows = w_scales[0].bitcast(I32)
+        for q in range(4):
+            nc.sync.dma_start(out=table_scales[32 * q : 32 * q + 4, :], in_=scale_rows[4 * q : 4 * q + 4, :])
+        load_xT(0, 1)
+        nc.sync.dma_start(out=table_words[:], in_=w_words[0].rearrange("p n t -> p (n t)").bitcast(I32))
+        nc.scalar.dma_start(out=wt_sb[:], in_=wt[0].rearrange("(o p t) one -> p o (t one)", o=PASSES, t=PACK))
+        load_y(0, 0)
+        load_xT(1, 0)
+        load_xT(1, 1)
+        load_y(0, 1)
+        load_y(1, 0)
+        load_y(1, 1)
+        for h in range(2):
+            for o in range(PASSES):
+                load_xm(o, h)
+
+        for c in range(D_BLOCKS):
+            nc.vector.memset(windows[c][:], 0.0)
+
+        w_codes = keep.tile([P, N], U32, align_bytes=64)
+        w_sc = keep.tile([P, N], U8, align_bytes=64)
+        xT_bf = [keep.tile([P, PACK, P, PACK], BF16, align_bytes=64, name=f"xT_bf{o}") for o in range(PASSES)]
+        xT_codes = [keep.tile([P, K_PASS], U32, align_bytes=64, name=f"xT_codes{o}") for o in range(PASSES)]
+        xT_sc = [keep.tile([P, K_PASS], U8, align_bytes=64, name=f"xT_sc{o}") for o in range(PASSES)]
+        xm_codes = [keep.tile([P, D], U32, align_bytes=64, name=f"xm_codes{o}") for o in range(PASSES)]
+        xm_sc = [keep.tile([P, D], U8, align_bytes=64, name=f"xm_sc{o}") for o in range(PASSES)]
+        g_codes = [keep.tile([P, N], U32, align_bytes=64, name=f"g_codes{o}") for o in range(PASSES)]
+        g_sc = [keep.tile([P, N], U8, align_bytes=64, name=f"g_sc{o}") for o in range(PASSES)]
+
+        def round_xT(o, h):
+            m = slice(h * (P // 2), (h + 1) * (P // 2))
+            nc.scalar.copy(
+                out=xT_bf[o][:, :, m, :].rearrange("p t m j -> p m j t"),
+                in_=xT_raw[o][h][:].rearrange("p j (m t) -> p m j t", t=PACK),
+            )
+
+        def quantize_xT(o):
+            nc.vector.quantize_mx(
+                out=xT_codes[o][:].bitcast(E4M3),
+                scales=xT_sc[o][:],
+                in_=xT_bf[o][:].rearrange("p t m j -> p (t m j)"),
+            )
+
+        def gather_words(h):
+            nc.vector.tensor_copy(
+                w_codes[:, h * HALF : (h + 1) * HALF],
+                table_words[:].bitcast(U32).indirect(offsets[:, h * HALF // 16 : (h + 1) * HALF // 16]),
+            )
+
+        def means(o, q):
+            cols = slice(q * SLOT_BLOCK, (q + 1) * SLOT_BLOCK)
+            a = psum_a.tile([P, PACK, SLOT_BLOCK], F32, name="a")
+            for t in range(PACK):
+                rows = slice(t * P, (t + 1) * P)
+                nc.tensor.matmul_mx(
+                    out=a[:, t, :],
+                    lhsT=xT_codes[o][:, rows].bitcast(E4M3),
+                    lhsT_scale=xT_sc[o][:, rows],
+                    rhs=w_codes[:, cols].bitcast(E4M3),
+                    rhs_scale=w_sc[:, cols],
+                    start=True,
+                    stop=True,
+                )
+            mean = ring.tile([P, PACK, SLOT_BLOCK], F32, name="mean")
+            nc.scalar.activation(out=mean[:], in_=a[:], func=EXP)
+            return mean
+
+        def residual(o, q, mean):
+            h, i0 = divmod(q * SLOT_BLOCK, HALF)
+            resid = ring.tile([P, PACK, SLOT_BLOCK], F32, name="resid")
+            nc.vector.tensor_tensor(resid[:], mean[:], y_sb[o][h][:, :, i0 : i0 + SLOT_BLOCK], SUB)
+            return resid
+
+        def weigh(o, resid):
+            g_bf = ring.tile([P, SLOT_BLOCK, PACK], BF16, align_bytes=64, name="g_bf")
+            nc.vector.tensor_tensor(
+                g_bf[:].rearrange("p (c i) t -> p c t i", i=4),
+                resid[:].rearrange("p t (c i) -> p c t i", i=4),
+                wt_sb[:, o, :].unsqueeze(1).unsqueeze(3).to_broadcast([P, SLOT_BLOCK // 4, PACK, 4]),
+                MUL,
+            )
+            return g_bf
+
+        def quantize_g(o, q, g_bf):
+            cols = slice(q * SLOT_BLOCK, (q + 1) * SLOT_BLOCK)
+            nc.vector.quantize_mx(
+                out=g_codes[o][:, cols].bitcast(E5M2),
+                scales=g_sc[o][:, cols],
+                in_=g_bf[:].rearrange("p i t -> p (i t)"),
+            )
+
+        def round_xm(o, h):
+            xm_bf = ring.tile([P, HALF, PACK], BF16, align_bytes=64, name="xm_bf", bufs=4)
+            nc.scalar.copy(
+                out=xm_bf[:].rearrange("p (c i) t -> p c t i", i=4),
+                in_=xm_raw[o][h][:].rearrange("p t (c i) -> p c t i", i=4),
+            )
+            return xm_bf
+
+        def quantize_xm(o, h, xm_bf):
+            cols = slice(h * HALF, (h + 1) * HALF)
+            nc.vector.quantize_mx(
+                out=xm_codes[o][:, cols].bitcast(E4M3),
+                scales=xm_sc[o][:, cols],
+                in_=xm_bf[:].rearrange("p d t -> p (d t)"),
+            )
+
+        nc.vector.tensor_copy(w_sc[:], table_scales[:].bitcast(U8).indirect(offsets[:]))
+        round_xT(0, 0)
+        round_xT(0, 1)
+        quantize_xT(0)
+        gather_words(0)
+        gather_words(1)
+
+        units = [(o, q) for o in range(PASSES) for q in range(SLOT_BLOCKS)]
+        mean_of, resid_of, g_of, xm_of = {}, {}, {}, {}
+        for step in range(len(units) + 3):
+            if step == 3:
+                round_xT(1, 0)
+                round_xT(1, 1)
+                quantize_xT(1)
+            if step < len(units):
+                mean_of[step] = means(*units[step])
+            if 0 <= step - 1 < len(units):
+                resid_of[step - 1] = residual(*units[step - 1], mean_of[step - 1])
+            if 0 <= step - 2 < len(units):
+                g_of[step - 2] = weigh(units[step - 2][0], resid_of[step - 2])
+            if step == len(units):
+                for o in range(PASSES):
+                    xm_of[o] = round_xm(o, 0)
+            if step == len(units) + 2:
+                for o in range(PASSES):
+                    quantize_xm(o, 0, xm_of[o])
+            if 0 <= step - 3 < len(units):
+                quantize_g(*units[step - 3], g_of[step - 3])
+
+        def products(c):
+            cols = slice(c * P, (c + 1) * P)
+            dw = psum_dw.tile([P, N], F32, name="dw")
+            for o in range(PASSES):
+                nc.tensor.matmul_mx(
+                    out=dw[:],
+                    lhsT=xm_codes[o][:, cols].bitcast(E4M3),
+                    lhsT_scale=xm_sc[o][:, cols],
+                    rhs=g_codes[o][:].bitcast(E5M2),
+                    rhs_scale=g_sc[o][:],
+                    start=(o == 0),
+                    stop=(o == PASSES - 1),
+                )
+            dw_sb = ring.tile([P, N], F32, name="dw_sb", bufs=4)
+            nc.scalar.copy(out=dw_sb[:], in_=dw[:])
+            return dw_sb
+
+        def place(c, dw_sb):
+            nc.vector.tensor_copy(windows[c][:].indirect(offsets[:]), dw_sb[:])
+            nc.sync.dma_start(out=out[c * P : (c + 1) * P, :], in_=windows[c][:])
+
+        first = [products(c) for c in range(2)]
+        for o in range(PASSES):
+            xm_of[o] = round_xm(o, 1)
+        place(0, first[0])
+        for o in range(PASSES):
+            quantize_xm(o, 1, xm_of[o])
+        second = [products(c) for c in range(2, 4)]
+        place(1, first[1])
+        place(2, second[0])
+        place(3, second[1])

@@ -13,6 +13,7 @@ U16 = mybir.dt.uint16
 U8 = mybir.dt.uint8
 E4M3 = mybir.dt.float8_e4m3fn_x4
 E5M2 = mybir.dt.float8_e5m2_x4
+COPY = mybir.ActivationFunctionType.Copy
 EXP = mybir.ActivationFunctionType.Exp
 SUB = mybir.AluOpType.subtract
 MUL = mybir.AluOpType.mult
@@ -21,10 +22,9 @@ P = 128
 PACK = 4
 K_PASS = P * PACK
 PASSES = R // K_PASS
-SLOT_BLOCK = 128
-SLOT_BLOCKS = N // SLOT_BLOCK
 D_BLOCKS = D // P
 HALF = 256
+WINDOWS = 3
 
 
 def tile_attend_gpoi_w_kernel(tc, xT, w_words, w_scales, y, wt, xm, offs, out):
@@ -42,7 +42,7 @@ def tile_attend_gpoi_w_kernel(tc, xT, w_words, w_scales, y, wt, xm, offs, out):
         xT_raw = [[keep.tile([P, PACK, HALF], F32, name=f"xT_raw{o}{h}") for h in range(2)] for o in range(PASSES)]
         y_sb = [[keep.tile([P, PACK, HALF], F32, name=f"y_sb{o}{h}") for h in range(2)] for o in range(PASSES)]
         xm_raw = [[keep.tile([P, PACK, HALF], F32, name=f"xm_raw{o}{h}") for h in range(2)] for o in range(PASSES)]
-        windows = [keep.tile([P, T], F32, name=f"window{c}") for c in range(D_BLOCKS)]
+        windows = [keep.tile([P, T], F32, name=f"window{c}") for c in range(WINDOWS)]
 
         xT_v = xT[0].rearrange("(p j) r -> p j r", j=PACK)
         y_v = y[0].rearrange("(o p t) i -> o p t i", o=PASSES, t=PACK)
@@ -58,7 +58,7 @@ def tile_attend_gpoi_w_kernel(tc, xT, w_words, w_scales, y, wt, xm, offs, out):
         def load_xm(o, h):
             nc.sync.dma_start(out=xm_raw[o][h][:], in_=xm_v[o, :, :, h * HALF : (h + 1) * HALF])
 
-        nc.vector.memset(table_scales[:], 0)
+        nc.gpsimd.memset(table_scales[:], 0)
         nc.sync.dma_start(offsets[:], offs)
         load_xT(0, 0)
         scale_rows = w_scales[0].bitcast(I32)
@@ -67,18 +67,20 @@ def tile_attend_gpoi_w_kernel(tc, xT, w_words, w_scales, y, wt, xm, offs, out):
         load_xT(0, 1)
         nc.sync.dma_start(out=table_words[:], in_=w_words[0].rearrange("p n t -> p (n t)").bitcast(I32))
         nc.scalar.dma_start(out=wt_sb[:], in_=wt[0].rearrange("(o p t) one -> p o (t one)", o=PASSES, t=PACK))
-        load_y(0, 0)
         load_xT(1, 0)
+        load_y(0, 0)
         load_xT(1, 1)
         load_y(0, 1)
+        load_xm(0, 0)
         load_y(1, 0)
+        load_xm(1, 0)
         load_y(1, 1)
-        for h in range(2):
-            for o in range(PASSES):
-                load_xm(o, h)
+        load_xm(0, 1)
+        load_xm(1, 1)
 
-        for c in range(D_BLOCKS):
-            nc.vector.memset(windows[c][:], 0.0)
+        nc.vector.memset(windows[0][:].bitcast(I32), 0)
+        for c in range(1, WINDOWS):
+            nc.gpsimd.memset(windows[c][:].bitcast(I32), 0)
 
         w_codes = keep.tile([P, N], U32, align_bytes=64)
         w_sc = keep.tile([P, N], U8, align_bytes=64)
@@ -87,12 +89,15 @@ def tile_attend_gpoi_w_kernel(tc, xT, w_words, w_scales, y, wt, xm, offs, out):
         xT_sc = [keep.tile([P, K_PASS], U8, align_bytes=64, name=f"xT_sc{o}") for o in range(PASSES)]
         xm_codes = [keep.tile([P, D], U32, align_bytes=64, name=f"xm_codes{o}") for o in range(PASSES)]
         xm_sc = [keep.tile([P, D], U8, align_bytes=64, name=f"xm_sc{o}") for o in range(PASSES)]
-        g_codes = [keep.tile([P, N], U32, align_bytes=64, name=f"g_codes{o}") for o in range(PASSES)]
+        g_codes = [keep.tile([P, N], I32, align_bytes=64, name=f"g_codes{o}") for o in range(PASSES)]
         g_sc = [keep.tile([P, N], U8, align_bytes=64, name=f"g_sc{o}") for o in range(PASSES)]
 
-        def round_xT(o, h):
+        nc.gpsimd.memset(g_codes[1][:, HALF:], 0)
+        nc.gpsimd.memset(g_sc[1][:, HALF:], 0)
+
+        def round_xT(o, h, copy):
             m = slice(h * (P // 2), (h + 1) * (P // 2))
-            nc.scalar.copy(
+            copy(
                 out=xT_bf[o][:, :, m, :].rearrange("p t m j -> p m j t"),
                 in_=xT_raw[o][h][:].rearrange("p j (m t) -> p m j t", t=PACK),
             )
@@ -110,13 +115,13 @@ def tile_attend_gpoi_w_kernel(tc, xT, w_words, w_scales, y, wt, xm, offs, out):
                 table_words[:].bitcast(U32).indirect(offsets[:, h * HALF // 16 : (h + 1) * HALF // 16]),
             )
 
-        def means(o, q):
-            cols = slice(q * SLOT_BLOCK, (q + 1) * SLOT_BLOCK)
-            a = psum_a.tile([P, PACK, SLOT_BLOCK], F32, name="a")
-            for t in range(PACK):
-                rows = slice(t * P, (t + 1) * P)
+        def means(o, h, u):
+            cols = slice(h * HALF, (h + 1) * HALF)
+            a = psum_a.tile([P, 2, HALF], F32, name="a")
+            for e in range(2):
+                rows = slice((2 * u + e) * P, (2 * u + e + 1) * P)
                 nc.tensor.matmul_mx(
-                    out=a[:, t, :],
+                    out=a[:, e, :],
                     lhsT=xT_codes[o][:, rows].bitcast(E4M3),
                     lhsT_scale=xT_sc[o][:, rows],
                     rhs=w_codes[:, cols].bitcast(E4M3),
@@ -124,28 +129,25 @@ def tile_attend_gpoi_w_kernel(tc, xT, w_words, w_scales, y, wt, xm, offs, out):
                     start=True,
                     stop=True,
                 )
-            mean = ring.tile([P, PACK, SLOT_BLOCK], F32, name="mean")
+            mean = ring.tile([P, 2, HALF], F32, name="mean", bufs=4)
             nc.scalar.activation(out=mean[:], in_=a[:], func=EXP)
             return mean
 
-        def residual(o, q, mean):
-            h, i0 = divmod(q * SLOT_BLOCK, HALF)
-            resid = ring.tile([P, PACK, SLOT_BLOCK], F32, name="resid")
-            nc.vector.tensor_tensor(resid[:], mean[:], y_sb[o][h][:, :, i0 : i0 + SLOT_BLOCK], SUB)
-            return resid
+        def residual(o, h, u, mean, resid):
+            nc.vector.tensor_tensor(resid[:, 2 * u : 2 * u + 2, :], mean[:], y_sb[o][h][:, 2 * u : 2 * u + 2, :], SUB)
 
         def weigh(o, resid):
-            g_bf = ring.tile([P, SLOT_BLOCK, PACK], BF16, align_bytes=64, name="g_bf")
+            g_bf = ring.tile([P, HALF, PACK], BF16, align_bytes=64, name="g_bf")
             nc.vector.tensor_tensor(
                 g_bf[:].rearrange("p (c i) t -> p c t i", i=4),
                 resid[:].rearrange("p t (c i) -> p c t i", i=4),
-                wt_sb[:, o, :].unsqueeze(1).unsqueeze(3).to_broadcast([P, SLOT_BLOCK // 4, PACK, 4]),
+                wt_sb[:, o, :].unsqueeze(1).unsqueeze(3).to_broadcast([P, HALF // 4, PACK, 4]),
                 MUL,
             )
             return g_bf
 
-        def quantize_g(o, q, g_bf):
-            cols = slice(q * SLOT_BLOCK, (q + 1) * SLOT_BLOCK)
+        def quantize_g(o, h, g_bf):
+            cols = slice(h * HALF, (h + 1) * HALF)
             nc.vector.quantize_mx(
                 out=g_codes[o][:, cols].bitcast(E5M2),
                 scales=g_sc[o][:, cols],
@@ -169,62 +171,92 @@ def tile_attend_gpoi_w_kernel(tc, xT, w_words, w_scales, y, wt, xm, offs, out):
             )
 
         nc.vector.tensor_copy(w_sc[:], table_scales[:].bitcast(U8).indirect(offsets[:]))
-        round_xT(0, 0)
-        round_xT(0, 1)
+        round_xT(0, 0, nc.scalar.copy)
+        round_xT(0, 1, nc.scalar.copy)
         quantize_xT(0)
         gather_words(0)
         gather_words(1)
 
-        units = [(o, q) for o in range(PASSES) for q in range(SLOT_BLOCKS)]
-        mean_of, resid_of, g_of, xm_of = {}, {}, {}, {}
-        for step in range(len(units) + 3):
-            if step == 3:
-                round_xT(1, 0)
-                round_xT(1, 1)
-                quantize_xT(1)
-            if step < len(units):
-                mean_of[step] = means(*units[step])
-            if 0 <= step - 1 < len(units):
-                resid_of[step - 1] = residual(*units[step - 1], mean_of[step - 1])
-            if 0 <= step - 2 < len(units):
-                g_of[step - 2] = weigh(units[step - 2][0], resid_of[step - 2])
-            if step == len(units):
-                for o in range(PASSES):
-                    xm_of[o] = round_xm(o, 0)
-            if step == len(units) + 2:
-                for o in range(PASSES):
-                    quantize_xm(o, 0, xm_of[o])
-            if 0 <= step - 3 < len(units):
-                quantize_g(*units[step - 3], g_of[step - 3])
-
-        def products(c):
-            cols = slice(c * P, (c + 1) * P)
+        def products(c, cols):
+            rows = slice(c * P, (c + 1) * P)
             dw = psum_dw.tile([P, N], F32, name="dw")
             for o in range(PASSES):
                 nc.tensor.matmul_mx(
                     out=dw[:],
-                    lhsT=xm_codes[o][:, cols].bitcast(E4M3),
-                    lhsT_scale=xm_sc[o][:, cols],
+                    lhsT=xm_codes[o][:, rows].bitcast(E4M3),
+                    lhsT_scale=xm_sc[o][:, rows],
                     rhs=g_codes[o][:].bitcast(E5M2),
                     rhs_scale=g_sc[o][:],
                     start=(o == 0),
                     stop=(o == PASSES - 1),
                 )
-            dw_sb = ring.tile([P, N], F32, name="dw_sb", bufs=4)
-            nc.scalar.copy(out=dw_sb[:], in_=dw[:])
+            dw_sb = ring.tile([P, cols.stop - cols.start], F32, name="dw_sb", bufs=4)
+            nc.scalar.copy(out=dw_sb[:], in_=dw[:, cols])
             return dw_sb
 
-        def place(c, dw_sb):
-            nc.vector.tensor_copy(windows[c][:].indirect(offsets[:]), dw_sb[:])
-            nc.sync.dma_start(out=out[c * P : (c + 1) * P, :], in_=windows[c][:])
+        def scatter(c, cols, dw_sb):
+            nc.vector.tensor_copy(
+                windows[c % WINDOWS][:].indirect(offsets[:, cols.start // 16 : cols.stop // 16]), dw_sb[:]
+            )
 
-        first = [products(c) for c in range(2)]
+        def store(c):
+            nc.sync.dma_start(out=out[c * P : (c + 1) * P, :], in_=windows[c % WINDOWS][:])
+
+        lo, hi, both = slice(0, HALF), slice(HALF, N), slice(0, N)
+
+        round_xT(1, 0, nc.vector.tensor_copy)
+        mean = [means(0, 0, u) for u in range(2)]
+        resid00 = ring.tile([P, PACK, HALF], F32, name="resid")
+        residual(0, 0, 0, mean[0], resid00)
+        residual(0, 0, 1, mean[1], resid00)
+        mean = [means(0, 1, u) for u in range(2)]
+        round_xT(1, 1, nc.scalar.copy)
+        g00 = weigh(0, resid00)
+        resid01 = ring.tile([P, PACK, HALF], F32, name="resid")
+        residual(0, 1, 0, mean[0], resid01)
+        quantize_xT(1)
+        residual(0, 1, 1, mean[1], resid01)
+        quantize_g(0, 0, g00)
+        xm00 = round_xm(0, 0)
+        g01 = weigh(0, resid01)
+        mean = [means(1, 0, u) for u in range(2)]
+        xm10 = round_xm(1, 0)
+        resid10 = ring.tile([P, PACK, HALF], F32, name="resid")
+        residual(1, 0, 0, mean[0], resid10)
+        quantize_g(0, 1, g01)
+        residual(1, 0, 1, mean[1], resid10)
+        quantize_xm(0, 0, xm00)
+        g10 = weigh(1, resid10)
+        quantize_xm(1, 0, xm10)
+        quantize_g(1, 0, g10)
+
+        mean = [means(1, 1, u) for u in range(2)]
+        wy = keep.tile([P, PACK, HALF], F32)
+        g11_rows = keep.tile([P, PACK, HALF], BF16)
+        for t in range(PACK):
+            nc.scalar.activation(out=wy[:, t, :], in_=y_sb[1][1][:, t, :], func=COPY, scale=wt_sb[:, 1, t : t + 1])
+        early = [products(c, lo) for c in range(2)]
+        for t in range(PACK):
+            nc.vector.scalar_tensor_tensor(
+                g11_rows[:, t, :], mean[t // 2][:, t % 2, :], wt_sb[:, 1, t : t + 1], wy[:, t, :], MUL, SUB
+            )
+        g11 = ring.tile([P, HALF, PACK], BF16, align_bytes=64, name="g_bf")
+        nc.scalar.copy(
+            out=g11[:].rearrange("p (c i) t -> p c t i", i=4),
+            in_=g11_rows[:].rearrange("p t (c i) -> p c t i", i=4),
+        )
+        scatter(0, lo, early[0])
+        quantize_g(1, 1, g11)
+        late = [products(c, hi) for c in range(2)]
+        xm_hi = [round_xm(o, 1) for o in range(PASSES)]
+        scatter(1, lo, early[1])
+        scatter(0, hi, late[0])
+        store(0)
         for o in range(PASSES):
-            xm_of[o] = round_xm(o, 1)
-        place(0, first[0])
-        for o in range(PASSES):
-            quantize_xm(o, 1, xm_of[o])
-        second = [products(c) for c in range(2, 4)]
-        place(1, first[1])
-        place(2, second[0])
-        place(3, second[1])
+            quantize_xm(o, 1, xm_hi[o])
+        rest = [products(c, both) for c in range(2, D_BLOCKS)]
+        scatter(1, hi, late[1])
+        store(1)
+        for c in range(2, D_BLOCKS):
+            scatter(c, both, rest[c - 2])
+            store(c)

@@ -25,6 +25,7 @@ PASSES = R // K_PASS
 D_BLOCKS = D // P
 HALF = 256
 WINDOWS = 3
+RUN = 4
 
 
 def tile_attend_gpoi_w_kernel(tc, xT, w_words, w_scales, y, wt, xm, offs, out):
@@ -38,7 +39,8 @@ def tile_attend_gpoi_w_kernel(tc, xT, w_words, w_scales, y, wt, xm, offs, out):
         offsets = keep.tile([P, N // 16], U16)
         table_words = keep.tile([P, T], I32, align_bytes=64)
         table_scales = keep.tile([P, T // 4], I32, align_bytes=64)
-        wt_sb = keep.tile([P, PASSES, PACK], F32)
+        wt_rows = keep.tile([P, PASSES, 2 * PACK], F32)
+        wt_sb = wt_rows[:, :, :PACK]
         xT_raw = [[keep.tile([P, PACK, HALF], F32, name=f"xT_raw{o}{h}") for h in range(2)] for o in range(PASSES)]
         y_sb = [[keep.tile([P, PACK, HALF], F32, name=f"y_sb{o}{h}") for h in range(2)] for o in range(PASSES)]
         xm_raw = [[keep.tile([P, PACK, HALF], F32, name=f"xm_raw{o}{h}") for h in range(2)] for o in range(PASSES)]
@@ -66,7 +68,7 @@ def tile_attend_gpoi_w_kernel(tc, xT, w_words, w_scales, y, wt, xm, offs, out):
             nc.sync.dma_start(out=table_scales[32 * q : 32 * q + 4, :], in_=scale_rows[4 * q : 4 * q + 4, :])
         load_xT(0, 1)
         nc.sync.dma_start(out=table_words[:], in_=w_words[0].rearrange("p n t -> p (n t)").bitcast(I32))
-        nc.scalar.dma_start(out=wt_sb[:], in_=wt[0].rearrange("(o p t) one -> p o (t one)", o=PASSES, t=PACK))
+        nc.scalar.dma_start(out=wt_sb, in_=wt[0].rearrange("(o p t) one -> p o (t one)", o=PASSES, t=PACK))
         load_xT(1, 0)
         load_y(0, 0)
         load_xT(1, 1)
@@ -139,9 +141,9 @@ def tile_attend_gpoi_w_kernel(tc, xT, w_words, w_scales, y, wt, xm, offs, out):
         def weigh(o, resid):
             g_bf = ring.tile([P, HALF, PACK], BF16, align_bytes=64, name="g_bf")
             nc.vector.tensor_tensor(
-                g_bf[:].rearrange("p (c i) t -> p c t i", i=4),
-                resid[:].rearrange("p t (c i) -> p c t i", i=4),
-                wt_sb[:, o, :].unsqueeze(1).unsqueeze(3).to_broadcast([P, HALF // 4, PACK, 4]),
+                g_bf[:].rearrange("p (c i) t -> p c t i", i=RUN),
+                resid[:].rearrange("p t (c i) -> p c t i", i=RUN),
+                wt_sb[:, o, :].unsqueeze(1).unsqueeze(3).to_broadcast([P, HALF // RUN, PACK, RUN]),
                 MUL,
             )
             return g_bf
@@ -157,8 +159,8 @@ def tile_attend_gpoi_w_kernel(tc, xT, w_words, w_scales, y, wt, xm, offs, out):
         def round_xm(o, h):
             xm_bf = ring.tile([P, HALF, PACK], BF16, align_bytes=64, name="xm_bf", bufs=4)
             nc.scalar.copy(
-                out=xm_bf[:].rearrange("p (c i) t -> p c t i", i=4),
-                in_=xm_raw[o][h][:].rearrange("p t (c i) -> p c t i", i=4),
+                out=xm_bf[:].rearrange("p (c i) t -> p c t i", i=RUN),
+                in_=xm_raw[o][h][:].rearrange("p t (c i) -> p c t i", i=RUN),
             )
             return xm_bf
 
@@ -177,19 +179,25 @@ def tile_attend_gpoi_w_kernel(tc, xT, w_words, w_scales, y, wt, xm, offs, out):
         gather_words(0)
         gather_words(1)
 
-        def products(c, cols):
+        def gradient_pass(c, o, dw):
             rows = slice(c * P, (c + 1) * P)
+            nc.tensor.matmul_mx(
+                out=dw[:],
+                lhsT=xm_codes[o][:, rows].bitcast(E4M3),
+                lhsT_scale=xm_sc[o][:, rows],
+                rhs=g_codes[o][:].bitcast(E5M2),
+                rhs_scale=g_sc[o][:],
+                start=(o == 0),
+                stop=(o == PASSES - 1),
+            )
+
+        def open_gradient(c):
             dw = psum_dw.tile([P, N], F32, name="dw")
-            for o in range(PASSES):
-                nc.tensor.matmul_mx(
-                    out=dw[:],
-                    lhsT=xm_codes[o][:, rows].bitcast(E4M3),
-                    lhsT_scale=xm_sc[o][:, rows],
-                    rhs=g_codes[o][:].bitcast(E5M2),
-                    rhs_scale=g_sc[o][:],
-                    start=(o == 0),
-                    stop=(o == PASSES - 1),
-                )
+            gradient_pass(c, 0, dw)
+            return dw
+
+        def close_gradient(c, dw, cols):
+            gradient_pass(c, 1, dw)
             dw_sb = ring.tile([P, cols.stop - cols.start], F32, name="dw_sb", bufs=4)
             nc.scalar.copy(out=dw_sb[:], in_=dw[:, cols])
             return dw_sb
@@ -235,7 +243,9 @@ def tile_attend_gpoi_w_kernel(tc, xT, w_words, w_scales, y, wt, xm, offs, out):
         g11_rows = keep.tile([P, PACK, HALF], BF16)
         for t in range(PACK):
             nc.scalar.activation(out=wy[:, t, :], in_=y_sb[1][1][:, t, :], func=COPY, scale=wt_sb[:, 1, t : t + 1])
-        early = [products(c, lo) for c in range(2)]
+        early_open = [open_gradient(c) for c in range(2)]
+        early = [close_gradient(c, early_open[c], lo) for c in range(2)]
+        late_open = [open_gradient(c) for c in range(2)]
         for t in range(PACK):
             nc.vector.scalar_tensor_tensor(
                 g11_rows[:, t, :], mean[t // 2][:, t % 2, :], wt_sb[:, 1, t : t + 1], wy[:, t, :], MUL, SUB
@@ -247,14 +257,15 @@ def tile_attend_gpoi_w_kernel(tc, xT, w_words, w_scales, y, wt, xm, offs, out):
         )
         scatter(0, lo, early[0])
         quantize_g(1, 1, g11)
-        late = [products(c, hi) for c in range(2)]
+        late = [close_gradient(c, late_open[c], hi) for c in range(2)]
         xm_hi = [round_xm(o, 1) for o in range(PASSES)]
         scatter(1, lo, early[1])
         scatter(0, hi, late[0])
         store(0)
-        for o in range(PASSES):
-            quantize_xm(o, 1, xm_hi[o])
-        rest = [products(c, both) for c in range(2, D_BLOCKS)]
+        quantize_xm(0, 1, xm_hi[0])
+        rest_open = [open_gradient(c) for c in range(2, D_BLOCKS)]
+        quantize_xm(1, 1, xm_hi[1])
+        rest = [close_gradient(c, rest_open[c - 2], both) for c in range(2, D_BLOCKS)]
         scatter(1, hi, late[1])
         store(1)
         for c in range(2, D_BLOCKS):

@@ -15,6 +15,7 @@ E4M3 = mybir.dt.float8_e4m3fn_x4
 E5M2 = mybir.dt.float8_e5m2_x4
 COPY = mybir.ActivationFunctionType.Copy
 EXP = mybir.ActivationFunctionType.Exp
+ADD = mybir.AluOpType.add
 SUB = mybir.AluOpType.subtract
 MUL = mybir.AluOpType.mult
 
@@ -32,70 +33,68 @@ def tile_attend_gpoi_w_kernel(tc, xT, w_words, w_scales, y, wt, xm, offs, out):
     nc = tc.nc
     with ExitStack() as ctx:
         keep = ctx.enter_context(tc.tile_pool(name="keep", bufs=1))
-        ring = ctx.enter_context(tc.tile_pool(name="ring", bufs=3))
-        psum_a = ctx.enter_context(tc.psum_pool(name="psum_a", bufs=4))
-        psum_dw = ctx.enter_context(tc.psum_pool(name="psum_dw", bufs=4))
+        psum = ctx.enter_context(tc.psum_pool(name="psum", bufs=1))
+        bank = [psum.tile([P, N], F32, name=f"bank{b}") for b in range(8)]
+
+        def units(name, shape, dtype):
+            return [
+                [keep.tile(shape, dtype, align_bytes=64, name=f"{name}{o}{h}") for h in range(2)]
+                for o in range(PASSES)
+            ]
+
+        def passes(name, shape, dtype):
+            return [keep.tile(shape, dtype, align_bytes=64, name=f"{name}{o}") for o in range(PASSES)]
 
         offsets = keep.tile([P, N // 16], U16)
         table_words = keep.tile([P, T], I32, align_bytes=64)
         table_scales = keep.tile([P, T // 4], I32, align_bytes=64)
         wt_rows = keep.tile([P, PASSES, 2 * PACK], F32)
         wt_sb = wt_rows[:, :, :PACK]
-        xT_raw = [[keep.tile([P, PACK, HALF], F32, name=f"xT_raw{o}{h}") for h in range(2)] for o in range(PASSES)]
-        y_sb = [[keep.tile([P, PACK, HALF], F32, name=f"y_sb{o}{h}") for h in range(2)] for o in range(PASSES)]
-        xm_raw = [[keep.tile([P, PACK, HALF], F32, name=f"xm_raw{o}{h}") for h in range(2)] for o in range(PASSES)]
+        wt_neg = keep.tile([P, PASSES, PACK], F32)
+        xT_raw = units("xT_raw", [P, PACK, HALF], F32)
+        y_sb = units("y_sb", [P, PACK, HALF], F32)
+        xm_raw = units("xm_raw", [P, PACK, HALF], F32)
         windows = [keep.tile([P, T], F32, name=f"window{c}") for c in range(WINDOWS)]
+
+        w_codes = keep.tile([P, N], U32, align_bytes=64)
+        w_sc = keep.tile([P, N], U8, align_bytes=64)
+        xT_bf = passes("xT_bf", [P, PACK, P, PACK], BF16)
+        xT_codes = passes("xT_codes", [P, K_PASS], U32)
+        xT_sc = passes("xT_sc", [P, K_PASS], U8)
+        xm_bf = units("xm_bf", [P, HALF, PACK], BF16)
+        xm_codes = units("xm_codes", [P, HALF], U32)
+        xm_sc = units("xm_sc", [P, HALF], U8)
+        mean = units("mean", [P, PACK, HALF], F32)
+        work = units("work", [P, PACK, HALF], F32)
+        g_rows = units("g_rows", [P, PACK, HALF], BF16)
+        g_bf = units("g_bf", [P, HALF, PACK], BF16)
+        g_codes = passes("g_codes", [P, N], I32)
+        g_sc = passes("g_sc", [P, N], U8)
 
         xT_v = xT[0].rearrange("(p j) r -> p j r", j=PACK)
         y_v = y[0].rearrange("(o p t) i -> o p t i", o=PASSES, t=PACK)
         xm_v = xm[0].rearrange("(o p t) d -> o p t d", o=PASSES, t=PACK)
+        lo, hi, both = slice(0, HALF), slice(HALF, N), slice(0, N)
+        halves = (lo, hi)
+        quarters = (slice(0, P), slice(P, HALF))
 
         def load_xT(o, h):
             r0 = o * K_PASS + h * HALF
             nc.sync.dma_start(out=xT_raw[o][h][:], in_=xT_v[:, :, r0 : r0 + HALF])
 
         def load_y(o, h):
-            nc.sync.dma_start(out=y_sb[o][h][:], in_=y_v[o, :, :, h * HALF : (h + 1) * HALF])
+            nc.sync.dma_start(out=y_sb[o][h][:], in_=y_v[o, :, :, halves[h]])
 
         def load_xm(o, h):
-            nc.sync.dma_start(out=xm_raw[o][h][:], in_=xm_v[o, :, :, h * HALF : (h + 1) * HALF])
+            nc.sync.dma_start(out=xm_raw[o][h][:], in_=xm_v[o, :, :, halves[h]])
 
-        nc.gpsimd.memset(table_scales[:], 0)
-        nc.sync.dma_start(offsets[:], offs)
-        load_xT(0, 0)
-        scale_rows = w_scales[0].bitcast(I32)
-        for q in range(4):
-            nc.sync.dma_start(out=table_scales[32 * q : 32 * q + 4, :], in_=scale_rows[4 * q : 4 * q + 4, :])
-        load_xT(0, 1)
-        nc.sync.dma_start(out=table_words[:], in_=w_words[0].rearrange("p n t -> p (n t)").bitcast(I32))
-        nc.scalar.dma_start(out=wt_sb, in_=wt[0].rearrange("(o p t) one -> p o (t one)", o=PASSES, t=PACK))
-        load_xT(1, 0)
-        load_y(0, 0)
-        load_xT(1, 1)
-        load_y(0, 1)
-        load_xm(0, 0)
-        load_y(1, 0)
-        load_xm(1, 0)
-        load_y(1, 1)
-        load_xm(0, 1)
-        load_xm(1, 1)
+        def load_scales():
+            scale_rows = w_scales[0].bitcast(I32)
+            for q in range(4):
+                nc.sync.dma_start(out=table_scales[32 * q : 32 * q + 4, :], in_=scale_rows[4 * q : 4 * q + 4, :])
 
-        nc.vector.memset(windows[0][:].bitcast(I32), 0)
-        for c in range(1, WINDOWS):
-            nc.gpsimd.memset(windows[c][:].bitcast(I32), 0)
-
-        w_codes = keep.tile([P, N], U32, align_bytes=64)
-        w_sc = keep.tile([P, N], U8, align_bytes=64)
-        xT_bf = [keep.tile([P, PACK, P, PACK], BF16, align_bytes=64, name=f"xT_bf{o}") for o in range(PASSES)]
-        xT_codes = [keep.tile([P, K_PASS], U32, align_bytes=64, name=f"xT_codes{o}") for o in range(PASSES)]
-        xT_sc = [keep.tile([P, K_PASS], U8, align_bytes=64, name=f"xT_sc{o}") for o in range(PASSES)]
-        xm_codes = [keep.tile([P, D], U32, align_bytes=64, name=f"xm_codes{o}") for o in range(PASSES)]
-        xm_sc = [keep.tile([P, D], U8, align_bytes=64, name=f"xm_sc{o}") for o in range(PASSES)]
-        g_codes = [keep.tile([P, N], I32, align_bytes=64, name=f"g_codes{o}") for o in range(PASSES)]
-        g_sc = [keep.tile([P, N], U8, align_bytes=64, name=f"g_sc{o}") for o in range(PASSES)]
-
-        nc.gpsimd.memset(g_codes[1][:, HALF:], 0)
-        nc.gpsimd.memset(g_sc[1][:, HALF:], 0)
+        def load_words():
+            nc.sync.dma_start(out=table_words[:], in_=w_words[0].rearrange("p n t -> p (n t)").bitcast(I32))
 
         def round_xT(o, h, copy):
             m = slice(h * (P // 2), (h + 1) * (P // 2))
@@ -111,162 +110,204 @@ def tile_attend_gpoi_w_kernel(tc, xT, w_words, w_scales, y, wt, xm, offs, out):
                 in_=xT_bf[o][:].rearrange("p t m j -> p (t m j)"),
             )
 
+        def gather_scales():
+            nc.vector.tensor_copy(w_sc[:], table_scales[:].bitcast(U8).indirect(offsets[:]))
+
         def gather_words(h):
             nc.vector.tensor_copy(
-                w_codes[:, h * HALF : (h + 1) * HALF],
+                w_codes[:, halves[h]],
                 table_words[:].bitcast(U32).indirect(offsets[:, h * HALF // 16 : (h + 1) * HALF // 16]),
             )
 
-        def means(o, h, u):
-            cols = slice(h * HALF, (h + 1) * HALF)
-            a = psum_a.tile([P, 2, HALF], F32, name="a")
-            for e in range(2):
-                rows = slice((2 * u + e) * P, (2 * u + e + 1) * P)
-                nc.tensor.matmul_mx(
-                    out=a[:, e, :],
-                    lhsT=xT_codes[o][:, rows].bitcast(E4M3),
-                    lhsT_scale=xT_sc[o][:, rows],
-                    rhs=w_codes[:, cols].bitcast(E4M3),
-                    rhs_scale=w_sc[:, cols],
-                    start=True,
-                    stop=True,
+        def means(o, h, banks):
+            cols = halves[h]
+            for u, b in banks.items():
+                a = bank[b][:].rearrange("p (e i) -> p e i", e=2)
+                for e in range(2):
+                    rows = slice((2 * u + e) * P, (2 * u + e + 1) * P)
+                    nc.tensor.matmul_mx(
+                        out=a[:, e, :],
+                        lhsT=xT_codes[o][:, rows].bitcast(E4M3),
+                        lhsT_scale=xT_sc[o][:, rows],
+                        rhs=w_codes[:, cols].bitcast(E4M3),
+                        rhs_scale=w_sc[:, cols],
+                        start=True,
+                        stop=True,
+                    )
+                nc.scalar.activation(out=mean[o][h][:, 2 * u : 2 * u + 2, :], in_=a, func=EXP)
+
+        def interleave(copy, out, in_, cols=lo):
+            copy(
+                out=out[:, cols, :].rearrange("p (c i) t -> p c t i", i=RUN),
+                in_=in_[:, :, cols].rearrange("p t (c i) -> p c t i", i=RUN),
+            )
+
+        def resid(o, s):
+            return work[o][0][:].rearrange("p t i -> p (t i)").rearrange("p (s t i) -> p s t i", s=2, t=PACK)[:, s]
+
+        def residual(o, h):
+            for s, cols in enumerate(quarters):
+                nc.vector.tensor_tensor(resid(o, s), mean[o][h][:, :, cols], y_sb[o][h][:, :, cols], SUB)
+
+        def weigh(o, h):
+            for s, cols in enumerate(quarters):
+                nc.vector.tensor_tensor(
+                    g_bf[o][h][:, cols, :].rearrange("p (c i) t -> p c t i", i=RUN),
+                    resid(o, s).rearrange("p t (c i) -> p c t i", i=RUN),
+                    wt_sb[:, o, :].unsqueeze(1).unsqueeze(3).to_broadcast([P, P // RUN, PACK, RUN]),
+                    MUL,
                 )
-            mean = ring.tile([P, 2, HALF], F32, name="mean", bufs=4)
-            nc.scalar.activation(out=mean[:], in_=a[:], func=EXP)
-            return mean
 
-        def residual(o, h, u, mean, resid):
-            nc.vector.tensor_tensor(resid[:, 2 * u : 2 * u + 2, :], mean[:], y_sb[o][h][:, 2 * u : 2 * u + 2, :], SUB)
+        def weigh_means(o, h):
+            for t in range(PACK):
+                nc.scalar.activation(
+                    out=work[o][h][:, t, :], in_=mean[o][h][:, t, :], func=COPY, scale=wt_sb[:, o, t : t + 1]
+                )
 
-        def weigh(o, resid):
-            g_bf = ring.tile([P, HALF, PACK], BF16, align_bytes=64, name="g_bf")
-            nc.vector.tensor_tensor(
-                g_bf[:].rearrange("p (c i) t -> p c t i", i=RUN),
-                resid[:].rearrange("p t (c i) -> p c t i", i=RUN),
-                wt_sb[:, o, :].unsqueeze(1).unsqueeze(3).to_broadcast([P, HALF // RUN, PACK, RUN]),
-                MUL,
-            )
-            return g_bf
+        def finish_rows(o, h):
+            for t in range(PACK):
+                nc.vector.scalar_tensor_tensor(
+                    g_rows[o][h][:, t, :], y_sb[o][h][:, t, :], wt_neg[:, o, t : t + 1], work[o][h][:, t, :], MUL, ADD
+                )
 
-        def quantize_g(o, h, g_bf):
-            cols = slice(h * HALF, (h + 1) * HALF)
+        def interleave_g(o, h, copy, cols=lo):
+            interleave(copy, g_bf[o][h], g_rows[o][h], cols)
+
+        def quantize_g(o, h):
             nc.vector.quantize_mx(
-                out=g_codes[o][:, cols].bitcast(E5M2),
-                scales=g_sc[o][:, cols],
-                in_=g_bf[:].rearrange("p i t -> p (i t)"),
+                out=g_codes[o][:, halves[h]].bitcast(E5M2),
+                scales=g_sc[o][:, halves[h]],
+                in_=g_bf[o][h][:].rearrange("p i t -> p (i t)"),
             )
 
-        def round_xm(o, h):
-            xm_bf = ring.tile([P, HALF, PACK], BF16, align_bytes=64, name="xm_bf", bufs=4)
-            nc.scalar.copy(
-                out=xm_bf[:].rearrange("p (c i) t -> p c t i", i=RUN),
-                in_=xm_raw[o][h][:].rearrange("p t (c i) -> p c t i", i=RUN),
-            )
-            return xm_bf
+        def round_xm(o, h, copy, cols=lo):
+            interleave(copy, xm_bf[o][h], xm_raw[o][h], cols)
 
-        def quantize_xm(o, h, xm_bf):
-            cols = slice(h * HALF, (h + 1) * HALF)
+        def quantize_xm(o, h):
             nc.vector.quantize_mx(
-                out=xm_codes[o][:, cols].bitcast(E4M3),
-                scales=xm_sc[o][:, cols],
-                in_=xm_bf[:].rearrange("p d t -> p (d t)"),
+                out=xm_codes[o][h][:].bitcast(E4M3),
+                scales=xm_sc[o][h][:],
+                in_=xm_bf[o][h][:].rearrange("p d t -> p (d t)"),
             )
 
-        nc.vector.tensor_copy(w_sc[:], table_scales[:].bitcast(U8).indirect(offsets[:]))
-        round_xT(0, 0, nc.scalar.copy)
-        round_xT(0, 1, nc.scalar.copy)
-        quantize_xT(0)
-        gather_words(0)
-        gather_words(1)
-
-        def gradient_pass(c, o, dw):
-            rows = slice(c * P, (c + 1) * P)
+        def gradient_pass(c, o, dw, first):
+            h, rows = c // 2, slice(c % 2 * P, (c % 2 + 1) * P)
             nc.tensor.matmul_mx(
                 out=dw[:],
-                lhsT=xm_codes[o][:, rows].bitcast(E4M3),
-                lhsT_scale=xm_sc[o][:, rows],
+                lhsT=xm_codes[o][h][:, rows].bitcast(E4M3),
+                lhsT_scale=xm_sc[o][h][:, rows],
                 rhs=g_codes[o][:].bitcast(E5M2),
                 rhs_scale=g_sc[o][:],
-                start=(o == 0),
-                stop=(o == PASSES - 1),
+                start=first,
+                stop=not first,
             )
 
-        def open_gradient(c):
-            dw = psum_dw.tile([P, N], F32, name="dw")
-            gradient_pass(c, 0, dw)
-            return dw
+        def multiply(c, b):
+            order = (0, 1) if c == 0 else (1, 0)
+            for o in order:
+                gradient_pass(c, o, bank[b], o == order[0])
 
-        def close_gradient(c, dw, cols):
-            gradient_pass(c, 1, dw)
-            dw_sb = ring.tile([P, cols.stop - cols.start], F32, name="dw_sb", bufs=4)
-            nc.scalar.copy(out=dw_sb[:], in_=dw[:, cols])
+        def gradient(c, cols, b, dw_sb=None):
+            multiply(c, b)
+            return drain(c, cols, b, dw_sb)
+
+        def drain(c, cols, b, dw_sb=None):
+            dw = bank[b]
+            if dw_sb is None:
+                dw_sb = keep.tile([P, cols.stop - cols.start], F32, name=f"dw_sb{c}_{cols.start}")[:]
+            nc.scalar.copy(out=dw_sb, in_=dw[:, cols])
             return dw_sb
 
         def scatter(c, cols, dw_sb):
             nc.vector.tensor_copy(
-                windows[c % WINDOWS][:].indirect(offsets[:, cols.start // 16 : cols.stop // 16]), dw_sb[:]
+                windows[c % WINDOWS][:].indirect(offsets[:, cols.start // 16 : cols.stop // 16]), dw_sb
             )
 
         def store(c):
             nc.sync.dma_start(out=out[c * P : (c + 1) * P, :], in_=windows[c % WINDOWS][:])
 
-        lo, hi, both = slice(0, HALF), slice(HALF, N), slice(0, N)
+        on_vector, on_scalar = nc.vector.tensor_copy, nc.scalar.copy
 
-        round_xT(1, 0, nc.vector.tensor_copy)
-        mean = [means(0, 0, u) for u in range(2)]
-        resid00 = ring.tile([P, PACK, HALF], F32, name="resid")
-        residual(0, 0, 0, mean[0], resid00)
-        residual(0, 0, 1, mean[1], resid00)
-        mean = [means(0, 1, u) for u in range(2)]
-        round_xT(1, 1, nc.scalar.copy)
-        g00 = weigh(0, resid00)
-        resid01 = ring.tile([P, PACK, HALF], F32, name="resid")
-        residual(0, 1, 0, mean[0], resid01)
+        nc.gpsimd.memset(table_scales[:], 0)
+        nc.sync.dma_start(offsets[:], offs)
+        load_xT(0, 0)
+        load_scales()
+        load_xT(0, 1)
+        load_words()
+        nc.scalar.dma_start(out=wt_sb, in_=wt[0].rearrange("(o p t) one -> p o (t one)", o=PASSES, t=PACK))
+        load_xT(1, 0)
+        load_xT(1, 1)
+        for h in range(2):
+            for o in range(PASSES):
+                load_y(o, h)
+            for o in range(PASSES):
+                load_xm(o, h)
+
+        for c in range(3):
+            nc.vector.memset(windows[c][:].bitcast(I32), 0)
+        for o in range(PASSES):
+            nc.vector.memset(g_codes[o][:, hi], 0)
+            nc.vector.memset(g_sc[o][:, hi].bitcast(I32), 0)
+
+        work[0][1] = xm_raw[0][0]
+        for o in range(PASSES):
+            xm_bf[o][0] = resid(0, o).rearrange("p t i -> p (t i)").bitcast(BF16).rearrange("p (d t) -> p d t", t=PACK)
+        g_bf[0][1] = y_sb[1][1][:].rearrange("p t i -> p (t i)").bitcast(BF16)[:, : HALF * PACK].rearrange("p (d t) -> p d t", t=PACK)
+        xm_bf[0][1] = g_bf[0][1]
+        xm_bf[1][1] = g_bf[1][1]
+        early0_sb = mean[1][1][:, 3, :]
+        early1_sb = g_rows[1][1][:].rearrange("p t i -> p (t i)").bitcast(F32)[:, :HALF]
+
+        nc.scalar.activation(out=wt_neg[:], in_=wt_sb, func=COPY, scale=-1.0)
+        gather_scales()
+        round_xT(0, 0, on_scalar)
+        round_xT(0, 1, on_scalar)
+        quantize_xT(0)
+        gather_words(0)
+        gather_words(1)
+        means(0, 0, {0: 0, 1: 1})
+        round_xT(1, 0, on_vector)
+        round_xT(1, 1, on_vector)
         quantize_xT(1)
-        residual(0, 1, 1, mean[1], resid01)
-        quantize_g(0, 0, g00)
-        xm00 = round_xm(0, 0)
-        g01 = weigh(0, resid01)
-        mean = [means(1, 0, u) for u in range(2)]
-        xm10 = round_xm(1, 0)
-        resid10 = ring.tile([P, PACK, HALF], F32, name="resid")
-        residual(1, 0, 0, mean[0], resid10)
-        quantize_g(0, 1, g01)
-        residual(1, 0, 1, mean[1], resid10)
-        quantize_xm(0, 0, xm00)
-        g10 = weigh(1, resid10)
-        quantize_xm(1, 0, xm10)
-        quantize_g(1, 0, g10)
-
-        mean = [means(1, 1, u) for u in range(2)]
-        wy = keep.tile([P, PACK, HALF], F32)
-        g11_rows = keep.tile([P, PACK, HALF], BF16)
-        for t in range(PACK):
-            nc.scalar.activation(out=wy[:, t, :], in_=y_sb[1][1][:, t, :], func=COPY, scale=wt_sb[:, 1, t : t + 1])
-        early_open = [open_gradient(c) for c in range(2)]
-        early = [close_gradient(c, early_open[c], lo) for c in range(2)]
-        late_open = [open_gradient(c) for c in range(2)]
-        for t in range(PACK):
-            nc.vector.scalar_tensor_tensor(
-                g11_rows[:, t, :], mean[t // 2][:, t % 2, :], wt_sb[:, 1, t : t + 1], wy[:, t, :], MUL, SUB
-            )
-        g11 = ring.tile([P, HALF, PACK], BF16, align_bytes=64, name="g_bf")
-        nc.scalar.copy(
-            out=g11[:].rearrange("p (c i) t -> p c t i", i=4),
-            in_=g11_rows[:].rearrange("p t (c i) -> p c t i", i=4),
-        )
-        scatter(0, lo, early[0])
-        quantize_g(1, 1, g11)
-        late = [close_gradient(c, late_open[c], hi) for c in range(2)]
-        xm_hi = [round_xm(o, 1) for o in range(PASSES)]
-        scatter(1, lo, early[1])
-        scatter(0, hi, late[0])
+        residual(0, 0)
+        weigh(0, 0)
+        means(1, 0, {0: 0, 1: 1})
+        residual(1, 0)
+        weigh(1, 0)
+        round_xm(0, 0, on_scalar)
+        round_xm(1, 0, on_scalar, quarters[0])
+        quantize_g(0, 0)
+        quantize_xm(0, 0)
+        round_xm(1, 0, on_vector, quarters[1])
+        quantize_g(1, 0)
+        quantize_xm(1, 0)
+        multiply(0, 3)
+        multiply(1, 4)
+        means(0, 1, {0: 2, 1: 7})
+        means(1, 1, {0: 0, 1: 1})
+        weigh_means(0, 1)
+        weigh_means(1, 1)
+        finish_rows(0, 1)
+        finish_rows(1, 1)
+        early0 = drain(0, lo, 3, early0_sb)
+        interleave_g(0, 1, on_scalar)
+        interleave_g(1, 1, on_scalar)
+        early1 = drain(1, lo, 4, early1_sb)
+        scatter(0, lo, early0)
+        quantize_g(0, 1)
+        quantize_g(1, 1)
+        scatter(1, lo, early1)
+        round_xm(0, 1, on_scalar, slice(0, P))
+        round_xm(0, 1, on_vector, slice(P, HALF))
+        round_xm(1, 1, on_scalar)
+        late0 = gradient(0, hi, 5, xm_raw[1][1][:, 0, :])
+        late1 = gradient(1, hi, 6, xm_raw[1][1][:, 1, :])
+        quantize_xm(0, 1)
+        quantize_xm(1, 1)
+        scatter(0, hi, late0)
         store(0)
-        quantize_xm(0, 1, xm_hi[0])
-        rest_open = [open_gradient(c) for c in range(2, D_BLOCKS)]
-        quantize_xm(1, 1, xm_hi[1])
-        rest = [close_gradient(c, rest_open[c - 2], both) for c in range(2, D_BLOCKS)]
-        scatter(1, hi, late[1])
+        rest = [gradient(2, both, 7), gradient(3, both, 2)]
+        scatter(1, hi, late1)
         store(1)
         for c in range(2, D_BLOCKS):
             scatter(c, both, rest[c - 2])

@@ -54,11 +54,12 @@ def tile_attend_gpoi_w_kernel(tc, xT, w_words, w_scales, y, wt, xm, offs, out):
         xT_raw = units("xT_raw", [P, PACK, HALF], F32)
         y_sb = units("y_sb", [P, PACK, HALF], F32)
         xm_raw = units("xm_raw", [P, PACK, HALF], F32)
-        windows = [keep.tile([P, T], F32, name=f"window{c}") for c in range(WINDOWS)]
+        windows = [keep.tile([P, T], F32, name="window0")]
 
         w_codes = keep.tile([P, N], U32, align_bytes=64)
         w_sc = keep.tile([P, N], U8, align_bytes=64)
         xT_bf = passes("xT_bf", [P, PACK, P, PACK], BF16)
+        xT_bf[1] = keep.tile([P, PACK, P, PACK], BF16, align_bytes=64, name="xT_bf_last", tag="window1")
         xT_codes = passes("xT_codes", [P, K_PASS], U32)
         xT_sc = passes("xT_sc", [P, K_PASS], U8)
         xm_bf = units("xm_bf", [P, HALF, PACK], BF16)
@@ -66,6 +67,7 @@ def tile_attend_gpoi_w_kernel(tc, xT, w_words, w_scales, y, wt, xm, offs, out):
         xm_sc = units("xm_sc", [P, HALF], U8)
         mean = units("mean", [P, PACK, HALF], F32)
         work = units("work", [P, PACK, HALF], F32)
+        work[0][0] = keep.tile([P, PACK, HALF], F32, align_bytes=64, name="work_first", tag="window2")
         g_rows = units("g_rows", [P, PACK, HALF], BF16)
         g_bf = units("g_bf", [P, HALF, PACK], BF16)
         g_codes = passes("g_codes", [P, N], I32)
@@ -243,8 +245,7 @@ def tile_attend_gpoi_w_kernel(tc, xT, w_words, w_scales, y, wt, xm, offs, out):
             for o in range(PASSES):
                 load_xm(o, h)
 
-        for c in range(3):
-            nc.vector.memset(windows[c][:].bitcast(I32), 0)
+        nc.vector.memset(windows[0][:].bitcast(I32), 0)
         for o in range(PASSES):
             nc.vector.memset(g_codes[o][:, hi], 0)
             nc.vector.memset(g_sc[o][:, hi].bitcast(I32), 0)
@@ -269,6 +270,8 @@ def tile_attend_gpoi_w_kernel(tc, xT, w_words, w_scales, y, wt, xm, offs, out):
         round_xT(1, 0, on_vector)
         round_xT(1, 1, on_vector)
         quantize_xT(1)
+        windows.append(keep.tile([P, T], F32, align_bytes=64, name="window1", tag="window1"))
+        nc.gpsimd.memset(windows[1][:].bitcast(I32), 0)
         residual(0, 0)
         weigh(0, 0)
         means(1, 0, {0: 0, 1: 1})
@@ -281,6 +284,8 @@ def tile_attend_gpoi_w_kernel(tc, xT, w_words, w_scales, y, wt, xm, offs, out):
         round_xm(1, 0, on_vector, quarters[1])
         quantize_g(1, 0)
         quantize_xm(1, 0)
+        windows.append(keep.tile([P, T], F32, align_bytes=64, name="window2", tag="window2"))
+        nc.gpsimd.memset(windows[2][:].bitcast(I32), 0)
         multiply(0, 3)
         multiply(1, 4)
         means(0, 1, {0: 2, 1: 7})

@@ -73,6 +73,11 @@ def tile_attend_gpoi_w_kernel(tc, xT, w_words, w_scales, y, wt, xm, offs, out):
         g_codes = passes("g_codes", [P, N], I32)
         g_sc = passes("g_sc", [P, N], U8)
 
+        mean[1][1] = xm_raw[1][0]
+
+        raw_low = keep.tile([P, 6 * HALF], F32, align_bytes=64)
+        xm_raw[0][0] = raw_low[:, 2 * HALF :].rearrange("p (t i) -> p t i", t=PACK)
+
         xT_v = xT[0].rearrange("(p j) r -> p j r", j=PACK)
         y_v = y[0].rearrange("(o p t) i -> o p t i", o=PASSES, t=PACK)
         xm_v = xm[0].rearrange("(o p t) d -> o p t d", o=PASSES, t=PACK)
@@ -137,6 +142,19 @@ def tile_attend_gpoi_w_kernel(tc, xT, w_words, w_scales, y, wt, xm, offs, out):
                         stop=True,
                     )
                 nc.scalar.activation(out=mean[o][h][:, 2 * u : 2 * u + 2, :], in_=a, func=EXP)
+
+        def first_means():
+            for t, b in ((0, 3), (1, 0)):
+                nc.tensor.matmul_mx(
+                    out=bank[b][:, lo],
+                    lhsT=xT_codes[0][:, t * P : (t + 1) * P].bitcast(E4M3),
+                    lhsT_scale=xT_sc[0][:, t * P : (t + 1) * P],
+                    rhs=w_codes[:, lo].bitcast(E4M3),
+                    rhs_scale=w_sc[:, lo],
+                    start=True,
+                    stop=True,
+                )
+                nc.scalar.activation(out=mean[0][0][:, t, :], in_=bank[b][:, lo], func=EXP)
 
         def interleave(copy, out, in_, cols=lo):
             copy(
@@ -250,14 +268,14 @@ def tile_attend_gpoi_w_kernel(tc, xT, w_words, w_scales, y, wt, xm, offs, out):
             nc.vector.memset(g_codes[o][:, hi], 0)
             nc.vector.memset(g_sc[o][:, hi].bitcast(I32), 0)
 
-        work[0][1] = xm_raw[0][0]
+        work[0][1] = raw_low[:, : PACK * HALF].rearrange("p (t i) -> p t i", t=PACK)
         for o in range(PASSES):
             xm_bf[o][0] = resid(0, o).rearrange("p t i -> p (t i)").bitcast(BF16).rearrange("p (d t) -> p d t", t=PACK)
         g_bf[0][1] = y_sb[1][1][:].rearrange("p t i -> p (t i)").bitcast(BF16)[:, : HALF * PACK].rearrange("p (d t) -> p d t", t=PACK)
         xm_bf[0][1] = g_bf[0][1]
         xm_bf[1][1] = g_bf[1][1]
-        early0_sb = mean[1][1][:, 3, :]
-        early1_sb = g_rows[1][1][:].rearrange("p t i -> p (t i)").bitcast(F32)[:, :HALF]
+        early0_sb = mean[1][1][:, 2, :]
+        early1_sb = g_rows[0][1][:].rearrange("p t i -> p (t i)").bitcast(F32)[:, :HALF]
 
         nc.scalar.activation(out=wt_neg[:], in_=wt_sb, func=COPY, scale=-1.0)
         gather_scales()
@@ -266,7 +284,8 @@ def tile_attend_gpoi_w_kernel(tc, xT, w_words, w_scales, y, wt, xm, offs, out):
         quantize_xT(0)
         gather_words(0)
         gather_words(1)
-        means(0, 0, {0: 0, 1: 1})
+        first_means()
+        means(0, 0, {1: 1})
         round_xT(1, 0, on_vector)
         round_xT(1, 1, on_vector)
         quantize_xT(1)
@@ -278,10 +297,9 @@ def tile_attend_gpoi_w_kernel(tc, xT, w_words, w_scales, y, wt, xm, offs, out):
         residual(1, 0)
         weigh(1, 0)
         round_xm(0, 0, on_scalar)
-        round_xm(1, 0, on_scalar, quarters[0])
+        round_xm(1, 0, on_scalar)
         quantize_g(0, 0)
         quantize_xm(0, 0)
-        round_xm(1, 0, on_vector, quarters[1])
         quantize_g(1, 0)
         quantize_xm(1, 0)
         windows.append(keep.tile([P, T], F32, align_bytes=64, name="window2", tag="window2"))
@@ -302,8 +320,8 @@ def tile_attend_gpoi_w_kernel(tc, xT, w_words, w_scales, y, wt, xm, offs, out):
         quantize_g(0, 1)
         quantize_g(1, 1)
         scatter(1, lo, early1)
-        round_xm(0, 1, on_scalar, slice(0, P))
-        round_xm(0, 1, on_vector, slice(P, HALF))
+        round_xm(0, 1, on_scalar, quarters[0])
+        round_xm(0, 1, on_vector, quarters[1])
         round_xm(1, 1, on_scalar)
         late0 = gradient(0, hi, 5, xm_raw[1][1][:, 0, :])
         late1 = gradient(1, hi, 6, xm_raw[1][1][:, 1, :])

@@ -54,12 +54,11 @@ def tile_attend_gpoi_w_kernel(tc, xT, w_words, w_scales, y, wt, xm, offs, out):
         xT_raw = units("xT_raw", [P, PACK, HALF], F32)
         y_sb = units("y_sb", [P, PACK, HALF], F32)
         xm_raw = units("xm_raw", [P, PACK, HALF], F32)
-        windows = [keep.tile([P, T], F32, name="window0")]
+        windows = [keep.tile([P, T], F32, name=f"window{c}") for c in range(2)]
 
         w_codes = keep.tile([P, N], U32, align_bytes=64)
         w_sc = keep.tile([P, N], U8, align_bytes=64)
         xT_bf = passes("xT_bf", [P, PACK, P, PACK], BF16)
-        xT_bf[1] = keep.tile([P, PACK, P, PACK], BF16, align_bytes=64, name="xT_bf_last", tag="window1")
         xT_codes = passes("xT_codes", [P, K_PASS], U32)
         xT_sc = passes("xT_sc", [P, K_PASS], U8)
         xm_bf = units("xm_bf", [P, HALF, PACK], BF16)
@@ -166,17 +165,15 @@ def tile_attend_gpoi_w_kernel(tc, xT, w_words, w_scales, y, wt, xm, offs, out):
             return work[o][0][:].rearrange("p t i -> p (t i)").rearrange("p (s t i) -> p s t i", s=2, t=PACK)[:, s]
 
         def residual(o, h):
-            for s, cols in enumerate(quarters):
-                nc.vector.tensor_tensor(resid(o, s), mean[o][h][:, :, cols], y_sb[o][h][:, :, cols], SUB)
+            for pair in (slice(0, 2), slice(2, 4)):
+                nc.vector.tensor_tensor(work[o][h][:, pair, :], mean[o][h][:, pair, :], y_sb[o][h][:, pair, :], SUB)
 
         def weigh(o, h):
-            for s, cols in enumerate(quarters):
-                nc.vector.tensor_tensor(
-                    g_bf[o][h][:, cols, :].rearrange("p (c i) t -> p c t i", i=RUN),
-                    resid(o, s).rearrange("p t (c i) -> p c t i", i=RUN),
-                    wt_sb[:, o, :].unsqueeze(1).unsqueeze(3).to_broadcast([P, P // RUN, PACK, RUN]),
-                    MUL,
+            for t in range(PACK):
+                nc.vector.tensor_scalar(
+                    g_rows[o][h][:, t, :], work[o][h][:, t, :], wt_sb[:, o, t : t + 1], None, MUL
                 )
+            interleave_g(o, h, on_vector)
 
         def weigh_means(o, h):
             for t in range(PACK):
@@ -263,7 +260,8 @@ def tile_attend_gpoi_w_kernel(tc, xT, w_words, w_scales, y, wt, xm, offs, out):
             for o in range(PASSES):
                 load_xm(o, h)
 
-        nc.vector.memset(windows[0][:].bitcast(I32), 0)
+        for window in windows:
+            nc.vector.memset(window[:].bitcast(I32), 0)
         for o in range(PASSES):
             nc.vector.memset(g_codes[o][:, hi], 0)
             nc.vector.memset(g_sc[o][:, hi].bitcast(I32), 0)
@@ -289,8 +287,6 @@ def tile_attend_gpoi_w_kernel(tc, xT, w_words, w_scales, y, wt, xm, offs, out):
         round_xT(1, 0, on_vector)
         round_xT(1, 1, on_vector)
         quantize_xT(1)
-        windows.append(keep.tile([P, T], F32, align_bytes=64, name="window1", tag="window1"))
-        nc.gpsimd.memset(windows[1][:].bitcast(I32), 0)
         residual(0, 0)
         weigh(0, 0)
         means(1, 0, {0: 0, 1: 1})

@@ -54,7 +54,7 @@ def tile_attend_gpoi_w_kernel(tc, xT, w_words, w_scales, y, wt, xm, offs, out):
         xT_raw = units("xT_raw", [P, PACK, HALF], F32)
         y_sb = units("y_sb", [P, PACK, HALF], F32)
         xm_raw = units("xm_raw", [P, PACK, HALF], F32)
-        windows = [keep.tile([P, T], F32, name=f"window{c}") for c in range(2)]
+        windows = [keep.tile([P, T], F32, name=f"window{c}") for c in range(WINDOWS)]
 
         w_codes = keep.tile([P, N], U32, align_bytes=64)
         w_sc = keep.tile([P, N], U8, align_bytes=64)
@@ -66,7 +66,6 @@ def tile_attend_gpoi_w_kernel(tc, xT, w_words, w_scales, y, wt, xm, offs, out):
         xm_sc = units("xm_sc", [P, HALF], U8)
         mean = units("mean", [P, PACK, HALF], F32)
         work = units("work", [P, PACK, HALF], F32)
-        work[0][0] = keep.tile([P, PACK, HALF], F32, align_bytes=64, name="work_first", tag="window2")
         g_rows = units("g_rows", [P, PACK, HALF], BF16)
         g_bf = units("g_bf", [P, HALF, PACK], BF16)
         g_codes = passes("g_codes", [P, N], I32)
@@ -246,8 +245,8 @@ def tile_attend_gpoi_w_kernel(tc, xT, w_words, w_scales, y, wt, xm, offs, out):
         on_vector, on_scalar = nc.vector.tensor_copy, nc.scalar.copy
 
         nc.gpsimd.memset(table_scales[:], 0)
-        nc.sync.dma_start(offsets[:], offs)
         load_xT(0, 0)
+        nc.sync.dma_start(offsets[:], offs)
         load_scales()
         load_xT(0, 1)
         load_words()
@@ -298,8 +297,6 @@ def tile_attend_gpoi_w_kernel(tc, xT, w_words, w_scales, y, wt, xm, offs, out):
         quantize_xm(0, 0)
         quantize_g(1, 0)
         quantize_xm(1, 0)
-        windows.append(keep.tile([P, T], F32, align_bytes=64, name="window2", tag="window2"))
-        nc.gpsimd.memset(windows[2][:].bitcast(I32), 0)
         multiply(0, 3)
         multiply(1, 4)
         means(0, 1, {0: 2, 1: 7})

@@ -27,6 +27,7 @@ D_BLOCKS = D // P
 HALF = 256
 WINDOWS = 3
 RUN = 4
+POOL_COLS = 192
 
 
 def tile_attend_gpoi_w_kernel(tc, xT, w_words, w_scales, y, wt, xm, offs, out):
@@ -54,7 +55,7 @@ def tile_attend_gpoi_w_kernel(tc, xT, w_words, w_scales, y, wt, xm, offs, out):
         xT_raw = units("xT_raw", [P, PACK, HALF], F32)
         y_sb = units("y_sb", [P, PACK, HALF], F32)
         xm_raw = units("xm_raw", [P, PACK, HALF], F32)
-        windows = [keep.tile([P, T], F32, name=f"window{c}") for c in range(WINDOWS)]
+        windows = [keep.tile([P, T], F32, align_bytes=64, name=f"window{c}") for c in range(2)]
 
         w_codes = keep.tile([P, N], U32, align_bytes=64)
         w_sc = keep.tile([P, N], U8, align_bytes=64)
@@ -68,6 +69,7 @@ def tile_attend_gpoi_w_kernel(tc, xT, w_words, w_scales, y, wt, xm, offs, out):
         work = units("work", [P, PACK, HALF], F32)
         g_rows = units("g_rows", [P, PACK, HALF], BF16)
         g_bf = units("g_bf", [P, HALF, PACK], BF16)
+        g_bf[1][1] = keep.tile([P, HALF, PACK], BF16, align_bytes=64, name="g_last", tag="last")
         g_codes = passes("g_codes", [P, N], I32)
         g_sc = passes("g_sc", [P, N], U8)
 
@@ -244,20 +246,24 @@ def tile_attend_gpoi_w_kernel(tc, xT, w_words, w_scales, y, wt, xm, offs, out):
 
         on_vector, on_scalar = nc.vector.tensor_copy, nc.scalar.copy
 
-        nc.gpsimd.memset(table_scales[:], 0)
+        nc.gpsimd.memset(table_scales[:, : T // 8], 0)
+        nc.vector.memset(table_scales[:, T // 8 :], 0)
         load_xT(0, 0)
         nc.sync.dma_start(offsets[:], offs)
         load_scales()
         load_xT(0, 1)
         load_words()
-        nc.scalar.dma_start(out=wt_sb, in_=wt[0].rearrange("(o p t) one -> p o (t one)", o=PASSES, t=PACK))
         load_xT(1, 0)
         load_xT(1, 1)
-        for h in range(2):
-            for o in range(PASSES):
-                load_y(o, h)
-            for o in range(PASSES):
-                load_xm(o, h)
+        load_y(0, 0)
+        nc.sync.dma_start(out=wt_sb, in_=wt[0].rearrange("(o p t) one -> p o (t one)", o=PASSES, t=PACK))
+        load_y(1, 0)
+        load_xm(0, 0)
+        load_xm(1, 0)
+        load_y(0, 1)
+        load_y(1, 1)
+        load_xm(0, 1)
+        load_xm(1, 1)
 
         for window in windows:
             nc.vector.memset(window[:].bitcast(I32), 0)
@@ -269,14 +275,13 @@ def tile_attend_gpoi_w_kernel(tc, xT, w_words, w_scales, y, wt, xm, offs, out):
         for o in range(PASSES):
             xm_bf[o][0] = resid(0, o).rearrange("p t i -> p (t i)").bitcast(BF16).rearrange("p (d t) -> p d t", t=PACK)
         g_bf[0][1] = y_sb[1][1][:].rearrange("p t i -> p (t i)").bitcast(BF16)[:, : HALF * PACK].rearrange("p (d t) -> p d t", t=PACK)
-        xm_bf[0][1] = g_bf[0][1]
-        xm_bf[1][1] = g_bf[1][1]
+        xm_bf[0][1] = g_bf[1][1]
+        xm_bf[1][1] = g_bf[0][1]
         early0_sb = mean[1][1][:, 2, :]
         early1_sb = g_rows[0][1][:].rearrange("p t i -> p (t i)").bitcast(F32)[:, :HALF]
 
-        nc.scalar.activation(out=wt_neg[:], in_=wt_sb, func=COPY, scale=-1.0)
         gather_scales()
-        round_xT(0, 0, on_scalar)
+        round_xT(0, 0, lambda out, in_: nc.scalar.activation(out=out, in_=in_, func=COPY))
         round_xT(0, 1, on_scalar)
         quantize_xT(0)
         gather_words(0)
@@ -286,6 +291,7 @@ def tile_attend_gpoi_w_kernel(tc, xT, w_words, w_scales, y, wt, xm, offs, out):
         round_xT(1, 0, on_vector)
         round_xT(1, 1, on_vector)
         quantize_xT(1)
+        nc.gpsimd.tensor_scalar(wt_neg[:], wt_sb, -1.0, 0.0, MUL, ADD)
         residual(0, 0)
         weigh(0, 0)
         means(1, 0, {0: 0, 1: 1})
@@ -313,13 +319,22 @@ def tile_attend_gpoi_w_kernel(tc, xT, w_words, w_scales, y, wt, xm, offs, out):
         quantize_g(0, 1)
         quantize_g(1, 1)
         scatter(1, lo, early1)
-        round_xm(0, 1, on_scalar, quarters[0])
-        round_xm(0, 1, on_vector, quarters[1])
+        nc.gpsimd.tensor_scalar(
+            xm_bf[0][1][:, :POOL_COLS, :],
+            xm_raw[0][1][:, :, :POOL_COLS].rearrange("p t d -> p d t"),
+            1.0,
+            0.0,
+            MUL,
+            ADD,
+        )
         round_xm(1, 1, on_scalar)
+        round_xm(0, 1, on_scalar, slice(POOL_COLS, HALF))
         late0 = gradient(0, hi, 5, xm_raw[1][1][:, 0, :])
         late1 = gradient(1, hi, 6, xm_raw[1][1][:, 1, :])
-        quantize_xm(0, 1)
         quantize_xm(1, 1)
+        quantize_xm(0, 1)
+        windows.append(keep.tile([P, T], F32, align_bytes=64, name="window2", tag="last"))
+        nc.gpsimd.memset(windows[2][:], 0.0)
         scatter(0, hi, late0)
         store(0)
         rest = [gradient(2, both, 7), gradient(3, both, 2)]

@@ -27,7 +27,7 @@ D_BLOCKS = D // P
 HALF = 256
 WINDOWS = 3
 RUN = 4
-POOL_COLS = 192
+POOL_COLS = 128
 
 
 def tile_attend_gpoi_w_kernel(tc, xT, w_words, w_scales, y, wt, xm, offs, out):
@@ -51,7 +51,6 @@ def tile_attend_gpoi_w_kernel(tc, xT, w_words, w_scales, y, wt, xm, offs, out):
         table_scales = keep.tile([P, T // 4], I32, align_bytes=64)
         wt_rows = keep.tile([P, PASSES, 2 * PACK], F32)
         wt_sb = wt_rows[:, :, :PACK]
-        wt_neg = keep.tile([P, PASSES, PACK], F32)
         xT_raw = units("xT_raw", [P, PACK, HALF], F32)
         y_sb = units("y_sb", [P, PACK, HALF], F32)
         xm_raw = units("xm_raw", [P, PACK, HALF], F32)
@@ -167,7 +166,7 @@ def tile_attend_gpoi_w_kernel(tc, xT, w_words, w_scales, y, wt, xm, offs, out):
 
         def residual(o, h):
             for pair in (slice(0, 2), slice(2, 4)):
-                nc.vector.tensor_tensor(work[o][h][:, pair, :], mean[o][h][:, pair, :], y_sb[o][h][:, pair, :], SUB)
+                nc.vector.tensor_tensor(work[o][h][:, pair, :], y_sb[o][h][:, pair, :], mean[o][h][:, pair, :], SUB)
 
         def weigh(o, h):
             for t in range(PACK):
@@ -185,7 +184,7 @@ def tile_attend_gpoi_w_kernel(tc, xT, w_words, w_scales, y, wt, xm, offs, out):
         def finish_rows(o, h):
             for t in range(PACK):
                 nc.vector.scalar_tensor_tensor(
-                    g_rows[o][h][:, t, :], y_sb[o][h][:, t, :], wt_neg[:, o, t : t + 1], work[o][h][:, t, :], MUL, ADD
+                    g_rows[o][h][:, t, :], y_sb[o][h][:, t, :], wt_sb[:, o, t : t + 1], work[o][h][:, t, :], MUL, SUB
                 )
 
         def interleave_g(o, h, copy, cols=lo):
@@ -233,7 +232,7 @@ def tile_attend_gpoi_w_kernel(tc, xT, w_words, w_scales, y, wt, xm, offs, out):
             dw = bank[b]
             if dw_sb is None:
                 dw_sb = keep.tile([P, cols.stop - cols.start], F32, name=f"dw_sb{c}_{cols.start}")[:]
-            nc.scalar.copy(out=dw_sb, in_=dw[:, cols])
+            nc.scalar.activation(out=dw_sb, in_=dw[:, cols], func=COPY, scale=-1.0)
             return dw_sb
 
         def scatter(c, cols, dw_sb):
@@ -291,7 +290,6 @@ def tile_attend_gpoi_w_kernel(tc, xT, w_words, w_scales, y, wt, xm, offs, out):
         round_xT(1, 0, on_vector)
         round_xT(1, 1, on_vector)
         quantize_xT(1)
-        nc.gpsimd.tensor_scalar(wt_neg[:], wt_sb, -1.0, 0.0, MUL, ADD)
         residual(0, 0)
         weigh(0, 0)
         means(1, 0, {0: 0, 1: 1})

@@ -28,6 +28,7 @@ HALF = 256
 WINDOWS = 3
 RUN = 4
 POOL_COLS = 128
+SCALAR_COLS = 160
 
 
 def tile_attend_gpoi_w_kernel(tc, xT, w_words, w_scales, y, wt, xm, offs, out):
@@ -311,7 +312,15 @@ def tile_attend_gpoi_w_kernel(tc, xT, w_words, w_scales, y, wt, xm, offs, out):
         finish_rows(1, 1)
         early0 = drain(0, lo, 3, early0_sb)
         interleave_g(0, 1, on_scalar)
-        interleave_g(1, 1, on_scalar)
+        interleave_g(1, 1, on_scalar, slice(0, SCALAR_COLS))
+        nc.gpsimd.tensor_scalar(
+            g_bf[1][1][:, SCALAR_COLS:, :],
+            g_rows[1][1][:, :, SCALAR_COLS:].rearrange("p t i -> p i t"),
+            1.0,
+            0.0,
+            MUL,
+            ADD,
+        )
         early1 = drain(1, lo, 4, early1_sb)
         scatter(0, lo, early0)
         quantize_g(0, 1)

@@ -28,7 +28,8 @@ HALF = 256
 WINDOWS = 3
 RUN = 4
 POOL_COLS = 128
-SCALAR_COLS = 160
+SCALAR_COLS = 96
+FIRST_COLS = 176
 
 
 def tile_attend_gpoi_w_kernel(tc, xT, w_words, w_scales, y, wt, xm, offs, out):
@@ -174,16 +175,15 @@ def tile_attend_gpoi_w_kernel(tc, xT, w_words, w_scales, y, wt, xm, offs, out):
                 nc.vector.tensor_scalar(
                     g_rows[o][h][:, t, :], work[o][h][:, t, :], wt_sb[:, o, t : t + 1], None, MUL
                 )
-            interleave_g(o, h, on_vector)
 
-        def weigh_means(o, h):
-            for t in range(PACK):
+        def weigh_means(o, h, places):
+            for t in places:
                 nc.scalar.activation(
                     out=work[o][h][:, t, :], in_=mean[o][h][:, t, :], func=COPY, scale=wt_sb[:, o, t : t + 1]
                 )
 
-        def finish_rows(o, h):
-            for t in range(PACK):
+        def finish_rows(o, h, places):
+            for t in places:
                 nc.vector.scalar_tensor_tensor(
                     g_rows[o][h][:, t, :], y_sb[o][h][:, t, :], wt_sb[:, o, t : t + 1], work[o][h][:, t, :], MUL, SUB
                 )
@@ -265,8 +265,8 @@ def tile_attend_gpoi_w_kernel(tc, xT, w_words, w_scales, y, wt, xm, offs, out):
         load_xm(0, 1)
         load_xm(1, 1)
 
-        for window in windows:
-            nc.vector.memset(window[:].bitcast(I32), 0)
+        nc.vector.memset(windows[0][:].bitcast(I32), 0)
+        nc.gpsimd.memset(windows[1][:].bitcast(I32), 0)
         for o in range(PASSES):
             nc.vector.memset(g_codes[o][:, hi], 0)
             nc.vector.memset(g_sc[o][:, hi].bitcast(I32), 0)
@@ -274,10 +274,10 @@ def tile_attend_gpoi_w_kernel(tc, xT, w_words, w_scales, y, wt, xm, offs, out):
         work[0][1] = raw_low[:, : PACK * HALF].rearrange("p (t i) -> p t i", t=PACK)
         for o in range(PASSES):
             xm_bf[o][0] = resid(0, o).rearrange("p t i -> p (t i)").bitcast(BF16).rearrange("p (d t) -> p d t", t=PACK)
-        g_bf[0][1] = y_sb[1][1][:].rearrange("p t i -> p (t i)").bitcast(BF16)[:, : HALF * PACK].rearrange("p (d t) -> p d t", t=PACK)
+        g_bf[0][1] = y_sb[1][1][:].rearrange("p t i -> p (t i)").bitcast(BF16)[:, 2 * HALF - PACK * SCALAR_COLS : 6 * HALF - PACK * SCALAR_COLS].rearrange("p (d t) -> p d t", t=PACK)
         xm_bf[0][1] = g_bf[1][1]
         xm_bf[1][1] = g_bf[0][1]
-        early0_sb = mean[1][1][:, 2, :]
+        early0_sb = mean[1][1][:, 0, :]
         early1_sb = g_rows[0][1][:].rearrange("p t i -> p (t i)").bitcast(F32)[:, :HALF]
 
         gather_scales()
@@ -290,12 +290,23 @@ def tile_attend_gpoi_w_kernel(tc, xT, w_words, w_scales, y, wt, xm, offs, out):
         means(0, 0, {1: 1})
         round_xT(1, 0, on_vector)
         round_xT(1, 1, on_vector)
-        quantize_xT(1)
+        for h in range(2):
+            for t in range(PACK):
+                m = slice(h * (P // 2), (h + 1) * (P // 2))
+                cols = slice(t * P + m.start, t * P + m.stop)
+                nc.vector.quantize_mx(
+                    out=xT_codes[1][:, cols].bitcast(E4M3),
+                    scales=xT_sc[1][:, cols],
+                    in_=xT_bf[1][:, t, m, :].rearrange("p m j -> p (m j)"),
+                )
         residual(0, 0)
         weigh(0, 0)
+        interleave_g(0, 0, on_vector, slice(0, FIRST_COLS))
         means(1, 0, {0: 0, 1: 1})
         residual(1, 0)
         weigh(1, 0)
+        interleave_g(1, 0, on_vector)
+        interleave_g(0, 0, on_scalar, slice(FIRST_COLS, HALF))
         round_xm(0, 0, on_scalar)
         round_xm(1, 0, on_scalar)
         quantize_g(0, 0)
@@ -305,17 +316,22 @@ def tile_attend_gpoi_w_kernel(tc, xT, w_words, w_scales, y, wt, xm, offs, out):
         multiply(0, 3)
         multiply(1, 4)
         means(0, 1, {0: 2, 1: 7})
-        means(1, 1, {0: 0, 1: 1})
-        weigh_means(0, 1)
-        weigh_means(1, 1)
-        finish_rows(0, 1)
-        finish_rows(1, 1)
+        means(1, 1, {1: 0, 0: 1})
+        weigh_means(0, 1, range(PACK))
+        weigh_means(1, 1, range(2))
+        finish_rows(0, 1, range(PACK))
+        nc.vector.tensor_tensor(work[1][1][:, 2:, :], y_sb[1][1][:, 2:, :], mean[1][1][:, 2:, :], SUB)
+        finish_rows(1, 1, range(2))
         early0 = drain(0, lo, 3, early0_sb)
-        interleave_g(0, 1, on_scalar)
-        interleave_g(1, 1, on_scalar, slice(0, SCALAR_COLS))
+        interleave_g(0, 1, on_scalar, slice(0, SCALAR_COLS))
+        for t in (2, 3):
+            nc.scalar.activation(
+                out=g_rows[1][1][:, t, :], in_=work[1][1][:, t, :], func=COPY, scale=wt_sb[:, 1, t : t + 1]
+            )
+        interleave_g(1, 1, on_scalar)
         nc.gpsimd.tensor_scalar(
-            g_bf[1][1][:, SCALAR_COLS:, :],
-            g_rows[1][1][:, :, SCALAR_COLS:].rearrange("p t i -> p i t"),
+            g_bf[0][1][:, SCALAR_COLS:, :],
+            g_rows[0][1][:, :, SCALAR_COLS:].rearrange("p t i -> p i t"),
             1.0,
             0.0,
             MUL,

@@ -265,8 +265,8 @@ def tile_attend_gpoi_w_kernel(tc, xT, w_words, w_scales, y, wt, xm, offs, out):
         load_xm(0, 1)
         load_xm(1, 1)
 
-        nc.vector.memset(windows[0][:].bitcast(I32), 0)
-        nc.gpsimd.memset(windows[1][:].bitcast(I32), 0)
+        for window in windows:
+            nc.vector.memset(window[:].bitcast(I32), 0)
         for o in range(PASSES):
             nc.vector.memset(g_codes[o][:, hi], 0)
             nc.vector.memset(g_sc[o][:, hi].bitcast(I32), 0)

@@ -25,11 +25,12 @@ K_PASS = P * PACK
 PASSES = R // K_PASS
 D_BLOCKS = D // P
 HALF = 256
+UNIT = PACK * HALF
 WINDOWS = 3
 RUN = 4
-POOL_COLS = 128
-SCALAR_COLS = 96
-FIRST_COLS = 176
+FIRST_G_VECTOR = 160
+HIGH_G_SCALAR = 64
+HIGH_XM_GPSIMD = 128
 
 
 def tile_attend_gpoi_w_kernel(tc, xT, w_words, w_scales, y, wt, xm, offs, out):
@@ -39,52 +40,89 @@ def tile_attend_gpoi_w_kernel(tc, xT, w_words, w_scales, y, wt, xm, offs, out):
         psum = ctx.enter_context(tc.psum_pool(name="psum", bufs=1))
         bank = [psum.tile([P, N], F32, name=f"bank{b}") for b in range(8)]
 
+        def tile(name, shape, dtype, **kw):
+            return keep.tile(shape, dtype, align_bytes=64, name=name, **kw)
+
         def units(name, shape, dtype):
-            return [
-                [keep.tile(shape, dtype, align_bytes=64, name=f"{name}{o}{h}") for h in range(2)]
-                for o in range(PASSES)
-            ]
+            return [[tile(f"{name}{o}{h}", shape, dtype) for h in range(2)] for o in range(PASSES)]
 
         def passes(name, shape, dtype):
-            return [keep.tile(shape, dtype, align_bytes=64, name=f"{name}{o}") for o in range(PASSES)]
+            return [tile(f"{name}{o}", shape, dtype) for o in range(PASSES)]
+
+        def flat(ap):
+            return ap[:].rearrange("p t i -> p (t i)")
+
+        def by_place(ap):
+            return ap.rearrange("p (t i) -> p t i", t=PACK)
+
+        def by_word(ap):
+            return ap.rearrange("p (i t) -> p i t", t=PACK)
+
+        placed, worded = [P, PACK, HALF], [P, HALF, PACK]
 
         offsets = keep.tile([P, N // 16], U16)
-        table_words = keep.tile([P, T], I32, align_bytes=64)
-        table_scales = keep.tile([P, T // 4], I32, align_bytes=64)
+        table_words = tile("table_words", [P, T], I32)
+        table_scales = tile("table_scales", [P, T // 4], I32)
         wt_rows = keep.tile([P, PASSES, 2 * PACK], F32)
         wt_sb = wt_rows[:, :, :PACK]
-        xT_raw = units("xT_raw", [P, PACK, HALF], F32)
-        y_sb = units("y_sb", [P, PACK, HALF], F32)
-        xm_raw = units("xm_raw", [P, PACK, HALF], F32)
-        windows = [keep.tile([P, T], F32, align_bytes=64, name=f"window{c}") for c in range(2)]
+        xT_raw = units("xT_raw", placed, F32)
+        y_sb = units("y_sb", placed, F32)
+        raw_low = tile("raw_low", [P, UNIT + 2 * HALF], F32)
+        xm_raw = [
+            [by_place(raw_low[:, 2 * HALF :]), tile("xm_raw01", placed, F32)],
+            [tile("xm_raw10", placed, F32), tile("xm_raw11", placed, F32)],
+        ]
+        windows = [tile(f"window{c}", [P, T], F32) for c in range(WINDOWS - 1)]
 
-        w_codes = keep.tile([P, N], U32, align_bytes=64)
-        w_sc = keep.tile([P, N], U8, align_bytes=64)
+        w_codes = tile("w_codes", [P, N], U32)
+        w_sc = tile("w_sc", [P, N], U8)
         xT_bf = passes("xT_bf", [P, PACK, P, PACK], BF16)
         xT_codes = passes("xT_codes", [P, K_PASS], U32)
         xT_sc = passes("xT_sc", [P, K_PASS], U8)
-        xm_bf = units("xm_bf", [P, HALF, PACK], BF16)
         xm_codes = units("xm_codes", [P, HALF], U32)
         xm_sc = units("xm_sc", [P, HALF], U8)
-        mean = units("mean", [P, PACK, HALF], F32)
-        work = units("work", [P, PACK, HALF], F32)
-        g_rows = units("g_rows", [P, PACK, HALF], BF16)
-        g_bf = units("g_bf", [P, HALF, PACK], BF16)
-        g_bf[1][1] = keep.tile([P, HALF, PACK], BF16, align_bytes=64, name="g_last", tag="last")
+        g_rows = units("g_rows", placed, BF16)
         g_codes = passes("g_codes", [P, N], I32)
         g_sc = passes("g_sc", [P, N], U8)
 
-        mean[1][1] = xm_raw[1][0]
-
-        raw_low = keep.tile([P, 6 * HALF], F32, align_bytes=64)
-        xm_raw[0][0] = raw_low[:, 2 * HALF :].rearrange("p (t i) -> p t i", t=PACK)
+        mean = [
+            [tile("mean00", placed, F32), tile("mean01", placed, F32)],
+            [tile("mean10", placed, F32), xm_raw[1][0]],
+        ]
+        work = [
+            [tile("work00", placed, F32), by_place(raw_low[:, :UNIT])],
+            [tile("work10", placed, F32), tile("work11", placed, F32)],
+        ]
+        g_high0 = 2 * HALF - PACK * HIGH_G_SCALAR
+        g_bf = [
+            [tile("g_bf00", worded, BF16), by_word(flat(y_sb[1][1]).bitcast(BF16)[:, g_high0 : g_high0 + UNIT])],
+            [tile("g_bf10", worded, BF16), tile("g_bf11", worded, BF16, tag="last")],
+        ]
+        first_residual = flat(work[0][0]).bitcast(BF16)
+        xm_bf = [
+            [by_word(first_residual[:, :UNIT]), g_bf[1][1]],
+            [by_word(first_residual[:, UNIT:]), g_bf[0][1]],
+        ]
+        early_sb = [mean[1][1][:, 0, :], flat(g_rows[0][1]).bitcast(F32)[:, :HALF]]
+        late_sb = [xm_raw[1][1][:, 0, :], xm_raw[1][1][:, 1, :]]
 
         xT_v = xT[0].rearrange("(p j) r -> p j r", j=PACK)
         y_v = y[0].rearrange("(o p t) i -> o p t i", o=PASSES, t=PACK)
         xm_v = xm[0].rearrange("(o p t) d -> o p t d", o=PASSES, t=PACK)
         lo, hi, both = slice(0, HALF), slice(HALF, N), slice(0, N)
         halves = (lo, hi)
-        quarters = (slice(0, P), slice(P, HALF))
+
+        def on_vector(dst, src):
+            nc.vector.tensor_copy(out=dst, in_=src)
+
+        def on_scalar(dst, src):
+            nc.scalar.copy(out=dst, in_=src)
+
+        def on_scalar_activation(dst, src):
+            nc.scalar.activation(out=dst, in_=src, func=COPY)
+
+        def entries(cols):
+            return offsets[:, cols.start // 16 : cols.stop // 16]
 
         def load_xT(o, h):
             r0 = o * K_PASS + h * HALF
@@ -96,163 +134,107 @@ def tile_attend_gpoi_w_kernel(tc, xT, w_words, w_scales, y, wt, xm, offs, out):
         def load_xm(o, h):
             nc.sync.dma_start(out=xm_raw[o][h][:], in_=xm_v[o, :, :, halves[h]])
 
-        def load_scales():
-            scale_rows = w_scales[0].bitcast(I32)
-            for q in range(4):
-                nc.sync.dma_start(out=table_scales[32 * q : 32 * q + 4, :], in_=scale_rows[4 * q : 4 * q + 4, :])
-
-        def load_words():
-            nc.sync.dma_start(out=table_words[:], in_=w_words[0].rearrange("p n t -> p (n t)").bitcast(I32))
+        def dealt(h):
+            return slice(h * (P // 2), (h + 1) * (P // 2))
 
         def round_xT(o, h, copy):
-            m = slice(h * (P // 2), (h + 1) * (P // 2))
             copy(
-                out=xT_bf[o][:, :, m, :].rearrange("p t m j -> p m j t"),
-                in_=xT_raw[o][h][:].rearrange("p j (m t) -> p m j t", t=PACK),
+                xT_bf[o][:, :, dealt(h), :].rearrange("p t m j -> p m j t"),
+                xT_raw[o][h][:].rearrange("p j (m t) -> p m j t", t=PACK),
             )
 
-        def quantize_xT(o):
-            nc.vector.quantize_mx(
-                out=xT_codes[o][:].bitcast(E4M3),
-                scales=xT_sc[o][:],
-                in_=xT_bf[o][:].rearrange("p t m j -> p (t m j)"),
+        def quantize(codes, scales, values):
+            nc.vector.quantize_mx(out=codes, scales=scales, in_=values)
+
+        def score(o, h, t, scores):
+            rows = slice(t * P, (t + 1) * P)
+            nc.tensor.matmul_mx(
+                out=scores,
+                lhsT=xT_codes[o][:, rows].bitcast(E4M3),
+                lhsT_scale=xT_sc[o][:, rows],
+                rhs=w_codes[:, halves[h]].bitcast(E4M3),
+                rhs_scale=w_sc[:, halves[h]],
+                start=True,
+                stop=True,
             )
 
-        def gather_scales():
-            nc.vector.tensor_copy(w_sc[:], table_scales[:].bitcast(U8).indirect(offsets[:]))
+        def means(o, h, pair, b):
+            scores = bank[b][:].rearrange("p (e i) -> p e i", e=2)
+            for e in range(2):
+                score(o, h, 2 * pair + e, scores[:, e, :])
+            nc.scalar.activation(out=mean[o][h][:, 2 * pair : 2 * pair + 2, :], in_=scores, func=EXP)
 
-        def gather_words(h):
-            nc.vector.tensor_copy(
-                w_codes[:, halves[h]],
-                table_words[:].bitcast(U32).indirect(offsets[:, h * HALF // 16 : (h + 1) * HALF // 16]),
-            )
+        def subtract(o, h, places):
+            nc.vector.tensor_tensor(work[o][h][:, places, :], y_sb[o][h][:, places, :], mean[o][h][:, places, :], SUB)
 
-        def means(o, h, banks):
-            cols = halves[h]
-            for u, b in banks.items():
-                a = bank[b][:].rearrange("p (e i) -> p e i", e=2)
-                for e in range(2):
-                    rows = slice((2 * u + e) * P, (2 * u + e + 1) * P)
-                    nc.tensor.matmul_mx(
-                        out=a[:, e, :],
-                        lhsT=xT_codes[o][:, rows].bitcast(E4M3),
-                        lhsT_scale=xT_sc[o][:, rows],
-                        rhs=w_codes[:, cols].bitcast(E4M3),
-                        rhs_scale=w_sc[:, cols],
-                        start=True,
-                        stop=True,
-                    )
-                nc.scalar.activation(out=mean[o][h][:, 2 * u : 2 * u + 2, :], in_=a, func=EXP)
-
-        def first_means():
-            for t, b in ((0, 3), (1, 0)):
-                nc.tensor.matmul_mx(
-                    out=bank[b][:, lo],
-                    lhsT=xT_codes[0][:, t * P : (t + 1) * P].bitcast(E4M3),
-                    lhsT_scale=xT_sc[0][:, t * P : (t + 1) * P],
-                    rhs=w_codes[:, lo].bitcast(E4M3),
-                    rhs_scale=w_sc[:, lo],
-                    start=True,
-                    stop=True,
-                )
-                nc.scalar.activation(out=mean[0][0][:, t, :], in_=bank[b][:, lo], func=EXP)
-
-        def interleave(copy, out, in_, cols=lo):
-            copy(
-                out=out[:, cols, :].rearrange("p (c i) t -> p c t i", i=RUN),
-                in_=in_[:, :, cols].rearrange("p t (c i) -> p c t i", i=RUN),
-            )
-
-        def resid(o, s):
-            return work[o][0][:].rearrange("p t i -> p (t i)").rearrange("p (s t i) -> p s t i", s=2, t=PACK)[:, s]
-
-        def residual(o, h):
-            for pair in (slice(0, 2), slice(2, 4)):
-                nc.vector.tensor_tensor(work[o][h][:, pair, :], y_sb[o][h][:, pair, :], mean[o][h][:, pair, :], SUB)
-
-        def weigh(o, h):
+        def low_rows(o):
+            subtract(o, 0, slice(0, 2))
+            subtract(o, 0, slice(2, 4))
             for t in range(PACK):
-                nc.vector.tensor_scalar(
-                    g_rows[o][h][:, t, :], work[o][h][:, t, :], wt_sb[:, o, t : t + 1], None, MUL
-                )
+                nc.vector.tensor_scalar(g_rows[o][0][:, t, :], work[o][0][:, t, :], wt_sb[:, o, t : t + 1], None, MUL)
 
-        def weigh_means(o, h, places):
+        def weigh_on_scalar(dst, src, o, places):
             for t in places:
-                nc.scalar.activation(
-                    out=work[o][h][:, t, :], in_=mean[o][h][:, t, :], func=COPY, scale=wt_sb[:, o, t : t + 1]
-                )
+                nc.scalar.activation(out=dst[:, t, :], in_=src[:, t, :], func=COPY, scale=wt_sb[:, o, t : t + 1])
 
-        def finish_rows(o, h, places):
+        def finish_rows(o, places):
             for t in places:
                 nc.vector.scalar_tensor_tensor(
-                    g_rows[o][h][:, t, :], y_sb[o][h][:, t, :], wt_sb[:, o, t : t + 1], work[o][h][:, t, :], MUL, SUB
+                    g_rows[o][1][:, t, :], y_sb[o][1][:, t, :], wt_sb[:, o, t : t + 1], work[o][1][:, t, :], MUL, SUB
                 )
 
-        def interleave_g(o, h, copy, cols=lo):
-            interleave(copy, g_bf[o][h], g_rows[o][h], cols)
+        def interleave(copy, dst, src, cols=lo):
+            copy(
+                dst[:, cols, :].rearrange("p (c i) t -> p c t i", i=RUN),
+                src[:, :, cols].rearrange("p t (c i) -> p c t i", i=RUN),
+            )
+
+        def interleave_on_gpsimd(dst, src, cols):
+            nc.gpsimd.tensor_scalar(dst[:, cols, :], src[:, :, cols].rearrange("p t i -> p i t"), 1.0, 0.0, MUL, ADD)
 
         def quantize_g(o, h):
-            nc.vector.quantize_mx(
-                out=g_codes[o][:, halves[h]].bitcast(E5M2),
-                scales=g_sc[o][:, halves[h]],
-                in_=g_bf[o][h][:].rearrange("p i t -> p (i t)"),
+            quantize(
+                g_codes[o][:, halves[h]].bitcast(E5M2),
+                g_sc[o][:, halves[h]],
+                g_bf[o][h][:].rearrange("p i t -> p (i t)"),
             )
-
-        def round_xm(o, h, copy, cols=lo):
-            interleave(copy, xm_bf[o][h], xm_raw[o][h], cols)
 
         def quantize_xm(o, h):
-            nc.vector.quantize_mx(
-                out=xm_codes[o][h][:].bitcast(E4M3),
-                scales=xm_sc[o][h][:],
-                in_=xm_bf[o][h][:].rearrange("p d t -> p (d t)"),
-            )
-
-        def gradient_pass(c, o, dw, first):
-            h, rows = c // 2, slice(c % 2 * P, (c % 2 + 1) * P)
-            nc.tensor.matmul_mx(
-                out=dw[:],
-                lhsT=xm_codes[o][h][:, rows].bitcast(E4M3),
-                lhsT_scale=xm_sc[o][h][:, rows],
-                rhs=g_codes[o][:].bitcast(E5M2),
-                rhs_scale=g_sc[o][:],
-                start=first,
-                stop=not first,
-            )
+            quantize(xm_codes[o][h][:].bitcast(E4M3), xm_sc[o][h][:], xm_bf[o][h][:].rearrange("p d t -> p (d t)"))
 
         def multiply(c, b):
+            h, features = c // 2, slice(c % 2 * P, (c % 2 + 1) * P)
             order = (0, 1) if c == 0 else (1, 0)
             for o in order:
-                gradient_pass(c, o, bank[b], o == order[0])
+                nc.tensor.matmul_mx(
+                    out=bank[b][:],
+                    lhsT=xm_codes[o][h][:, features].bitcast(E4M3),
+                    lhsT_scale=xm_sc[o][h][:, features],
+                    rhs=g_codes[o][:].bitcast(E5M2),
+                    rhs_scale=g_sc[o][:],
+                    start=o == order[0],
+                    stop=o == order[1],
+                )
 
-        def gradient(c, cols, b, dw_sb=None):
-            multiply(c, b)
-            return drain(c, cols, b, dw_sb)
-
-        def drain(c, cols, b, dw_sb=None):
-            dw = bank[b]
-            if dw_sb is None:
-                dw_sb = keep.tile([P, cols.stop - cols.start], F32, name=f"dw_sb{c}_{cols.start}")[:]
-            nc.scalar.activation(out=dw_sb, in_=dw[:, cols], func=COPY, scale=-1.0)
-            return dw_sb
+        def drain(b, cols, dw_sb):
+            nc.scalar.activation(out=dw_sb, in_=bank[b][:, cols], func=COPY, scale=-1.0)
 
         def scatter(c, cols, dw_sb):
-            nc.vector.tensor_copy(
-                windows[c % WINDOWS][:].indirect(offsets[:, cols.start // 16 : cols.stop // 16]), dw_sb
-            )
+            nc.vector.tensor_copy(windows[c % WINDOWS][:].indirect(entries(cols)), dw_sb)
 
         def store(c):
             nc.sync.dma_start(out=out[c * P : (c + 1) * P, :], in_=windows[c % WINDOWS][:])
 
-        on_vector, on_scalar = nc.vector.tensor_copy, nc.scalar.copy
-
         nc.gpsimd.memset(table_scales[:, : T // 8], 0)
         nc.vector.memset(table_scales[:, T // 8 :], 0)
+
         load_xT(0, 0)
         nc.sync.dma_start(offsets[:], offs)
-        load_scales()
+        scale_rows = w_scales[0].bitcast(I32)
+        for q in range(4):
+            nc.sync.dma_start(out=table_scales[32 * q : 32 * q + 4, :], in_=scale_rows[4 * q : 4 * q + 4, :])
         load_xT(0, 1)
-        load_words()
+        nc.sync.dma_start(out=table_words[:], in_=w_words[0].rearrange("p n t -> p (n t)").bitcast(I32))
         load_xT(1, 0)
         load_xT(1, 1)
         load_y(0, 0)
@@ -271,98 +253,84 @@ def tile_attend_gpoi_w_kernel(tc, xT, w_words, w_scales, y, wt, xm, offs, out):
             nc.vector.memset(g_codes[o][:, hi], 0)
             nc.vector.memset(g_sc[o][:, hi].bitcast(I32), 0)
 
-        work[0][1] = raw_low[:, : PACK * HALF].rearrange("p (t i) -> p t i", t=PACK)
-        for o in range(PASSES):
-            xm_bf[o][0] = resid(0, o).rearrange("p t i -> p (t i)").bitcast(BF16).rearrange("p (d t) -> p d t", t=PACK)
-        g_bf[0][1] = y_sb[1][1][:].rearrange("p t i -> p (t i)").bitcast(BF16)[:, 2 * HALF - PACK * SCALAR_COLS : 6 * HALF - PACK * SCALAR_COLS].rearrange("p (d t) -> p d t", t=PACK)
-        xm_bf[0][1] = g_bf[1][1]
-        xm_bf[1][1] = g_bf[0][1]
-        early0_sb = mean[1][1][:, 0, :]
-        early1_sb = g_rows[0][1][:].rearrange("p t i -> p (t i)").bitcast(F32)[:, :HALF]
-
-        gather_scales()
-        round_xT(0, 0, lambda out, in_: nc.scalar.activation(out=out, in_=in_, func=COPY))
+        nc.vector.tensor_copy(w_sc[:], table_scales[:].bitcast(U8).indirect(offsets[:]))
+        round_xT(0, 0, on_scalar_activation)
         round_xT(0, 1, on_scalar)
-        quantize_xT(0)
-        gather_words(0)
-        gather_words(1)
-        first_means()
-        means(0, 0, {1: 1})
+        quantize(xT_codes[0][:].bitcast(E4M3), xT_sc[0][:], xT_bf[0][:].rearrange("p t m j -> p (t m j)"))
+        for cols in halves:
+            nc.vector.tensor_copy(w_codes[:, cols], table_words[:].bitcast(U32).indirect(entries(cols)))
+
+        for t, b in ((0, 3), (1, 0)):
+            score(0, 0, t, bank[b][:, lo])
+            nc.scalar.activation(out=mean[0][0][:, t, :], in_=bank[b][:, lo], func=EXP)
+        means(0, 0, 1, 1)
+
         round_xT(1, 0, on_vector)
         round_xT(1, 1, on_vector)
         for h in range(2):
             for t in range(PACK):
-                m = slice(h * (P // 2), (h + 1) * (P // 2))
-                cols = slice(t * P + m.start, t * P + m.stop)
-                nc.vector.quantize_mx(
-                    out=xT_codes[1][:, cols].bitcast(E4M3),
-                    scales=xT_sc[1][:, cols],
-                    in_=xT_bf[1][:, t, m, :].rearrange("p m j -> p (m j)"),
+                cols = slice(t * P + dealt(h).start, t * P + dealt(h).stop)
+                quantize(
+                    xT_codes[1][:, cols].bitcast(E4M3),
+                    xT_sc[1][:, cols],
+                    xT_bf[1][:, t, dealt(h), :].rearrange("p m j -> p (m j)"),
                 )
-        residual(0, 0)
-        weigh(0, 0)
-        interleave_g(0, 0, on_vector, slice(0, FIRST_COLS))
-        means(1, 0, {0: 0, 1: 1})
-        residual(1, 0)
-        weigh(1, 0)
-        interleave_g(1, 0, on_vector)
-        interleave_g(0, 0, on_scalar, slice(FIRST_COLS, HALF))
-        round_xm(0, 0, on_scalar)
-        round_xm(1, 0, on_scalar)
-        quantize_g(0, 0)
-        quantize_xm(0, 0)
-        quantize_g(1, 0)
-        quantize_xm(1, 0)
+
+        low_rows(0)
+        interleave(on_vector, g_bf[0][0], g_rows[0][0], slice(0, FIRST_G_VECTOR))
+        means(1, 0, 0, 0)
+        means(1, 0, 1, 1)
+        low_rows(1)
+        interleave(on_vector, g_bf[1][0], g_rows[1][0])
+        interleave(on_scalar, g_bf[0][0], g_rows[0][0], slice(FIRST_G_VECTOR, HALF))
+        for o in range(PASSES):
+            interleave(on_scalar, xm_bf[o][0], xm_raw[o][0])
+        for o in range(PASSES):
+            quantize_g(o, 0)
+            quantize_xm(o, 0)
         multiply(0, 3)
         multiply(1, 4)
-        means(0, 1, {0: 2, 1: 7})
-        means(1, 1, {1: 0, 0: 1})
-        weigh_means(0, 1, range(PACK))
-        weigh_means(1, 1, range(2))
-        finish_rows(0, 1, range(PACK))
-        nc.vector.tensor_tensor(work[1][1][:, 2:, :], y_sb[1][1][:, 2:, :], mean[1][1][:, 2:, :], SUB)
-        finish_rows(1, 1, range(2))
-        early0 = drain(0, lo, 3, early0_sb)
-        interleave_g(0, 1, on_scalar, slice(0, SCALAR_COLS))
-        for t in (2, 3):
-            nc.scalar.activation(
-                out=g_rows[1][1][:, t, :], in_=work[1][1][:, t, :], func=COPY, scale=wt_sb[:, 1, t : t + 1]
-            )
-        interleave_g(1, 1, on_scalar)
-        nc.gpsimd.tensor_scalar(
-            g_bf[0][1][:, SCALAR_COLS:, :],
-            g_rows[0][1][:, :, SCALAR_COLS:].rearrange("p t i -> p i t"),
-            1.0,
-            0.0,
-            MUL,
-            ADD,
-        )
-        early1 = drain(1, lo, 4, early1_sb)
-        scatter(0, lo, early0)
+
+        means(0, 1, 0, 2)
+        means(0, 1, 1, 7)
+        means(1, 1, 1, 0)
+        means(1, 1, 0, 1)
+        weigh_on_scalar(work[0][1], mean[0][1], 0, range(PACK))
+        weigh_on_scalar(work[1][1], mean[1][1], 1, range(2))
+        finish_rows(0, range(PACK))
+        subtract(1, 1, slice(2, 4))
+        finish_rows(1, range(2))
+        drain(3, lo, early_sb[0])
+        interleave(on_scalar, g_bf[0][1], g_rows[0][1], slice(0, HIGH_G_SCALAR))
+        weigh_on_scalar(g_rows[1][1], work[1][1], 1, range(2, PACK))
+        interleave(on_scalar, g_bf[1][1], g_rows[1][1])
+        interleave_on_gpsimd(g_bf[0][1], g_rows[0][1], slice(HIGH_G_SCALAR, HALF))
+        drain(4, lo, early_sb[1])
+        scatter(0, lo, early_sb[0])
         quantize_g(0, 1)
         quantize_g(1, 1)
-        scatter(1, lo, early1)
-        nc.gpsimd.tensor_scalar(
-            xm_bf[0][1][:, :POOL_COLS, :],
-            xm_raw[0][1][:, :, :POOL_COLS].rearrange("p t d -> p d t"),
-            1.0,
-            0.0,
-            MUL,
-            ADD,
-        )
-        round_xm(1, 1, on_scalar)
-        round_xm(0, 1, on_scalar, slice(POOL_COLS, HALF))
-        late0 = gradient(0, hi, 5, xm_raw[1][1][:, 0, :])
-        late1 = gradient(1, hi, 6, xm_raw[1][1][:, 1, :])
+
+        scatter(1, lo, early_sb[1])
+        interleave_on_gpsimd(xm_bf[0][1], xm_raw[0][1], slice(0, HIGH_XM_GPSIMD))
+        interleave(on_scalar, xm_bf[1][1], xm_raw[1][1])
+        interleave(on_scalar, xm_bf[0][1], xm_raw[0][1], slice(HIGH_XM_GPSIMD, HALF))
+        for c, b in ((0, 5), (1, 6)):
+            multiply(c, b)
+            drain(b, hi, late_sb[c])
         quantize_xm(1, 1)
         quantize_xm(0, 1)
-        windows.append(keep.tile([P, T], F32, align_bytes=64, name="window2", tag="last"))
+
+        windows.append(tile("window2", [P, T], F32, tag="last"))
         nc.gpsimd.memset(windows[2][:], 0.0)
-        scatter(0, hi, late0)
+        scatter(0, hi, late_sb[0])
         store(0)
-        rest = [gradient(2, both, 7), gradient(3, both, 2)]
-        scatter(1, hi, late1)
+        whole_sb = {}
+        for c, b in ((2, 7), (3, 2)):
+            multiply(c, b)
+            whole_sb[c] = keep.tile([P, N], F32, name=f"whole_sb{c}")[:]
+            drain(b, both, whole_sb[c])
+        scatter(1, hi, late_sb[1])
         store(1)
         for c in range(2, D_BLOCKS):
-            scatter(c, both, rest[c - 2])
+            scatter(c, both, whole_sb[c])
             store(c)

@@ -26,11 +26,8 @@ PASSES = R // K_PASS
 D_BLOCKS = D // P
 HALF = 256
 UNIT = PACK * HALF
-WINDOWS = 3
 RUN = 4
-FIRST_G_VECTOR = 160
-HIGH_G_SCALAR = 64
-HIGH_XM_GPSIMD = 128
+EARLY_COLS = 192
 
 
 def tile_attend_gpoi_w_kernel(tc, xT, w_words, w_scales, y, wt, xm, offs, out):
@@ -49,16 +46,10 @@ def tile_attend_gpoi_w_kernel(tc, xT, w_words, w_scales, y, wt, xm, offs, out):
         def passes(name, shape, dtype):
             return [tile(f"{name}{o}", shape, dtype) for o in range(PASSES)]
 
-        def flat(ap):
-            return ap[:].rearrange("p t i -> p (t i)")
-
-        def by_place(ap):
-            return ap.rearrange("p (t i) -> p t i", t=PACK)
-
         def by_word(ap):
             return ap.rearrange("p (i t) -> p i t", t=PACK)
 
-        placed, worded = [P, PACK, HALF], [P, HALF, PACK]
+        placed = [P, PACK, HALF]
 
         offsets = keep.tile([P, N // 16], U16)
         table_words = tile("table_words", [P, T], I32)
@@ -67,49 +58,61 @@ def tile_attend_gpoi_w_kernel(tc, xT, w_words, w_scales, y, wt, xm, offs, out):
         wt_sb = wt_rows[:, :, :PACK]
         xT_raw = units("xT_raw", placed, F32)
         y_sb = units("y_sb", placed, F32)
-        raw_low = tile("raw_low", [P, UNIT + 2 * HALF], F32)
-        xm_raw = [
-            [by_place(raw_low[:, 2 * HALF :]), tile("xm_raw01", placed, F32)],
-            [tile("xm_raw10", placed, F32), tile("xm_raw11", placed, F32)],
+        last_words = tile("last_words", [P, EARLY_COLS + UNIT], F32)
+        late_raw = [
+            tile("late_raw0", [P, PASSES, PACK, P], F32),
+            last_words[:, EARLY_COLS:].rearrange("p (o t i) -> p o t i", o=PASSES, t=PACK),
         ]
-        windows = [tile(f"window{c}", [P, T], F32) for c in range(WINDOWS - 1)]
+        windows = [tile(f"window{c}", [P, T], F32) for c in range(D_BLOCKS)]
 
         w_codes = tile("w_codes", [P, N], U32)
         w_sc = tile("w_sc", [P, N], U8)
         xT_bf = passes("xT_bf", [P, PACK, P, PACK], BF16)
         xT_codes = passes("xT_codes", [P, K_PASS], U32)
         xT_sc = passes("xT_sc", [P, K_PASS], U8)
-        xm_codes = units("xm_codes", [P, HALF], U32)
-        xm_sc = units("xm_sc", [P, HALF], U8)
-        g_rows = units("g_rows", placed, BF16)
-        g_codes = passes("g_codes", [P, N], I32)
-        g_sc = passes("g_sc", [P, N], U8)
+        xm_codes = [tile(f"xm_codes{c}", [P, PASSES * P], U32) for c in range(D_BLOCKS)]
+        xm_sc = [tile(f"xm_sc{c}", [P, PASSES * P], U8) for c in range(D_BLOCKS)]
+        high_words = tile("high_words", [P, UNIT], F32)
+        high_pair = high_words[:].bitcast(BF16)
+        g_rows = [
+            [tile("g_rows00", placed, BF16), high_pair[:, UNIT:].rearrange("p (t i) -> p t i", t=PACK)],
+            [tile("g_rows10", placed, BF16), tile("g_rows11", placed, BF16)],
+        ]
+        g_codes = units("g_codes", [P, HALF], U32)
+        g_sc = units("g_sc", [P, HALF], U8)
+        mean = units("mean", placed, F32)
+        work = units("work", placed, F32)
+        g_flat = [
+            [tile("g_flat00", [P, UNIT], BF16), tile("g_flat01", [P, UNIT], BF16)],
+            [tile("g_flat10", [P, UNIT], BF16), high_pair[:, :UNIT]],
+        ]
+        g_bf = [[by_word(g_flat[o][h][:]) for h in range(2)] for o in range(PASSES)]
+        dw_sb = [[tile(f"dw_sb{c}{h}", [P, HALF], F32)[:] for h in range(2)] for c in range(D_BLOCKS)]
 
-        mean = [
-            [tile("mean00", placed, F32), tile("mean01", placed, F32)],
-            [tile("mean10", placed, F32), xm_raw[1][0]],
+        last_g = high_pair[:, :UNIT]
+        first_raw = [
+            work[1][1][:, places, :].rearrange("p e (u i) -> p (e u) i", u=2) for places in (slice(2, 4), slice(0, 2))
         ]
-        work = [
-            [tile("work00", placed, F32), by_place(raw_low[:, :UNIT])],
-            [tile("work10", placed, F32), tile("work11", placed, F32)],
+        second_raw = [
+            tile("second_raw0", [P, PACK, P], F32)[:],
+            high_words[:, :K_PASS].rearrange("p (t i) -> p t i", t=PACK),
         ]
-        g_high0 = 2 * HALF - PACK * HIGH_G_SCALAR
-        g_bf = [
-            [tile("g_bf00", worded, BF16), by_word(flat(y_sb[1][1]).bitcast(BF16)[:, g_high0 : g_high0 + UNIT])],
-            [tile("g_bf10", worded, BF16), tile("g_bf11", worded, BF16, tag="last")],
+        xm_raw = [first_raw, second_raw] + [[raw[:, o, :, :] for o in range(PASSES)] for raw in late_raw]
+        first_rows = g_rows[0][0][:].rearrange("p t i -> p (t i)")
+        xm_flat = [
+            [first_rows[:, :K_PASS], first_rows[:, K_PASS:]],
+            [work[1][1][:, 1, :].bitcast(BF16), work[1][1][:, 2, :].bitcast(BF16)],
+            [last_g[:, :K_PASS], last_g[:, K_PASS:]],
+            [last_g[:, :K_PASS], last_g[:, K_PASS:]],
         ]
-        first_residual = flat(work[0][0]).bitcast(BF16)
-        xm_bf = [
-            [by_word(first_residual[:, :UNIT]), g_bf[1][1]],
-            [by_word(first_residual[:, UNIT:]), g_bf[0][1]],
-        ]
-        early_sb = [mean[1][1][:, 0, :], flat(g_rows[0][1]).bitcast(F32)[:, :HALF]]
-        late_sb = [xm_raw[1][1][:, 0, :], xm_raw[1][1][:, 1, :]]
+        last_dw = tile("last_dw", [P, N], F32)
+        dw_sb[1][0] = late_raw[0][:, 0, 2:, :].rearrange("p t i -> p (t i)")
+        dw_sb[1][1] = last_words[:, :HALF]
 
         xT_v = xT[0].rearrange("(p j) r -> p j r", j=PACK)
         y_v = y[0].rearrange("(o p t) i -> o p t i", o=PASSES, t=PACK)
         xm_v = xm[0].rearrange("(o p t) d -> o p t d", o=PASSES, t=PACK)
-        lo, hi, both = slice(0, HALF), slice(HALF, N), slice(0, N)
+        lo, hi = slice(0, HALF), slice(HALF, N)
         halves = (lo, hi)
 
         def on_vector(dst, src):
@@ -121,6 +124,11 @@ def tile_attend_gpoi_w_kernel(tc, xT, w_words, w_scales, y, wt, xm, offs, out):
         def on_scalar_activation(dst, src):
             nc.scalar.activation(out=dst, in_=src, func=COPY)
 
+        def zero_on_vector(words):
+            cut = words.shape[1] // 2 - 1
+            nc.vector.memset(words[:, :cut], 0)
+            nc.vector.memset(words[:, cut:], 0)
+
         def entries(cols):
             return offsets[:, cols.start // 16 : cols.stop // 16]
 
@@ -131,8 +139,9 @@ def tile_attend_gpoi_w_kernel(tc, xT, w_words, w_scales, y, wt, xm, offs, out):
         def load_y(o, h):
             nc.sync.dma_start(out=y_sb[o][h][:], in_=y_v[o, :, :, halves[h]])
 
-        def load_xm(o, h):
-            nc.sync.dma_start(out=xm_raw[o][h][:], in_=xm_v[o, :, :, halves[h]])
+        def load_xm(c, o):
+            nc.sync.dma_start(out=xm_raw[c][o], in_=xm_v[o, :, :, c * P : (c + 1) * P])
+
 
         def dealt(h):
             return slice(h * (P // 2), (h + 1) * (P // 2))
@@ -164,69 +173,89 @@ def tile_attend_gpoi_w_kernel(tc, xT, w_words, w_scales, y, wt, xm, offs, out):
                 score(o, h, 2 * pair + e, scores[:, e, :])
             nc.scalar.activation(out=mean[o][h][:, 2 * pair : 2 * pair + 2, :], in_=scores, func=EXP)
 
-        def subtract(o, h, places):
-            nc.vector.tensor_tensor(work[o][h][:, places, :], y_sb[o][h][:, places, :], mean[o][h][:, places, :], SUB)
-
-        def low_rows(o):
-            subtract(o, 0, slice(0, 2))
-            subtract(o, 0, slice(2, 4))
-            for t in range(PACK):
-                nc.vector.tensor_scalar(g_rows[o][0][:, t, :], work[o][0][:, t, :], wt_sb[:, o, t : t + 1], None, MUL)
-
-        def weigh_on_scalar(dst, src, o, places):
-            for t in places:
-                nc.scalar.activation(out=dst[:, t, :], in_=src[:, t, :], func=COPY, scale=wt_sb[:, o, t : t + 1])
-
-        def finish_rows(o, places):
-            for t in places:
-                nc.vector.scalar_tensor_tensor(
-                    g_rows[o][1][:, t, :], y_sb[o][1][:, t, :], wt_sb[:, o, t : t + 1], work[o][1][:, t, :], MUL, SUB
+        def subtract(o, h):
+            for places in (slice(0, 2), slice(2, 4)):
+                nc.vector.tensor_tensor(
+                    work[o][h][:, places, :], y_sb[o][h][:, places, :], mean[o][h][:, places, :], SUB
                 )
 
-        def interleave(copy, dst, src, cols=lo):
-            copy(
-                dst[:, cols, :].rearrange("p (c i) t -> p c t i", i=RUN),
-                src[:, :, cols].rearrange("p t (c i) -> p c t i", i=RUN),
-            )
+        def weigh_residual(o, h):
+            for t in range(PACK):
+                nc.vector.tensor_scalar(g_rows[o][h][:, t, :], work[o][h][:, t, :], wt_sb[:, o, t : t + 1], None, MUL)
 
-        def interleave_on_gpsimd(dst, src, cols):
-            nc.gpsimd.tensor_scalar(dst[:, cols, :], src[:, :, cols].rearrange("p t i -> p i t"), 1.0, 0.0, MUL, ADD)
+        def weigh_means(o, h):
+            for t in range(PACK):
+                nc.scalar.activation(
+                    out=work[o][h][:, t, :], in_=mean[o][h][:, t, :], func=COPY, scale=wt_sb[:, o, t : t + 1]
+                )
+
+        def finish_rows(o, h):
+            for t in range(PACK):
+                nc.vector.scalar_tensor_tensor(
+                    g_rows[o][h][:, t, :], y_sb[o][h][:, t, :], wt_sb[:, o, t : t + 1], work[o][h][:, t, :], MUL, SUB
+                )
+
+        def interleave(copy, dst, src):
+            copy(dst.rearrange("p (c i) t -> p c t i", i=RUN), src.rearrange("p t (c i) -> p c t i", i=RUN))
+
+        def interleave_g(o, h, copy, cols=lo):
+            interleave(copy, g_bf[o][h][:, cols, :], g_rows[o][h][:, :, cols])
+
+        def xm_block(c, o):
+            return xm_raw[c][o]
+
+        def round_xm(c, o, copy):
+            interleave(copy, by_word(xm_flat[c][o]), xm_block(c, o))
+
+        def round_last_xm_on_gpsimd():
+            nc.gpsimd.tensor_scalar(
+                last_g[:].rearrange("p (o i t) -> p o i t", o=PASSES, t=PACK),
+                late_raw[1][:].rearrange("p o t i -> p o i t"),
+                1.0,
+                0.0,
+                MUL,
+                ADD,
+            )
 
         def quantize_g(o, h):
-            quantize(
-                g_codes[o][:, halves[h]].bitcast(E5M2),
-                g_sc[o][:, halves[h]],
-                g_bf[o][h][:].rearrange("p i t -> p (i t)"),
-            )
+            quantize(g_codes[o][h][:].bitcast(E5M2), g_sc[o][h][:], g_flat[o][h][:])
 
-        def quantize_xm(o, h):
-            quantize(xm_codes[o][h][:].bitcast(E4M3), xm_sc[o][h][:], xm_bf[o][h][:].rearrange("p d t -> p (d t)"))
+        def quantize_xm(c, o):
+            cols = slice(o * P, (o + 1) * P)
+            quantize(xm_codes[c][:, cols].bitcast(E4M3), xm_sc[c][:, cols], xm_flat[c][o])
 
-        def multiply(c, b):
-            h, features = c // 2, slice(c % 2 * P, (c % 2 + 1) * P)
-            order = (0, 1) if c == 0 else (1, 0)
+        def quantize_late_xm(c):
+            quantize(xm_codes[c][:].bitcast(E4M3), xm_sc[c][:], last_g[:])
+
+        def multiply(c, h, b, order=(0, 1), cols=lo):
             for o in order:
                 nc.tensor.matmul_mx(
-                    out=bank[b][:],
-                    lhsT=xm_codes[o][h][:, features].bitcast(E4M3),
-                    lhsT_scale=xm_sc[o][h][:, features],
-                    rhs=g_codes[o][:].bitcast(E5M2),
-                    rhs_scale=g_sc[o][:],
+                    out=bank[b][:, cols],
+                    lhsT=xm_codes[c][:, o * P : (o + 1) * P].bitcast(E4M3),
+                    lhsT_scale=xm_sc[c][:, o * P : (o + 1) * P],
+                    rhs=g_codes[o][h][:].bitcast(E5M2),
+                    rhs_scale=g_sc[o][h][:],
                     start=o == order[0],
                     stop=o == order[1],
                 )
 
-        def drain(b, cols, dw_sb):
-            nc.scalar.activation(out=dw_sb, in_=bank[b][:, cols], func=COPY, scale=-1.0)
+        def drain_on_scalar(c, h, b):
+            nc.scalar.activation(out=dw_sb[c][h], in_=bank[b][:, lo], func=COPY, scale=-1.0)
 
-        def scatter(c, cols, dw_sb):
-            nc.vector.tensor_copy(windows[c % WINDOWS][:].indirect(entries(cols)), dw_sb)
+        def drain_on_vector(c, h, b, cols=lo):
+            nc.vector.tensor_scalar(dw_sb[c][h][:, cols], bank[b][:, cols], -1.0, None, MUL)
+
+        def scatter_on_scalar(c, h):
+            nc.scalar.activation(out=windows[c][:].indirect(entries(halves[h])), in_=dw_sb[c][h], func=COPY)
+
+        def scatter_on_vector(c, h):
+            nc.vector.tensor_copy(windows[c][:].indirect(entries(halves[h])), dw_sb[c][h])
 
         def store(c):
-            nc.sync.dma_start(out=out[c * P : (c + 1) * P, :], in_=windows[c % WINDOWS][:])
+            nc.sync.dma_start(out=out[c * P : (c + 1) * P, :], in_=windows[c][:])
 
         nc.gpsimd.memset(table_scales[:, : T // 8], 0)
-        nc.vector.memset(table_scales[:, T // 8 :], 0)
+        zero_on_vector(table_scales[:, T // 8 :])
 
         load_xT(0, 0)
         nc.sync.dma_start(offsets[:], offs)
@@ -240,18 +269,18 @@ def tile_attend_gpoi_w_kernel(tc, xT, w_words, w_scales, y, wt, xm, offs, out):
         load_y(0, 0)
         nc.sync.dma_start(out=wt_sb, in_=wt[0].rearrange("(o p t) one -> p o (t one)", o=PASSES, t=PACK))
         load_y(1, 0)
-        load_xm(0, 0)
-        load_xm(1, 0)
         load_y(0, 1)
-        load_y(1, 1)
+        load_xm(0, 0)
         load_xm(0, 1)
-        load_xm(1, 1)
+        load_y(1, 1)
+        for c in range(1, D_BLOCKS):
+            for o in range(PASSES):
+                load_xm(c, o)
 
-        for window in windows:
-            nc.vector.memset(window[:].bitcast(I32), 0)
-        for o in range(PASSES):
-            nc.vector.memset(g_codes[o][:, hi], 0)
-            nc.vector.memset(g_sc[o][:, hi].bitcast(I32), 0)
+        for window in windows[:2]:
+            zero_on_vector(window[:].bitcast(I32))
+        for window in windows[2:]:
+            nc.gpsimd.memset(window[:].bitcast(I32), 0)
 
         nc.vector.tensor_copy(w_sc[:], table_scales[:].bitcast(U8).indirect(offsets[:]))
         round_xT(0, 0, on_scalar_activation)
@@ -264,6 +293,8 @@ def tile_attend_gpoi_w_kernel(tc, xT, w_words, w_scales, y, wt, xm, offs, out):
             score(0, 0, t, bank[b][:, lo])
             nc.scalar.activation(out=mean[0][0][:, t, :], in_=bank[b][:, lo], func=EXP)
         means(0, 0, 1, 1)
+        means(0, 1, 0, 2)
+        means(0, 1, 1, 7)
 
         round_xT(1, 0, on_vector)
         round_xT(1, 1, on_vector)
@@ -276,61 +307,64 @@ def tile_attend_gpoi_w_kernel(tc, xT, w_words, w_scales, y, wt, xm, offs, out):
                     xT_bf[1][:, t, dealt(h), :].rearrange("p m j -> p (m j)"),
                 )
 
-        low_rows(0)
-        interleave(on_vector, g_bf[0][0], g_rows[0][0], slice(0, FIRST_G_VECTOR))
+        subtract(0, 0)
+        weigh_residual(0, 0)
         means(1, 0, 0, 0)
         means(1, 0, 1, 1)
-        low_rows(1)
-        interleave(on_vector, g_bf[1][0], g_rows[1][0])
-        interleave(on_scalar, g_bf[0][0], g_rows[0][0], slice(FIRST_G_VECTOR, HALF))
+        weigh_means(0, 1)
+        subtract(1, 0)
+        weigh_residual(1, 0)
+        interleave_g(0, 0, on_scalar)
+        means(1, 1, 0, 4)
+        means(1, 1, 1, 5)
+        quantize_g(0, 0)
+        interleave_g(1, 0, on_vector)
+        quantize_g(1, 0)
         for o in range(PASSES):
-            interleave(on_scalar, xm_bf[o][0], xm_raw[o][0])
-        for o in range(PASSES):
-            quantize_g(o, 0)
-            quantize_xm(o, 0)
-        multiply(0, 3)
-        multiply(1, 4)
+            round_xm(0, o, on_scalar)
+            quantize_xm(0, o)
+        weigh_means(1, 1)
+        finish_rows(0, 1)
+        interleave_g(0, 1, on_scalar)
+        multiply(0, 0, 6)
+        drain_on_scalar(0, 0, 6)
+        scatter_on_scalar(0, 0)
 
-        means(0, 1, 0, 2)
-        means(0, 1, 1, 7)
-        means(1, 1, 1, 0)
-        means(1, 1, 0, 1)
-        weigh_on_scalar(work[0][1], mean[0][1], 0, range(PACK))
-        weigh_on_scalar(work[1][1], mean[1][1], 1, range(2))
-        finish_rows(0, range(PACK))
-        subtract(1, 1, slice(2, 4))
-        finish_rows(1, range(2))
-        drain(3, lo, early_sb[0])
-        interleave(on_scalar, g_bf[0][1], g_rows[0][1], slice(0, HIGH_G_SCALAR))
-        weigh_on_scalar(g_rows[1][1], work[1][1], 1, range(2, PACK))
-        interleave(on_scalar, g_bf[1][1], g_rows[1][1])
-        interleave_on_gpsimd(g_bf[0][1], g_rows[0][1], slice(HIGH_G_SCALAR, HALF))
-        drain(4, lo, early_sb[1])
-        scatter(0, lo, early_sb[0])
+        finish_rows(1, 1)
+        round_xm(1, 0, on_vector)
+        round_xm(1, 1, on_vector)
+        interleave_g(1, 1, on_vector)
+        quantize_xm(1, 0)
+        quantize_xm(1, 1)
         quantize_g(0, 1)
         quantize_g(1, 1)
-
-        scatter(1, lo, early_sb[1])
-        interleave_on_gpsimd(xm_bf[0][1], xm_raw[0][1], slice(0, HIGH_XM_GPSIMD))
-        interleave(on_scalar, xm_bf[1][1], xm_raw[1][1])
-        interleave(on_scalar, xm_bf[0][1], xm_raw[0][1], slice(HIGH_XM_GPSIMD, HALF))
-        for c, b in ((0, 5), (1, 6)):
-            multiply(c, b)
-            drain(b, hi, late_sb[c])
-        quantize_xm(1, 1)
-        quantize_xm(0, 1)
-
-        windows.append(tile("window2", [P, T], F32, tag="last"))
-        nc.gpsimd.memset(windows[2][:], 0.0)
-        scatter(0, hi, late_sb[0])
+        multiply(1, 0, 2)
+        multiply(0, 1, 3)
+        drain_on_scalar(0, 1, 3)
+        scatter_on_scalar(0, 1)
         store(0)
-        whole_sb = {}
-        for c, b in ((2, 7), (3, 2)):
-            multiply(c, b)
-            whole_sb[c] = keep.tile([P, N], F32, name=f"whole_sb{c}")[:]
-            drain(b, both, whole_sb[c])
-        scatter(1, hi, late_sb[1])
+
+        multiply(1, 1, 7, order=(1, 0))
+        round_xm(2, 0, on_vector)
+        round_xm(2, 1, on_vector)
+        drain_on_vector(1, 0, 2)
+        quantize_late_xm(2)
+        drain_on_vector(1, 1, 7, slice(0, EARLY_COLS))
+        round_last_xm_on_gpsimd()
+        scatter_on_vector(1, 0)
+        multiply(2, 0, 0)
+        multiply(2, 1, 1)
+        drain_on_vector(1, 1, 7, slice(EARLY_COLS, HALF))
+        quantize_late_xm(3)
+        scatter_on_vector(1, 1)
         store(1)
-        for c in range(2, D_BLOCKS):
-            scatter(c, both, whole_sb[c])
-            store(c)
+        for h, b in ((0, 0), (1, 1)):
+            drain_on_scalar(2, h, b)
+        for h in range(2):
+            scatter_on_scalar(2, h)
+        store(2)
+        for h in range(2):
+            multiply(3, h, 4, cols=halves[h])
+        nc.vector.tensor_scalar(last_dw[:], bank[4][:], -1.0, None, MUL)
+        nc.vector.tensor_copy(windows[3][:].indirect(offsets[:]), last_dw[:])
+        store(3)

@@ -27,7 +27,6 @@ D_BLOCKS = D // P
 HALF = 256
 UNIT = PACK * HALF
 RUN = 4
-EARLY_COLS = 192
 
 
 def tile_attend_gpoi_w_kernel(tc, xT, w_words, w_scales, y, wt, xm, offs, out):
@@ -58,10 +57,10 @@ def tile_attend_gpoi_w_kernel(tc, xT, w_words, w_scales, y, wt, xm, offs, out):
         wt_sb = wt_rows[:, :, :PACK]
         xT_raw = units("xT_raw", placed, F32)
         y_sb = units("y_sb", placed, F32)
-        last_words = tile("last_words", [P, EARLY_COLS + UNIT], F32)
+        last_words = tile("last_words", [P, HALF + UNIT], F32)
         late_raw = [
             tile("late_raw0", [P, PASSES, PACK, P], F32),
-            last_words[:, EARLY_COLS:].rearrange("p (o t i) -> p o t i", o=PASSES, t=PACK),
+            last_words[:, HALF:].rearrange("p (o t i) -> p o t i", o=PASSES, t=PACK),
         ]
         windows = [tile(f"window{c}", [P, T], F32) for c in range(D_BLOCKS)]
 
@@ -89,6 +88,7 @@ def tile_attend_gpoi_w_kernel(tc, xT, w_words, w_scales, y, wt, xm, offs, out):
         g_bf = [[by_word(g_flat[o][h][:]) for h in range(2)] for o in range(PASSES)]
         dw_sb = [[tile(f"dw_sb{c}{h}", [P, HALF], F32)[:] for h in range(2)] for c in range(D_BLOCKS)]
 
+        lo_cols, hi_cols = slice(0, HALF), slice(HALF, N)
         last_g = high_pair[:, :UNIT]
         first_raw = [
             work[1][1][:, places, :].rearrange("p e (u i) -> p (e u) i", u=2) for places in (slice(2, 4), slice(0, 2))
@@ -105,9 +105,8 @@ def tile_attend_gpoi_w_kernel(tc, xT, w_words, w_scales, y, wt, xm, offs, out):
             [last_g[:, :K_PASS], last_g[:, K_PASS:]],
             [last_g[:, :K_PASS], last_g[:, K_PASS:]],
         ]
-        last_dw = tile("last_dw", [P, N], F32)
+        dw_sb[2] = [last_words[:, lo_cols], last_words[:, hi_cols]]
         dw_sb[1][0] = late_raw[0][:, 0, 2:, :].rearrange("p t i -> p (t i)")
-        dw_sb[1][1] = last_words[:, :HALF]
 
         xT_v = xT[0].rearrange("(p j) r -> p j r", j=PACK)
         y_v = y[0].rearrange("(o p t) i -> o p t i", o=PASSES, t=PACK)
@@ -349,22 +348,21 @@ def tile_attend_gpoi_w_kernel(tc, xT, w_words, w_scales, y, wt, xm, offs, out):
         round_xm(2, 1, on_vector)
         drain_on_vector(1, 0, 2)
         quantize_late_xm(2)
-        drain_on_vector(1, 1, 7, slice(0, EARLY_COLS))
+        drain_on_vector(1, 1, 7)
         round_last_xm_on_gpsimd()
         scatter_on_vector(1, 0)
         multiply(2, 0, 0)
         multiply(2, 1, 1)
-        drain_on_vector(1, 1, 7, slice(EARLY_COLS, HALF))
-        quantize_late_xm(3)
-        scatter_on_vector(1, 1)
+        drain_on_scalar(2, 0, 0)
+        scatter_on_scalar(1, 1)
         store(1)
-        for h, b in ((0, 0), (1, 1)):
-            drain_on_scalar(2, h, b)
-        for h in range(2):
-            scatter_on_scalar(2, h)
+        drain_on_vector(2, 1, 1)
+        quantize_late_xm(3)
+        nc.vector.tensor_copy(windows[2][:].indirect(offsets[:]), last_words[:, :N])
         store(2)
+        for h, b in ((0, 4), (1, 5)):
+            multiply(3, h, b)
+            drain_on_scalar(3, h, b)
         for h in range(2):
-            multiply(3, h, 4, cols=halves[h])
-        nc.vector.tensor_scalar(last_dw[:], bank[4][:], -1.0, None, MUL)
-        nc.vector.tensor_copy(windows[3][:].indirect(offsets[:]), last_dw[:])
+            scatter_on_scalar(3, h)
         store(3)

@@ -98,10 +98,10 @@ def tile_attend_gpoi_w_kernel(tc, xT, w_words, w_scales, y, wt, xm, offs, out):
             high_words[:, :K_PASS].rearrange("p (t i) -> p t i", t=PACK),
         ]
         xm_raw = [first_raw, second_raw] + [[raw[:, o, :, :] for o in range(PASSES)] for raw in late_raw]
-        first_rows = g_rows[0][0][:].rearrange("p t i -> p (t i)")
+        first_rows = mean[1][0][:, :2, :].rearrange("p t i -> p (t i)").bitcast(BF16)
         xm_flat = [
             [first_rows[:, :K_PASS], first_rows[:, K_PASS:]],
-            [work[1][1][:, 1, :].bitcast(BF16), work[1][1][:, 2, :].bitcast(BF16)],
+            [work[1][1][:, 2, :].bitcast(BF16), mean[1][1][:, 2, :].bitcast(BF16)],
             [last_g[:, :K_PASS], last_g[:, K_PASS:]],
             [last_g[:, :K_PASS], last_g[:, K_PASS:]],
         ]
@@ -113,6 +113,7 @@ def tile_attend_gpoi_w_kernel(tc, xT, w_words, w_scales, y, wt, xm, offs, out):
         xm_v = xm[0].rearrange("(o p t) d -> o p t d", o=PASSES, t=PACK)
         lo, hi = slice(0, HALF), slice(HALF, N)
         halves = (lo, hi)
+        quarters = (slice(0, P), slice(P, HALF))
 
         def on_vector(dst, src):
             nc.vector.tensor_copy(out=dst, in_=src)
@@ -173,14 +174,18 @@ def tile_attend_gpoi_w_kernel(tc, xT, w_words, w_scales, y, wt, xm, offs, out):
             nc.scalar.activation(out=mean[o][h][:, 2 * pair : 2 * pair + 2, :], in_=scores, func=EXP)
 
         def subtract(o, h):
-            for places in (slice(0, 2), slice(2, 4)):
-                nc.vector.tensor_tensor(
-                    work[o][h][:, places, :], y_sb[o][h][:, places, :], mean[o][h][:, places, :], SUB
-                )
+            for cols in quarters:
+                nc.vector.tensor_tensor(work[o][h][:, :, cols], y_sb[o][h][:, :, cols], mean[o][h][:, :, cols], SUB)
 
-        def weigh_residual(o, h):
-            for t in range(PACK):
-                nc.vector.tensor_scalar(g_rows[o][h][:, t, :], work[o][h][:, t, :], wt_sb[:, o, t : t + 1], None, MUL)
+        def weigh_and_interleave(o, h):
+            walk = [P, P // RUN, PACK, RUN]
+            for cols in quarters:
+                nc.vector.tensor_tensor(
+                    g_bf[o][h][:, cols, :].rearrange("p (c i) t -> p c t i", i=RUN),
+                    work[o][h][:, :, cols].rearrange("p t (c i) -> p c t i", i=RUN),
+                    wt_sb[:, o, :].unsqueeze(1).unsqueeze(3).to_broadcast(walk),
+                    MUL,
+                )
 
         def weigh_means(o, h):
             for t in range(PACK):
@@ -188,8 +193,8 @@ def tile_attend_gpoi_w_kernel(tc, xT, w_words, w_scales, y, wt, xm, offs, out):
                     out=work[o][h][:, t, :], in_=mean[o][h][:, t, :], func=COPY, scale=wt_sb[:, o, t : t + 1]
                 )
 
-        def finish_rows(o, h):
-            for t in range(PACK):
+        def finish_rows(o, h, places=range(PACK)):
+            for t in places:
                 nc.vector.scalar_tensor_tensor(
                     g_rows[o][h][:, t, :], y_sb[o][h][:, t, :], wt_sb[:, o, t : t + 1], work[o][h][:, t, :], MUL, SUB
                 )
@@ -307,23 +312,23 @@ def tile_attend_gpoi_w_kernel(tc, xT, w_words, w_scales, y, wt, xm, offs, out):
                 )
 
         subtract(0, 0)
-        weigh_residual(0, 0)
+        weigh_and_interleave(0, 0)
         means(1, 0, 0, 0)
         means(1, 0, 1, 1)
         weigh_means(0, 1)
         subtract(1, 0)
-        weigh_residual(1, 0)
-        interleave_g(0, 0, on_scalar)
+        quantize_g(0, 0)
+        weigh_and_interleave(1, 0)
         means(1, 1, 0, 4)
         means(1, 1, 1, 5)
-        quantize_g(0, 0)
-        interleave_g(1, 0, on_vector)
+        finish_rows(0, 1, range(1))
         quantize_g(1, 0)
+        finish_rows(0, 1, range(1, PACK))
         for o in range(PASSES):
             round_xm(0, o, on_scalar)
             quantize_xm(0, o)
         weigh_means(1, 1)
-        finish_rows(0, 1)
+        round_xm(1, 1, on_scalar)
         interleave_g(0, 1, on_scalar)
         multiply(0, 0, 6)
         drain_on_scalar(0, 0, 6)
@@ -331,13 +336,12 @@ def tile_attend_gpoi_w_kernel(tc, xT, w_words, w_scales, y, wt, xm, offs, out):
 
         finish_rows(1, 1)
         round_xm(1, 0, on_vector)
-        round_xm(1, 1, on_vector)
         interleave_g(1, 1, on_vector)
-        quantize_xm(1, 0)
         quantize_xm(1, 1)
+        quantize_xm(1, 0)
         quantize_g(0, 1)
         quantize_g(1, 1)
-        multiply(1, 0, 2)
+        multiply(1, 0, 2, order=(1, 0))
         multiply(0, 1, 3)
         drain_on_scalar(0, 1, 3)
         scatter_on_scalar(0, 1)

@@ -89,7 +89,7 @@ def tile_attend_gpoi_w_kernel(tc, xT, w_words, w_scales, y, wt, xm, offs, out):
         dw_sb = [[tile(f"dw_sb{c}{h}", [P, HALF], F32)[:] for h in range(2)] for c in range(D_BLOCKS)]
 
         lo_cols, hi_cols = slice(0, HALF), slice(HALF, N)
-        last_g = high_pair[:, :UNIT]
+        last_g = work[1][1][:, 2:, :].rearrange("p t i -> p (t i)").bitcast(BF16)
         first_raw = [
             work[1][1][:, places, :].rearrange("p e (u i) -> p (e u) i", u=2) for places in (slice(2, 4), slice(0, 2))
         ]
@@ -101,7 +101,7 @@ def tile_attend_gpoi_w_kernel(tc, xT, w_words, w_scales, y, wt, xm, offs, out):
         first_rows = mean[1][0][:, :2, :].rearrange("p t i -> p (t i)").bitcast(BF16)
         xm_flat = [
             [first_rows[:, :K_PASS], first_rows[:, K_PASS:]],
-            [work[1][1][:, 2, :].bitcast(BF16), mean[1][1][:, 2, :].bitcast(BF16)],
+            [mean[0][1][:, 2, :].bitcast(BF16), mean[0][1][:, 3, :].bitcast(BF16)],
             [last_g[:, :K_PASS], last_g[:, K_PASS:]],
             [last_g[:, :K_PASS], last_g[:, K_PASS:]],
         ]
@@ -173,16 +173,19 @@ def tile_attend_gpoi_w_kernel(tc, xT, w_words, w_scales, y, wt, xm, offs, out):
                 score(o, h, 2 * pair + e, scores[:, e, :])
             nc.scalar.activation(out=mean[o][h][:, 2 * pair : 2 * pair + 2, :], in_=scores, func=EXP)
 
+        def residual(o, h, e):
+            return work[o][h][:, 2 * e : 2 * e + 2, :].rearrange("p e (u i) -> p (e u) i", u=2)
+
         def subtract(o, h):
-            for cols in quarters:
-                nc.vector.tensor_tensor(work[o][h][:, :, cols], y_sb[o][h][:, :, cols], mean[o][h][:, :, cols], SUB)
+            for e, cols in enumerate(quarters):
+                nc.vector.tensor_tensor(residual(o, h, e), y_sb[o][h][:, :, cols], mean[o][h][:, :, cols], SUB)
 
         def weigh_and_interleave(o, h):
             walk = [P, P // RUN, PACK, RUN]
-            for cols in quarters:
+            for e, cols in enumerate(quarters):
                 nc.vector.tensor_tensor(
                     g_bf[o][h][:, cols, :].rearrange("p (c i) t -> p c t i", i=RUN),
-                    work[o][h][:, :, cols].rearrange("p t (c i) -> p c t i", i=RUN),
+                    residual(o, h, e).rearrange("p t (c i) -> p c t i", i=RUN),
                     wt_sb[:, o, :].unsqueeze(1).unsqueeze(3).to_broadcast(walk),
                     MUL,
                 )
@@ -274,10 +277,11 @@ def tile_attend_gpoi_w_kernel(tc, xT, w_words, w_scales, y, wt, xm, offs, out):
         nc.sync.dma_start(out=wt_sb, in_=wt[0].rearrange("(o p t) one -> p o (t one)", o=PASSES, t=PACK))
         load_y(1, 0)
         load_y(0, 1)
-        load_xm(0, 0)
-        load_xm(0, 1)
+        for c in range(2):
+            for o in range(PASSES):
+                load_xm(c, o)
         load_y(1, 1)
-        for c in range(1, D_BLOCKS):
+        for c in range(2, D_BLOCKS):
             for o in range(PASSES):
                 load_xm(c, o)
 
@@ -327,21 +331,20 @@ def tile_attend_gpoi_w_kernel(tc, xT, w_words, w_scales, y, wt, xm, offs, out):
         for o in range(PASSES):
             round_xm(0, o, on_scalar)
             quantize_xm(0, o)
-        weigh_means(1, 1)
+        round_xm(1, 0, on_scalar)
         round_xm(1, 1, on_scalar)
         interleave_g(0, 1, on_scalar)
         multiply(0, 0, 6)
         drain_on_scalar(0, 0, 6)
         scatter_on_scalar(0, 0)
 
-        finish_rows(1, 1)
-        round_xm(1, 0, on_vector)
-        interleave_g(1, 1, on_vector)
-        quantize_xm(1, 1)
+        subtract(1, 1)
         quantize_xm(1, 0)
+        quantize_xm(1, 1)
+        weigh_and_interleave(1, 1)
         quantize_g(0, 1)
         quantize_g(1, 1)
-        multiply(1, 0, 2, order=(1, 0))
+        multiply(1, 0, 2)
         multiply(0, 1, 3)
         drain_on_scalar(0, 1, 3)
         scatter_on_scalar(0, 1)

@@ -25,6 +25,7 @@ K_PASS = P * PACK
 PASSES = R // K_PASS
 D_BLOCKS = D // P
 HALF = 256
+SIDE = HALF // 2
 UNIT = PACK * HALF
 RUN = 4
 
@@ -36,8 +37,8 @@ def tile_attend_gpoi_w_kernel(tc, xT, w_words, w_scales, y, wt, xm, offs, out):
         psum = ctx.enter_context(tc.psum_pool(name="psum", bufs=1))
         bank = [psum.tile([P, N], F32, name=f"bank{b}") for b in range(8)]
 
-        def tile(name, shape, dtype, **kw):
-            return keep.tile(shape, dtype, align_bytes=64, name=name, **kw)
+        def tile(name, shape, dtype):
+            return keep.tile(shape, dtype, align_bytes=64, name=name)
 
         def units(name, shape, dtype):
             return [[tile(f"{name}{o}{h}", shape, dtype) for h in range(2)] for o in range(PASSES)]
@@ -45,9 +46,18 @@ def tile_attend_gpoi_w_kernel(tc, xT, w_words, w_scales, y, wt, xm, offs, out):
         def passes(name, shape, dtype):
             return [tile(f"{name}{o}", shape, dtype) for o in range(PASSES)]
 
+        def flat(ap):
+            return ap.rearrange("p t i -> p (t i)")
+
+        def by_place(ap):
+            return ap.rearrange("p (t i) -> p t i", t=PACK)
+
         def by_word(ap):
             return ap.rearrange("p (i t) -> p i t", t=PACK)
 
+        lo, hi = slice(0, HALF), slice(HALF, N)
+        halves = (lo, hi)
+        sides = (slice(0, SIDE), slice(SIDE, HALF))
         placed = [P, PACK, HALF]
 
         offsets = keep.tile([P, N // 16], U16)
@@ -57,11 +67,6 @@ def tile_attend_gpoi_w_kernel(tc, xT, w_words, w_scales, y, wt, xm, offs, out):
         wt_sb = wt_rows[:, :, :PACK]
         xT_raw = units("xT_raw", placed, F32)
         y_sb = units("y_sb", placed, F32)
-        last_words = tile("last_words", [P, HALF + UNIT], F32)
-        late_raw = [
-            tile("late_raw0", [P, PASSES, PACK, P], F32),
-            last_words[:, HALF:].rearrange("p (o t i) -> p o t i", o=PASSES, t=PACK),
-        ]
         windows = [tile(f"window{c}", [P, T], F32) for c in range(D_BLOCKS)]
 
         w_codes = tile("w_codes", [P, N], U32)
@@ -71,49 +76,46 @@ def tile_attend_gpoi_w_kernel(tc, xT, w_words, w_scales, y, wt, xm, offs, out):
         xT_sc = passes("xT_sc", [P, K_PASS], U8)
         xm_codes = [tile(f"xm_codes{c}", [P, PASSES * P], U32) for c in range(D_BLOCKS)]
         xm_sc = [tile(f"xm_sc{c}", [P, PASSES * P], U8) for c in range(D_BLOCKS)]
-        high_words = tile("high_words", [P, UNIT], F32)
-        high_pair = high_words[:].bitcast(BF16)
-        g_rows = [
-            [tile("g_rows00", placed, BF16), high_pair[:, UNIT:].rearrange("p (t i) -> p t i", t=PACK)],
-            [tile("g_rows10", placed, BF16), tile("g_rows11", placed, BF16)],
-        ]
         g_codes = units("g_codes", [P, HALF], U32)
         g_sc = units("g_sc", [P, HALF], U8)
         mean = units("mean", placed, F32)
-        work = units("work", placed, F32)
-        g_flat = [
-            [tile("g_flat00", [P, UNIT], BF16), tile("g_flat01", [P, UNIT], BF16)],
-            [tile("g_flat10", [P, UNIT], BF16), high_pair[:, :UNIT]],
-        ]
-        g_bf = [[by_word(g_flat[o][h][:]) for h in range(2)] for o in range(PASSES)]
-        dw_sb = [[tile(f"dw_sb{c}{h}", [P, HALF], F32)[:] for h in range(2)] for c in range(D_BLOCKS)]
+        work = units("work", [P, UNIT], F32)
+        high_rows = passes("high_rows", placed, BF16)
 
-        lo_cols, hi_cols = slice(0, HALF), slice(HALF, N)
-        last_g = work[1][1][:, 2:, :].rearrange("p t i -> p (t i)").bitcast(BF16)
-        first_raw = [
-            work[1][1][:, places, :].rearrange("p e (u i) -> p (e u) i", u=2) for places in (slice(2, 4), slice(0, 2))
+        def side_work(o, h, e):
+            return by_place(work[o][h][:, e * K_PASS : (e + 1) * K_PASS])
+
+        last_g = tile("last_g", [P, UNIT // 2], F32)
+        g_flat = [
+            [tile("g_flat00", [P, UNIT], BF16)[:], tile("g_flat01", [P, UNIT], BF16)[:]],
+            [tile("g_flat10", [P, UNIT], BF16)[:], last_g[:].bitcast(BF16)],
         ]
-        second_raw = [
-            tile("second_raw0", [P, PACK, P], F32)[:],
-            high_words[:, :K_PASS].rearrange("p (t i) -> p t i", t=PACK),
+        raw2 = tile("raw2", [P, UNIT], F32)
+        dw2_and_raw3 = tile("dw2_and_raw3", [P, HALF + UNIT], F32)
+        raw3 = dw2_and_raw3[:, HALF:]
+        xm_raw = [
+            [side_work(1, 1, 1), side_work(1, 1, 0)],
+            [tile("raw10", [P, PACK, P], F32)[:], by_place(last_g[:])],
+            [by_place(raw2[:, :K_PASS]), by_place(raw2[:, K_PASS:])],
+            [by_place(raw3[:, :K_PASS]), by_place(raw3[:, K_PASS:])],
         ]
-        xm_raw = [first_raw, second_raw] + [[raw[:, o, :, :] for o in range(PASSES)] for raw in late_raw]
-        first_rows = mean[1][0][:, :2, :].rearrange("p t i -> p (t i)").bitcast(BF16)
-        xm_flat = [
-            [first_rows[:, :K_PASS], first_rows[:, K_PASS:]],
+        first_bf = flat(mean[1][0][:, :2, :]).bitcast(BF16)
+        late_bf = work[1][1][:, K_PASS:].bitcast(BF16)
+        xm_bf = [
+            [first_bf[:, :K_PASS], first_bf[:, K_PASS:]],
             [mean[0][1][:, 2, :].bitcast(BF16), mean[0][1][:, 3, :].bitcast(BF16)],
-            [last_g[:, :K_PASS], last_g[:, K_PASS:]],
-            [last_g[:, :K_PASS], last_g[:, K_PASS:]],
+            [late_bf[:, :K_PASS], late_bf[:, K_PASS:]],
         ]
-        dw_sb[2] = [last_words[:, lo_cols], last_words[:, hi_cols]]
-        dw_sb[1][0] = late_raw[0][:, 0, 2:, :].rearrange("p t i -> p (t i)")
+        dw_sb = [
+            [tile("dw00", [P, HALF], F32)[:], tile("dw01", [P, HALF], F32)[:]],
+            [raw2[:, HALF:K_PASS], tile("dw11", [P, HALF], F32)[:]],
+            [dw2_and_raw3[:, lo], dw2_and_raw3[:, hi]],
+            [tile("dw30", [P, HALF], F32)[:], tile("dw31", [P, HALF], F32)[:]],
+        ]
 
         xT_v = xT[0].rearrange("(p j) r -> p j r", j=PACK)
         y_v = y[0].rearrange("(o p t) i -> o p t i", o=PASSES, t=PACK)
         xm_v = xm[0].rearrange("(o p t) d -> o p t d", o=PASSES, t=PACK)
-        lo, hi = slice(0, HALF), slice(HALF, N)
-        halves = (lo, hi)
-        quarters = (slice(0, P), slice(P, HALF))
 
         def on_vector(dst, src):
             nc.vector.tensor_copy(out=dst, in_=src)
@@ -139,9 +141,9 @@ def tile_attend_gpoi_w_kernel(tc, xT, w_words, w_scales, y, wt, xm, offs, out):
         def load_y(o, h):
             nc.sync.dma_start(out=y_sb[o][h][:], in_=y_v[o, :, :, halves[h]])
 
-        def load_xm(c, o):
-            nc.sync.dma_start(out=xm_raw[c][o], in_=xm_v[o, :, :, c * P : (c + 1) * P])
-
+        def load_xm(c):
+            for o in range(PASSES):
+                nc.sync.dma_start(out=xm_raw[c][o], in_=xm_v[o, :, :, c * P : (c + 1) * P])
 
         def dealt(h):
             return slice(h * (P // 2), (h + 1) * (P // 2))
@@ -173,71 +175,55 @@ def tile_attend_gpoi_w_kernel(tc, xT, w_words, w_scales, y, wt, xm, offs, out):
                 score(o, h, 2 * pair + e, scores[:, e, :])
             nc.scalar.activation(out=mean[o][h][:, 2 * pair : 2 * pair + 2, :], in_=scores, func=EXP)
 
-        def residual(o, h, e):
-            return work[o][h][:, 2 * e : 2 * e + 2, :].rearrange("p e (u i) -> p (e u) i", u=2)
+        def walk_words(ap):
+            return ap.rearrange("p (c i) t -> p c t i", i=RUN)
 
-        def subtract(o, h):
-            for e, cols in enumerate(quarters):
-                nc.vector.tensor_tensor(residual(o, h, e), y_sb[o][h][:, :, cols], mean[o][h][:, :, cols], SUB)
+        def walk_places(ap):
+            return ap.rearrange("p t (c i) -> p c t i", i=RUN)
 
-        def weigh_and_interleave(o, h):
-            walk = [P, P // RUN, PACK, RUN]
-            for e, cols in enumerate(quarters):
-                nc.vector.tensor_tensor(
-                    g_bf[o][h][:, cols, :].rearrange("p (c i) t -> p c t i", i=RUN),
-                    residual(o, h, e).rearrange("p t (c i) -> p c t i", i=RUN),
-                    wt_sb[:, o, :].unsqueeze(1).unsqueeze(3).to_broadcast(walk),
-                    MUL,
-                )
+        def subtract(o, h, e):
+            nc.vector.tensor_tensor(side_work(o, h, e), y_sb[o][h][:, :, sides[e]], mean[o][h][:, :, sides[e]], SUB)
 
-        def weigh_means(o, h):
-            for t in range(PACK):
-                nc.scalar.activation(
-                    out=work[o][h][:, t, :], in_=mean[o][h][:, t, :], func=COPY, scale=wt_sb[:, o, t : t + 1]
-                )
-
-        def finish_rows(o, h, places=range(PACK)):
-            for t in places:
-                nc.vector.scalar_tensor_tensor(
-                    g_rows[o][h][:, t, :], y_sb[o][h][:, t, :], wt_sb[:, o, t : t + 1], work[o][h][:, t, :], MUL, SUB
-                )
-
-        def interleave(copy, dst, src):
-            copy(dst.rearrange("p (c i) t -> p c t i", i=RUN), src.rearrange("p t (c i) -> p c t i", i=RUN))
-
-        def interleave_g(o, h, copy, cols=lo):
-            interleave(copy, g_bf[o][h][:, cols, :], g_rows[o][h][:, :, cols])
-
-        def xm_block(c, o):
-            return xm_raw[c][o]
-
-        def round_xm(c, o, copy):
-            interleave(copy, by_word(xm_flat[c][o]), xm_block(c, o))
-
-        def round_last_xm_on_gpsimd():
-            nc.gpsimd.tensor_scalar(
-                last_g[:].rearrange("p (o i t) -> p o i t", o=PASSES, t=PACK),
-                late_raw[1][:].rearrange("p o t i -> p o i t"),
-                1.0,
-                0.0,
+        def weigh_and_interleave(o, h, e):
+            nc.vector.tensor_tensor(
+                walk_words(by_word(g_flat[o][h])[:, sides[e], :]),
+                walk_places(side_work(o, h, e)),
+                wt_sb[:, o, :].unsqueeze(1).unsqueeze(3).to_broadcast([P, SIDE // RUN, PACK, RUN]),
                 MUL,
-                ADD,
             )
 
+        def weigh_means(o, cols, weighed):
+            for t in range(PACK):
+                nc.scalar.activation(
+                    out=weighed[:, t, :], in_=mean[o][1][:, t, cols], func=COPY, scale=wt_sb[:, o, t : t + 1]
+                )
+
+        def finish_rows(o, cols, weighed, places):
+            for t in places:
+                nc.vector.scalar_tensor_tensor(
+                    high_rows[o][:, t, cols], y_sb[o][1][:, t, cols], wt_sb[:, o, t : t + 1], weighed[:, t, :], MUL, SUB
+                )
+
+        def interleave_rows(o, cols, copy):
+            copy(walk_words(by_word(g_flat[o][1])[:, cols, :]), walk_places(high_rows[o][:, :, cols]))
+
+        def round_xm(c, o, copy):
+            copy(walk_words(by_word(xm_bf[c][o])), walk_places(xm_raw[c][o]))
+
         def quantize_g(o, h):
-            quantize(g_codes[o][h][:].bitcast(E5M2), g_sc[o][h][:], g_flat[o][h][:])
+            quantize(g_codes[o][h][:].bitcast(E5M2), g_sc[o][h][:], g_flat[o][h])
 
         def quantize_xm(c, o):
             cols = slice(o * P, (o + 1) * P)
-            quantize(xm_codes[c][:, cols].bitcast(E4M3), xm_sc[c][:, cols], xm_flat[c][o])
+            quantize(xm_codes[c][:, cols].bitcast(E4M3), xm_sc[c][:, cols], xm_bf[c][o])
 
         def quantize_late_xm(c):
-            quantize(xm_codes[c][:].bitcast(E4M3), xm_sc[c][:], last_g[:])
+            quantize(xm_codes[c][:].bitcast(E4M3), xm_sc[c][:], late_bf)
 
-        def multiply(c, h, b, order=(0, 1), cols=lo):
+        def multiply(c, h, b, order=(0, 1)):
             for o in order:
                 nc.tensor.matmul_mx(
-                    out=bank[b][:, cols],
+                    out=bank[b][:, lo],
                     lhsT=xm_codes[c][:, o * P : (o + 1) * P].bitcast(E4M3),
                     lhsT_scale=xm_sc[c][:, o * P : (o + 1) * P],
                     rhs=g_codes[o][h][:].bitcast(E5M2),
@@ -249,14 +235,11 @@ def tile_attend_gpoi_w_kernel(tc, xT, w_words, w_scales, y, wt, xm, offs, out):
         def drain_on_scalar(c, h, b):
             nc.scalar.activation(out=dw_sb[c][h], in_=bank[b][:, lo], func=COPY, scale=-1.0)
 
-        def drain_on_vector(c, h, b, cols=lo):
-            nc.vector.tensor_scalar(dw_sb[c][h][:, cols], bank[b][:, cols], -1.0, None, MUL)
+        def drain_on_vector(c, h, b):
+            nc.vector.tensor_scalar(dw_sb[c][h], bank[b][:, lo], -1.0, None, MUL)
 
         def scatter_on_scalar(c, h):
             nc.scalar.activation(out=windows[c][:].indirect(entries(halves[h])), in_=dw_sb[c][h], func=COPY)
-
-        def scatter_on_vector(c, h):
-            nc.vector.tensor_copy(windows[c][:].indirect(entries(halves[h])), dw_sb[c][h])
 
         def store(c):
             nc.sync.dma_start(out=out[c * P : (c + 1) * P, :], in_=windows[c][:])
@@ -277,13 +260,11 @@ def tile_attend_gpoi_w_kernel(tc, xT, w_words, w_scales, y, wt, xm, offs, out):
         nc.sync.dma_start(out=wt_sb, in_=wt[0].rearrange("(o p t) one -> p o (t one)", o=PASSES, t=PACK))
         load_y(1, 0)
         load_y(0, 1)
-        for c in range(2):
-            for o in range(PASSES):
-                load_xm(c, o)
+        load_xm(0)
+        load_xm(1)
         load_y(1, 1)
-        for c in range(2, D_BLOCKS):
-            for o in range(PASSES):
-                load_xm(c, o)
+        load_xm(2)
+        load_xm(3)
 
         for window in windows[:2]:
             zero_on_vector(window[:].bitcast(I32))
@@ -315,33 +296,42 @@ def tile_attend_gpoi_w_kernel(tc, xT, w_words, w_scales, y, wt, xm, offs, out):
                     xT_bf[1][:, t, dealt(h), :].rearrange("p m j -> p (m j)"),
                 )
 
-        subtract(0, 0)
-        weigh_and_interleave(0, 0)
+        high_means = by_place(work[0][1][:])
+        for e in range(2):
+            subtract(0, 0, e)
+        for e in range(2):
+            weigh_and_interleave(0, 0, e)
         means(1, 0, 0, 0)
         means(1, 0, 1, 1)
-        weigh_means(0, 1)
-        subtract(1, 0)
+        weigh_means(0, lo, high_means)
+        for e in range(2):
+            subtract(1, 0, e)
         quantize_g(0, 0)
-        weigh_and_interleave(1, 0)
+        for e in range(2):
+            weigh_and_interleave(1, 0, e)
         means(1, 1, 0, 4)
         means(1, 1, 1, 5)
-        finish_rows(0, 1, range(1))
+
+        finish_rows(0, lo, high_means, range(1))
         quantize_g(1, 0)
-        finish_rows(0, 1, range(1, PACK))
         for o in range(PASSES):
             round_xm(0, o, on_scalar)
             quantize_xm(0, o)
-        round_xm(1, 0, on_scalar)
-        round_xm(1, 1, on_scalar)
-        interleave_g(0, 1, on_scalar)
+        finish_rows(0, lo, high_means, range(1, PACK))
+        for o in range(PASSES):
+            round_xm(1, o, on_scalar)
+        weigh_means(1, sides[0], side_work(1, 1, 0))
         multiply(0, 0, 6)
         drain_on_scalar(0, 0, 6)
+        interleave_rows(0, lo, on_scalar)
         scatter_on_scalar(0, 0)
 
-        subtract(1, 1)
-        quantize_xm(1, 0)
-        quantize_xm(1, 1)
-        weigh_and_interleave(1, 1)
+        finish_rows(1, sides[0], side_work(1, 1, 0), range(PACK))
+        subtract(1, 1, 1)
+        interleave_rows(1, sides[0], on_vector)
+        for o in range(PASSES):
+            quantize_xm(1, o)
+        weigh_and_interleave(1, 1, 1)
         quantize_g(0, 1)
         quantize_g(1, 1)
         multiply(1, 0, 2)
@@ -351,13 +341,20 @@ def tile_attend_gpoi_w_kernel(tc, xT, w_words, w_scales, y, wt, xm, offs, out):
         store(0)
 
         multiply(1, 1, 7, order=(1, 0))
-        round_xm(2, 0, on_vector)
-        round_xm(2, 1, on_vector)
+        for o in range(PASSES):
+            round_xm(2, o, on_vector)
         drain_on_vector(1, 0, 2)
         quantize_late_xm(2)
         drain_on_vector(1, 1, 7)
-        round_last_xm_on_gpsimd()
-        scatter_on_vector(1, 0)
+        nc.gpsimd.tensor_scalar(
+            late_bf.rearrange("p (o i t) -> p o i t", o=PASSES, t=PACK),
+            raw3.rearrange("p (o t i) -> p o i t", o=PASSES, t=PACK),
+            1.0,
+            0.0,
+            MUL,
+            ADD,
+        )
+        nc.vector.tensor_copy(windows[1][:].indirect(entries(lo)), dw_sb[1][0])
         multiply(2, 0, 0)
         multiply(2, 1, 1)
         drain_on_scalar(2, 0, 0)
@@ -365,7 +362,7 @@ def tile_attend_gpoi_w_kernel(tc, xT, w_words, w_scales, y, wt, xm, offs, out):
         store(1)
         drain_on_vector(2, 1, 1)
         quantize_late_xm(3)
-        nc.vector.tensor_copy(windows[2][:].indirect(offsets[:]), last_words[:, :N])
+        nc.vector.tensor_copy(windows[2][:].indirect(offsets[:]), dw2_and_raw3[:, :N])
         store(2)
         for h, b in ((0, 4), (1, 5)):
             multiply(3, h, b)

@@ -1,6 +1,7 @@
 from contextlib import ExitStack
 
 import concourse.mybir as mybir
+from concourse.masks import make_identity
 
 D, R, N, T = 512, 1024, 512, 2048
 FLOPS = 2 * 2 * D * R * N
@@ -27,6 +28,7 @@ D_BLOCKS = D // P
 HALF = 256
 SIDE = HALF // 2
 UNIT = PACK * HALF
+SHARE = 96
 RUN = 4
 
 
@@ -63,8 +65,15 @@ def tile_attend_gpoi_w_kernel(tc, xT, w_words, w_scales, y, wt, xm, offs, out):
         offsets = keep.tile([P, N // 16], U16)
         table_words = tile("table_words", [P, T], I32)
         table_scales = tile("table_scales", [P, T // 4], I32)
-        wt_rows = keep.tile([P, PASSES, 2 * PACK], F32)
-        wt_sb = wt_rows[:, :, :PACK]
+        identity = tile("identity", [P, P], F32)
+        wt_square = tile("wt_square", [P, P], F32)
+        wt_turned = tile("wt_turned", [P, P], F32)
+
+        def weights(square):
+            return square[:, : PASSES * 2 * PACK].rearrange("p (o t) -> p o t", o=PASSES)[:, :, :PACK]
+
+        wt_sb = weights(wt_square)
+        wt_psum = weights(bank[6])
         xT_raw = units("xT_raw", placed, F32)
         y_sb = units("y_sb", placed, F32)
         windows = [tile(f"window{c}", [P, T], F32) for c in range(D_BLOCKS)]
@@ -80,27 +89,28 @@ def tile_attend_gpoi_w_kernel(tc, xT, w_words, w_scales, y, wt, xm, offs, out):
         g_sc = units("g_sc", [P, HALF], U8)
         mean = units("mean", placed, F32)
         work = units("work", [P, UNIT], F32)
-        high_rows = passes("high_rows", placed, BF16)
+        last_rows = tile("last_rows", [P, PACK, SIDE], BF16)
 
         def side_work(o, h, e):
             return by_place(work[o][h][:, e * K_PASS : (e + 1) * K_PASS])
 
-        last_g = tile("last_g", [P, UNIT // 2], F32)
-        g_flat = [
-            [tile("g_flat00", [P, UNIT], BF16)[:], tile("g_flat01", [P, UNIT], BF16)[:]],
-            [tile("g_flat10", [P, UNIT], BF16)[:], last_g[:].bitcast(BF16)],
+        g_words = [[tile(f"g_words{o}{h}", [P, K_PASS], F32)[:] for h in range(2)] for o in range(PASSES)]
+        g_flat = [[g_words[o][h].bitcast(BF16) for h in range(2)] for o in range(PASSES)]
+        residual = [
+            [[side_work(0, 0, 0), side_work(0, 0, 1)], [y_sb[0][0][:, :, sides[0]], by_place(g_words[0][0])]],
+            [[side_work(1, 0, 0), side_work(1, 0, 1)], [None, by_place(g_words[1][0])]],
         ]
         raw2 = tile("raw2", [P, UNIT], F32)
         dw2_and_raw3 = tile("dw2_and_raw3", [P, HALF + UNIT], F32)
         raw3 = dw2_and_raw3[:, HALF:]
         xm_raw = [
-            [side_work(1, 1, 1), side_work(1, 1, 0)],
-            [tile("raw10", [P, PACK, P], F32)[:], by_place(last_g[:])],
+            [tile("raw00", [P, PACK, P], F32)[:], by_place(g_words[0][1])],
+            [tile("raw10", [P, PACK, P], F32)[:], tile("raw11", [P, PACK, P], F32)[:]],
             [by_place(raw2[:, :K_PASS]), by_place(raw2[:, K_PASS:])],
             [by_place(raw3[:, :K_PASS]), by_place(raw3[:, K_PASS:])],
         ]
         first_bf = flat(mean[1][0][:, :2, :]).bitcast(BF16)
-        late_bf = work[1][1][:, K_PASS:].bitcast(BF16)
+        late_bf = g_flat[1][0]
         xm_bf = [
             [first_bf[:, :K_PASS], first_bf[:, K_PASS:]],
             [mean[0][1][:, 2, :].bitcast(BF16), mean[0][1][:, 3, :].bitcast(BF16)],
@@ -181,31 +191,35 @@ def tile_attend_gpoi_w_kernel(tc, xT, w_words, w_scales, y, wt, xm, offs, out):
         def walk_places(ap):
             return ap.rearrange("p t (c i) -> p c t i", i=RUN)
 
-        def subtract(o, h, e):
-            nc.vector.tensor_tensor(side_work(o, h, e), y_sb[o][h][:, :, sides[e]], mean[o][h][:, :, sides[e]], SUB)
+        def subtract(o, h, e, engine, cols=slice(0, SIDE)):
+            engine.tensor_tensor(
+                residual[o][h][e][:, :, cols],
+                y_sb[o][h][:, :, sides[e]][:, :, cols],
+                mean[o][h][:, :, sides[e]][:, :, cols],
+                SUB,
+            )
 
         def weigh_and_interleave(o, h, e):
             nc.vector.tensor_tensor(
                 walk_words(by_word(g_flat[o][h])[:, sides[e], :]),
-                walk_places(side_work(o, h, e)),
-                wt_sb[:, o, :].unsqueeze(1).unsqueeze(3).to_broadcast([P, SIDE // RUN, PACK, RUN]),
+                walk_places(residual[o][h][e]),
+                wt_psum[:, o, :].unsqueeze(1).unsqueeze(3).to_broadcast([P, SIDE // RUN, PACK, RUN]),
                 MUL,
             )
 
-        def weigh_means(o, cols, weighed):
+        weighed = [side_work(1, 1, 0)[:, t, :] for t in range(PACK)]
+
+        def weigh_last_means():
             for t in range(PACK):
                 nc.scalar.activation(
-                    out=weighed[:, t, :], in_=mean[o][1][:, t, cols], func=COPY, scale=wt_sb[:, o, t : t + 1]
+                    out=weighed[t], in_=mean[1][1][:, t, sides[0]], func=COPY, scale=wt_sb[:, 1, t : t + 1]
                 )
 
-        def finish_rows(o, cols, weighed, places):
-            for t in places:
+        def finish_last_rows():
+            for t in range(PACK):
                 nc.vector.scalar_tensor_tensor(
-                    high_rows[o][:, t, cols], y_sb[o][1][:, t, cols], wt_sb[:, o, t : t + 1], weighed[:, t, :], MUL, SUB
+                    last_rows[:, t, :], y_sb[1][1][:, t, sides[0]], wt_sb[:, 1, t : t + 1], weighed[t], MUL, SUB
                 )
-
-        def interleave_rows(o, cols, copy):
-            copy(walk_words(by_word(g_flat[o][1])[:, cols, :]), walk_places(high_rows[o][:, :, cols]))
 
         def round_xm(c, o, copy):
             copy(walk_words(by_word(xm_bf[c][o])), walk_places(xm_raw[c][o]))
@@ -254,15 +268,16 @@ def tile_attend_gpoi_w_kernel(tc, xT, w_words, w_scales, y, wt, xm, offs, out):
             nc.sync.dma_start(out=table_scales[32 * q : 32 * q + 4, :], in_=scale_rows[4 * q : 4 * q + 4, :])
         load_xT(0, 1)
         nc.sync.dma_start(out=table_words[:], in_=w_words[0].rearrange("p n t -> p (n t)").bitcast(I32))
+        nc.vector.memset(wt_square[:], 0.0)
+        nc.sync.dma_start(out=wt_sb, in_=wt[0].rearrange("(o p t) one -> p o (t one)", o=PASSES, t=PACK))
         load_xT(1, 0)
         load_xT(1, 1)
         load_y(0, 0)
-        nc.sync.dma_start(out=wt_sb, in_=wt[0].rearrange("(o p t) one -> p o (t one)", o=PASSES, t=PACK))
-        load_y(1, 0)
         load_y(0, 1)
+        load_y(1, 0)
+        load_y(1, 1)
         load_xm(0)
         load_xm(1)
-        load_y(1, 1)
         load_xm(2)
         load_xm(3)
 
@@ -270,6 +285,7 @@ def tile_attend_gpoi_w_kernel(tc, xT, w_words, w_scales, y, wt, xm, offs, out):
             zero_on_vector(window[:].bitcast(I32))
         for window in windows[2:]:
             nc.gpsimd.memset(window[:].bitcast(I32), 0)
+        make_identity(nc, identity[:])
 
         nc.vector.tensor_copy(w_sc[:], table_scales[:].bitcast(U8).indirect(offsets[:]))
         round_xT(0, 0, on_scalar_activation)
@@ -285,6 +301,10 @@ def tile_attend_gpoi_w_kernel(tc, xT, w_words, w_scales, y, wt, xm, offs, out):
         means(0, 1, 0, 2)
         means(0, 1, 1, 7)
 
+        nc.tensor.transpose(bank[4][:, :P], wt_square[:], identity[:])
+        on_scalar(wt_turned[:], bank[4][:, :P])
+        nc.tensor.transpose(bank[6][:, :P], wt_turned[:], identity[:])
+
         round_xT(1, 0, on_vector)
         round_xT(1, 1, on_vector)
         for h in range(2):
@@ -296,39 +316,38 @@ def tile_attend_gpoi_w_kernel(tc, xT, w_words, w_scales, y, wt, xm, offs, out):
                     xT_bf[1][:, t, dealt(h), :].rearrange("p m j -> p (m j)"),
                 )
 
-        high_means = by_place(work[0][1][:])
         for e in range(2):
-            subtract(0, 0, e)
+            subtract(0, 0, e, nc.vector)
+        subtract(0, 1, 0, nc.gpsimd)
         for e in range(2):
             weigh_and_interleave(0, 0, e)
         means(1, 0, 0, 0)
         means(1, 0, 1, 1)
-        weigh_means(0, lo, high_means)
-        for e in range(2):
-            subtract(1, 0, e)
-        quantize_g(0, 0)
-        for e in range(2):
-            weigh_and_interleave(1, 0, e)
         means(1, 1, 0, 4)
         means(1, 1, 1, 5)
-
-        finish_rows(0, lo, high_means, range(1))
+        subtract(1, 0, 0, nc.vector)
+        quantize_g(0, 0)
+        subtract(1, 0, 1, nc.vector)
+        subtract(0, 1, 1, nc.gpsimd)
+        for e in range(2):
+            weigh_and_interleave(1, 0, e)
+        weigh_last_means()
+        finish_last_rows()
         quantize_g(1, 0)
         for o in range(PASSES):
             round_xm(0, o, on_scalar)
-            quantize_xm(0, o)
-        finish_rows(0, lo, high_means, range(1, PACK))
+        quantize(xm_codes[0][:].bitcast(E4M3), xm_sc[0][:], first_bf)
+        on_scalar(walk_words(by_word(g_flat[1][1])[:, sides[0], :]), walk_places(last_rows[:]))
         for o in range(PASSES):
             round_xm(1, o, on_scalar)
-        weigh_means(1, sides[0], side_work(1, 1, 0))
-        multiply(0, 0, 6)
-        drain_on_scalar(0, 0, 6)
-        interleave_rows(0, lo, on_scalar)
+        multiply(0, 0, 7)
+        drain_on_scalar(0, 0, 7)
         scatter_on_scalar(0, 0)
 
-        finish_rows(1, sides[0], side_work(1, 1, 0), range(PACK))
-        subtract(1, 1, 1)
-        interleave_rows(1, sides[0], on_vector)
+        subtract(1, 1, 1, nc.gpsimd, slice(0, SHARE))
+        for e in range(2):
+            weigh_and_interleave(0, 1, e)
+        subtract(1, 1, 1, nc.vector, slice(SHARE, SIDE))
         for o in range(PASSES):
             quantize_xm(1, o)
         weigh_and_interleave(1, 1, 1)

@@ -95,10 +95,13 @@ def tile_attend_gpoi_w_kernel(tc, xT, w_words, w_scales, y, wt, xm, offs, out):
             return by_place(work[o][h][:, e * K_PASS : (e + 1) * K_PASS])
 
         g_words = [[tile(f"g_words{o}{h}", [P, K_PASS], F32)[:] for h in range(2)] for o in range(PASSES)]
+        low_g_and_last = tile("low_g_and_last", [P, UNIT], F32)
+        g_words[1][0] = low_g_and_last[:, :K_PASS]
+        last_residual = low_g_and_last[:, K_PASS - SHARE : UNIT - SHARE]
         g_flat = [[g_words[o][h].bitcast(BF16) for h in range(2)] for o in range(PASSES)]
         residual = [
             [[side_work(0, 0, 0), side_work(0, 0, 1)], [y_sb[0][0][:, :, sides[0]], by_place(g_words[0][0])]],
-            [[side_work(1, 0, 0), side_work(1, 0, 1)], [None, by_place(g_words[1][0])]],
+            [[side_work(1, 0, 0), side_work(1, 0, 1)], [None, by_place(last_residual)]],
         ]
         raw2 = tile("raw2", [P, UNIT], F32)
         dw2_and_raw3 = tile("dw2_and_raw3", [P, HALF + UNIT], F32)
@@ -110,7 +113,7 @@ def tile_attend_gpoi_w_kernel(tc, xT, w_words, w_scales, y, wt, xm, offs, out):
             [by_place(raw3[:, :K_PASS]), by_place(raw3[:, K_PASS:])],
         ]
         first_bf = flat(mean[1][0][:, :2, :]).bitcast(BF16)
-        late_bf = g_flat[1][0]
+        late_bf = last_residual.bitcast(BF16)
         xm_bf = [
             [first_bf[:, :K_PASS], first_bf[:, K_PASS:]],
             [mean[0][1][:, 2, :].bitcast(BF16), mean[0][1][:, 3, :].bitcast(BF16)],
@@ -194,8 +197,8 @@ def tile_attend_gpoi_w_kernel(tc, xT, w_words, w_scales, y, wt, xm, offs, out):
         def subtract(o, h, e, engine, cols=slice(0, SIDE)):
             engine.tensor_tensor(
                 residual[o][h][e][:, :, cols],
-                y_sb[o][h][:, :, sides[e]][:, :, cols],
                 mean[o][h][:, :, sides[e]][:, :, cols],
+                y_sb[o][h][:, :, sides[e]][:, :, cols],
                 SUB,
             )
 
@@ -209,16 +212,46 @@ def tile_attend_gpoi_w_kernel(tc, xT, w_words, w_scales, y, wt, xm, offs, out):
 
         weighed = [side_work(1, 1, 0)[:, t, :] for t in range(PACK)]
 
-        def weigh_last_means():
+        turned_means = side_work(1, 1, 1)
+
+        def last_means():
+            slots = slice(HALF, HALF + SIDE)
+            nc.tensor.matmul_mx(
+                out=bank[5][:],
+                lhsT=w_codes[:, slots].bitcast(E4M3),
+                lhsT_scale=w_sc[:, slots],
+                rhs=xT_codes[1][:].bitcast(E4M3),
+                rhs_scale=xT_sc[1][:],
+                start=True,
+                stop=True,
+            )
+            nc.scalar.activation(out=turned_means, in_=by_place(bank[5][:]), func=EXP)
+            slots = slice(HALF + SIDE, N)
+            for t in range(PACK):
+                rows = slice(t * P, (t + 1) * P)
+                nc.tensor.matmul_mx(
+                    out=bank[2][:, rows],
+                    lhsT=xT_codes[1][:, rows].bitcast(E4M3),
+                    lhsT_scale=xT_sc[1][:, rows],
+                    rhs=w_codes[:, slots].bitcast(E4M3),
+                    rhs_scale=w_sc[:, slots],
+                    start=True,
+                    stop=True,
+                )
+            nc.scalar.activation(out=mean[1][1][:, :, sides[1]], in_=by_place(bank[2][:]), func=EXP)
+            for t in range(PACK):
+                nc.tensor.transpose(bank[4][:, t * P : (t + 1) * P], turned_means[:, t, :], identity[:])
+
+        def weigh_last_y():
             for t in range(PACK):
                 nc.scalar.activation(
-                    out=weighed[t], in_=mean[1][1][:, t, sides[0]], func=COPY, scale=wt_sb[:, 1, t : t + 1]
+                    out=weighed[t], in_=y_sb[1][1][:, t, sides[0]], func=COPY, scale=wt_sb[:, 1, t : t + 1]
                 )
 
         def finish_last_rows():
             for t in range(PACK):
                 nc.vector.scalar_tensor_tensor(
-                    last_rows[:, t, :], y_sb[1][1][:, t, sides[0]], wt_sb[:, 1, t : t + 1], weighed[t], MUL, SUB
+                    last_rows[:, t, :], bank[4][:, t * P : (t + 1) * P], wt_sb[:, 1, t : t + 1], weighed[t], MUL, SUB
                 )
 
         def round_xm(c, o, copy):
@@ -234,23 +267,30 @@ def tile_attend_gpoi_w_kernel(tc, xT, w_words, w_scales, y, wt, xm, offs, out):
         def quantize_late_xm(c):
             quantize(xm_codes[c][:].bitcast(E4M3), xm_sc[c][:], late_bf)
 
-        def multiply(c, h, b, order=(0, 1)):
+        def quantize_last_side(e):
+            quantize(
+                g_codes[1][1][:, sides[e]].bitcast(E5M2),
+                g_sc[1][1][:, sides[e]],
+                g_flat[1][1][:, e * K_PASS : (e + 1) * K_PASS],
+            )
+
+        def multiply(c, h, b, order=(0, 1), cols=lo):
             for o in order:
                 nc.tensor.matmul_mx(
-                    out=bank[b][:, lo],
+                    out=bank[b][:, cols],
                     lhsT=xm_codes[c][:, o * P : (o + 1) * P].bitcast(E4M3),
                     lhsT_scale=xm_sc[c][:, o * P : (o + 1) * P],
-                    rhs=g_codes[o][h][:].bitcast(E5M2),
-                    rhs_scale=g_sc[o][h][:],
+                    rhs=g_codes[o][h][:, cols].bitcast(E5M2),
+                    rhs_scale=g_sc[o][h][:, cols],
                     start=o == order[0],
                     stop=o == order[1],
                 )
 
-        def drain_on_scalar(c, h, b):
-            nc.scalar.activation(out=dw_sb[c][h], in_=bank[b][:, lo], func=COPY, scale=-1.0)
+        def drain_on_scalar(c, h, b, cols=lo):
+            on_scalar(dw_sb[c][h][:, cols], bank[b][:, cols])
 
         def drain_on_vector(c, h, b):
-            nc.vector.tensor_scalar(dw_sb[c][h], bank[b][:, lo], -1.0, None, MUL)
+            on_vector(dw_sb[c][h], bank[b][:, lo])
 
         def scatter_on_scalar(c, h):
             nc.scalar.activation(out=windows[c][:].indirect(entries(halves[h])), in_=dw_sb[c][h], func=COPY)
@@ -323,20 +363,19 @@ def tile_attend_gpoi_w_kernel(tc, xT, w_words, w_scales, y, wt, xm, offs, out):
             weigh_and_interleave(0, 0, e)
         means(1, 0, 0, 0)
         means(1, 0, 1, 1)
-        means(1, 1, 0, 4)
-        means(1, 1, 1, 5)
+        last_means()
         subtract(1, 0, 0, nc.vector)
         quantize_g(0, 0)
         subtract(1, 0, 1, nc.vector)
         subtract(0, 1, 1, nc.gpsimd)
         for e in range(2):
             weigh_and_interleave(1, 0, e)
-        weigh_last_means()
-        finish_last_rows()
+        weigh_last_y()
         quantize_g(1, 0)
         for o in range(PASSES):
             round_xm(0, o, on_scalar)
         quantize(xm_codes[0][:].bitcast(E4M3), xm_sc[0][:], first_bf)
+        finish_last_rows()
         on_scalar(walk_words(by_word(g_flat[1][1])[:, sides[0], :]), walk_places(last_rows[:]))
         for o in range(PASSES):
             round_xm(1, o, on_scalar)
@@ -344,18 +383,19 @@ def tile_attend_gpoi_w_kernel(tc, xT, w_words, w_scales, y, wt, xm, offs, out):
         drain_on_scalar(0, 0, 7)
         scatter_on_scalar(0, 0)
 
-        subtract(1, 1, 1, nc.gpsimd, slice(0, SHARE))
+        subtract(1, 1, 1, nc.gpsimd)
         for e in range(2):
             weigh_and_interleave(0, 1, e)
-        subtract(1, 1, 1, nc.vector, slice(SHARE, SIDE))
         for o in range(PASSES):
             quantize_xm(1, o)
+        quantize_last_side(0)
         weigh_and_interleave(1, 1, 1)
         quantize_g(0, 1)
-        quantize_g(1, 1)
+        quantize_last_side(1)
         multiply(1, 0, 2)
-        multiply(0, 1, 3)
-        drain_on_scalar(0, 1, 3)
+        for e, b in ((0, 0), (1, 3)):
+            multiply(0, 1, b, order=(1, 0) if e == 0 else (0, 1), cols=sides[e])
+            drain_on_scalar(0, 1, b, sides[e])
         scatter_on_scalar(0, 1)
         store(0)
 

@@ -29,6 +29,7 @@ HALF = 256
 SIDE = HALF // 2
 UNIT = PACK * HALF
 SHARE = 96
+EARLY = 108
 RUN = 4
 
 
@@ -89,7 +90,6 @@ def tile_attend_gpoi_w_kernel(tc, xT, w_words, w_scales, y, wt, xm, offs, out):
         g_sc = units("g_sc", [P, HALF], U8)
         mean = units("mean", placed, F32)
         work = units("work", [P, UNIT], F32)
-        last_rows = tile("last_rows", [P, PACK, SIDE], BF16)
 
         def side_work(o, h, e):
             return by_place(work[o][h][:, e * K_PASS : (e + 1) * K_PASS])
@@ -98,9 +98,12 @@ def tile_attend_gpoi_w_kernel(tc, xT, w_words, w_scales, y, wt, xm, offs, out):
         low_g_and_last = tile("low_g_and_last", [P, UNIT], F32)
         g_words[1][0] = low_g_and_last[:, :K_PASS]
         last_residual = low_g_and_last[:, K_PASS - SHARE : UNIT - SHARE]
+        first_g_and_high = tile("first_g_and_high", [P, PACK * (HALF - EARLY)], F32)
+        g_words[0][0] = first_g_and_high[:, :K_PASS]
         g_flat = [[g_words[o][h].bitcast(BF16) for h in range(2)] for o in range(PASSES)]
+        parts = [[sides, (slice(0, EARLY), slice(EARLY, HALF))], [sides, sides]]
         residual = [
-            [[side_work(0, 0, 0), side_work(0, 0, 1)], [y_sb[0][0][:, :, sides[0]], by_place(g_words[0][0])]],
+            [[side_work(0, 0, 0), side_work(0, 0, 1)], [y_sb[0][0][:, :, :EARLY], by_place(first_g_and_high[:])]],
             [[side_work(1, 0, 0), side_work(1, 0, 1)], [None, by_place(last_residual)]],
         ]
         raw2 = tile("raw2", [P, UNIT], F32)
@@ -113,6 +116,7 @@ def tile_attend_gpoi_w_kernel(tc, xT, w_words, w_scales, y, wt, xm, offs, out):
             [by_place(raw3[:, :K_PASS]), by_place(raw3[:, K_PASS:])],
         ]
         first_bf = flat(mean[1][0][:, :2, :]).bitcast(BF16)
+        last_rows = by_place(flat(mean[1][0][:])[:, K_PASS - SIDE : K_PASS + SIDE].bitcast(BF16))
         late_bf = last_residual.bitcast(BF16)
         xm_bf = [
             [first_bf[:, :K_PASS], first_bf[:, K_PASS:]],
@@ -194,19 +198,16 @@ def tile_attend_gpoi_w_kernel(tc, xT, w_words, w_scales, y, wt, xm, offs, out):
         def walk_places(ap):
             return ap.rearrange("p t (c i) -> p c t i", i=RUN)
 
-        def subtract(o, h, e, engine, cols=slice(0, SIDE)):
-            engine.tensor_tensor(
-                residual[o][h][e][:, :, cols],
-                mean[o][h][:, :, sides[e]][:, :, cols],
-                y_sb[o][h][:, :, sides[e]][:, :, cols],
-                SUB,
-            )
+        def subtract(o, h, e, engine):
+            cols = parts[o][h][e]
+            engine.tensor_tensor(residual[o][h][e], mean[o][h][:, :, cols], y_sb[o][h][:, :, cols], SUB)
 
         def weigh_and_interleave(o, h, e):
+            cols = parts[o][h][e]
             nc.vector.tensor_tensor(
-                walk_words(by_word(g_flat[o][h])[:, sides[e], :]),
+                walk_words(by_word(g_flat[o][h])[:, cols, :]),
                 walk_places(residual[o][h][e]),
-                wt_psum[:, o, :].unsqueeze(1).unsqueeze(3).to_broadcast([P, SIDE // RUN, PACK, RUN]),
+                wt_psum[:, o, :].unsqueeze(1).unsqueeze(3).to_broadcast([P, (cols.stop - cols.start) // RUN, PACK, RUN]),
                 MUL,
             )
 
@@ -243,16 +244,19 @@ def tile_attend_gpoi_w_kernel(tc, xT, w_words, w_scales, y, wt, xm, offs, out):
                 nc.tensor.transpose(bank[4][:, t * P : (t + 1) * P], turned_means[:, t, :], identity[:])
 
         def weigh_last_y():
-            for t in range(PACK):
+            for t in reversed(range(PACK)):
                 nc.scalar.activation(
                     out=weighed[t], in_=y_sb[1][1][:, t, sides[0]], func=COPY, scale=wt_sb[:, 1, t : t + 1]
                 )
 
         def finish_last_rows():
-            for t in range(PACK):
+            for t in reversed(range(PACK)):
                 nc.vector.scalar_tensor_tensor(
                     last_rows[:, t, :], bank[4][:, t * P : (t + 1) * P], wt_sb[:, 1, t : t + 1], weighed[t], MUL, SUB
                 )
+
+        def interleave_last_rows(cols):
+            on_scalar(walk_words(by_word(g_flat[1][1])[:, cols, :]), walk_places(last_rows[:, :, cols]))
 
         def round_xm(c, o, copy):
             copy(walk_words(by_word(xm_bf[c][o])), walk_places(xm_raw[c][o]))
@@ -376,18 +380,18 @@ def tile_attend_gpoi_w_kernel(tc, xT, w_words, w_scales, y, wt, xm, offs, out):
             round_xm(0, o, on_scalar)
         quantize(xm_codes[0][:].bitcast(E4M3), xm_sc[0][:], first_bf)
         finish_last_rows()
-        on_scalar(walk_words(by_word(g_flat[1][1])[:, sides[0], :]), walk_places(last_rows[:]))
         for o in range(PASSES):
             round_xm(1, o, on_scalar)
         multiply(0, 0, 7)
+        interleave_last_rows(slice(0, SIDE // 2))
         drain_on_scalar(0, 0, 7)
+        interleave_last_rows(slice(SIDE // 2, SIDE))
         scatter_on_scalar(0, 0)
 
         subtract(1, 1, 1, nc.gpsimd)
         for e in range(2):
             weigh_and_interleave(0, 1, e)
-        for o in range(PASSES):
-            quantize_xm(1, o)
+        quantize(xm_codes[1][:].bitcast(E4M3), xm_sc[1][:], flat(mean[0][1][:, 2:, :]).bitcast(BF16))
         quantize_last_side(0)
         weigh_and_interleave(1, 1, 1)
         quantize_g(0, 1)

@@ -28,8 +28,6 @@ D_BLOCKS = D // P
 HALF = 256
 SIDE = HALF // 2
 UNIT = PACK * HALF
-SHARE = 96
-EARLY = 108
 RUN = 4
 
 
@@ -41,16 +39,13 @@ def tile_attend_gpoi_w_kernel(tc, xT, w_words, w_scales, y, wt, xm, offs, out):
         bank = [psum.tile([P, N], F32, name=f"bank{b}") for b in range(8)]
 
         def tile(name, shape, dtype):
-            return keep.tile(shape, dtype, align_bytes=64, name=name)
+            return keep.tile(shape, dtype, align_bytes=256, name=name)
 
         def units(name, shape, dtype):
             return [[tile(f"{name}{o}{h}", shape, dtype) for h in range(2)] for o in range(PASSES)]
 
         def passes(name, shape, dtype):
             return [tile(f"{name}{o}", shape, dtype) for o in range(PASSES)]
-
-        def flat(ap):
-            return ap.rearrange("p t i -> p (t i)")
 
         def by_place(ap):
             return ap.rearrange("p (t i) -> p t i", t=PACK)
@@ -61,72 +56,76 @@ def tile_attend_gpoi_w_kernel(tc, xT, w_words, w_scales, y, wt, xm, offs, out):
         lo, hi = slice(0, HALF), slice(HALF, N)
         halves = (lo, hi)
         sides = (slice(0, SIDE), slice(SIDE, HALF))
+        pairs = (slice(0, 2), slice(2, 4))
         placed = [P, PACK, HALF]
 
         offsets = keep.tile([P, N // 16], U16)
         table_words = tile("table_words", [P, T], I32)
         table_scales = tile("table_scales", [P, T // 4], I32)
         identity = tile("identity", [P, P], F32)
-        wt_square = tile("wt_square", [P, P], F32)
-        wt_turned = tile("wt_turned", [P, P], F32)
-
-        def weights(square):
-            return square[:, : PASSES * 2 * PACK].rearrange("p (o t) -> p o t", o=PASSES)[:, :, :PACK]
-
-        wt_sb = weights(wt_square)
-        wt_psum = weights(bank[6])
+        wt_rows = tile("wt_rows", [P, K_PASS], F32)
+        wt_psum = bank[6][:].rearrange("p (t o) -> p o t", t=PACK)
         xT_raw = units("xT_raw", placed, F32)
-        y_sb = units("y_sb", placed, F32)
+        y_sb = units("y_sb", [P, 2, N], F32)
         windows = [tile(f"window{c}", [P, T], F32) for c in range(D_BLOCKS)]
 
         w_codes = tile("w_codes", [P, N], U32)
         w_sc = tile("w_sc", [P, N], U8)
-        xT_bf = passes("xT_bf", [P, PACK, P, PACK], BF16)
+        xT_words = passes("xT_words", [P, UNIT], F32)
+        xT_bf = [words[:].bitcast(BF16).rearrange("p (t m j) -> p t m j", t=PACK, j=PACK) for words in xT_words[:1]]
+        late_xT = xT_words[1][:].bitcast(BF16).rearrange("p (h t m j) -> p h t m j", h=2, t=PACK, j=PACK)
         xT_codes = passes("xT_codes", [P, K_PASS], U32)
         xT_sc = passes("xT_sc", [P, K_PASS], U8)
         xm_codes = [tile(f"xm_codes{c}", [P, PASSES * P], U32) for c in range(D_BLOCKS)]
         xm_sc = [tile(f"xm_sc{c}", [P, PASSES * P], U8) for c in range(D_BLOCKS)]
         g_codes = units("g_codes", [P, HALF], U32)
         g_sc = units("g_sc", [P, HALF], U8)
-        mean = units("mean", placed, F32)
-        work = units("work", [P, UNIT], F32)
 
-        def side_work(o, h, e):
-            return by_place(work[o][h][:, e * K_PASS : (e + 1) * K_PASS])
+        def mean_pair(name):
+            return tile(name, [P, 2, HALF], F32)[:]
 
-        g_words = [[tile(f"g_words{o}{h}", [P, K_PASS], F32)[:] for h in range(2)] for o in range(PASSES)]
-        low_g_and_last = tile("low_g_and_last", [P, UNIT], F32)
-        g_words[1][0] = low_g_and_last[:, :K_PASS]
-        last_residual = low_g_and_last[:, K_PASS - SHARE : UNIT - SHARE]
-        first_g_and_high = tile("first_g_and_high", [P, PACK * (HALF - EARLY)], F32)
-        g_words[0][0] = first_g_and_high[:, :K_PASS]
+        raw_step = 2 * UNIT - SIDE
+        strip = tile("strip", [P, 2 * raw_step], F32)
+        early_placed = strip[:].rearrange("p (o w) -> p o w", o=PASSES)[:, :, :UNIT].rearrange("p o (t i) -> p o t i", t=PACK)
+        last_residual = tile("last_residual", [P, UNIT], F32)
+        high_g = strip[:, raw_step + SIDE - K_PASS : raw_step + SIDE]
+        last_g = strip[:, raw_step + UNIT - SIDE : raw_step + UNIT - SIDE + K_PASS]
+        high_residual = tile("high_residual", [P, UNIT], F32)
+        mean = [
+            [
+                [mean_pair(f"mean00{q}") for q in range(2)],
+                [high_residual[:, K_PASS:].rearrange("p (t i) -> p t i", t=2), mean_pair("mean011")],
+            ],
+            [
+                [last_residual[:, :K_PASS].rearrange("p (t i) -> p t i", t=2), mean_pair("mean101")],
+                [mean_pair(f"mean11{q}") for q in range(2)],
+            ],
+        ]
+
+        def mean_of(o, h, places):
+            q = places.start // 2
+            return mean[o][h][q][:, places.start - 2 * q : places.stop - 2 * q, :]
+
+        g_words = [
+            [tile("g_words00", [P, K_PASS], F32)[:], high_g],
+            [tile("g_words10", [P, K_PASS], F32)[:], last_g],
+        ]
         g_flat = [[g_words[o][h].bitcast(BF16) for h in range(2)] for o in range(PASSES)]
-        parts = [[sides, (slice(0, EARLY), slice(EARLY, HALF))], [sides, sides]]
         residual = [
-            [[side_work(0, 0, 0), side_work(0, 0, 1)], [y_sb[0][0][:, :, :EARLY], by_place(first_g_and_high[:])]],
-            [[side_work(1, 0, 0), side_work(1, 0, 1)], [None, by_place(last_residual)]],
+            [tile("residual00", placed, F32)[:], by_place(high_residual[:])],
+            [tile("residual10", placed, F32)[:], by_place(last_residual[:])],
         ]
-        raw2 = tile("raw2", [P, UNIT], F32)
-        dw2_and_raw3 = tile("dw2_and_raw3", [P, HALF + UNIT], F32)
-        raw3 = dw2_and_raw3[:, HALF:]
-        xm_raw = [
-            [tile("raw00", [P, PACK, P], F32)[:], by_place(g_words[0][1])],
-            [tile("raw10", [P, PACK, P], F32)[:], tile("raw11", [P, PACK, P], F32)[:]],
-            [by_place(raw2[:, :K_PASS]), by_place(raw2[:, K_PASS:])],
-            [by_place(raw3[:, :K_PASS]), by_place(raw3[:, K_PASS:])],
-        ]
-        first_bf = flat(mean[1][0][:, :2, :]).bitcast(BF16)
-        last_rows = by_place(flat(mean[1][0][:])[:, K_PASS - SIDE : K_PASS + SIDE].bitcast(BF16))
-        late_bf = last_residual.bitcast(BF16)
-        xm_bf = [
-            [first_bf[:, :K_PASS], first_bf[:, K_PASS:]],
-            [mean[0][1][:, 2, :].bitcast(BF16), mean[0][1][:, 3, :].bitcast(BF16)],
-            [late_bf[:, :K_PASS], late_bf[:, K_PASS:]],
-        ]
+
+        late_raw = tile("late_raw", [P, PASSES, HALF + UNIT], F32)
+        late_placed = late_raw[:, :, HALF:].rearrange("p o (t i) -> p o t i", t=PACK)
+        raw = [[early_placed[:, o] for o in range(PASSES)], [late_placed[:, o] for o in range(PASSES)]]
+        late_bf = last_residual[:, K_PASS:].bitcast(BF16)
+        xm_bf = [late_bf, tile("xm_bf1", [P, UNIT], BF16)[:], late_bf]
+        dw2 = late_raw[:, 1, :N]
         dw_sb = [
             [tile("dw00", [P, HALF], F32)[:], tile("dw01", [P, HALF], F32)[:]],
-            [raw2[:, HALF:K_PASS], tile("dw11", [P, HALF], F32)[:]],
-            [dw2_and_raw3[:, lo], dw2_and_raw3[:, hi]],
+            [late_raw[:, 0, SIDE : SIDE + HALF], tile("dw11", [P, HALF], F32)[:]],
+            [dw2[:, lo], dw2[:, hi]],
             [tile("dw30", [P, HALF], F32)[:], tile("dw31", [P, HALF], F32)[:]],
         ]
 
@@ -155,42 +154,38 @@ def tile_attend_gpoi_w_kernel(tc, xT, w_words, w_scales, y, wt, xm, offs, out):
             r0 = o * K_PASS + h * HALF
             nc.sync.dma_start(out=xT_raw[o][h][:], in_=xT_v[:, :, r0 : r0 + HALF])
 
-        def load_y(o, h):
-            nc.sync.dma_start(out=y_sb[o][h][:], in_=y_v[o, :, :, halves[h]])
+        def load_y(o, places):
+            nc.sync.dma_start(out=y_sb[o][places.start // 2][:], in_=y_v[o, :, places, :])
 
-        def load_xm(c):
+        def load_xm(pair):
             for o in range(PASSES):
-                nc.sync.dma_start(out=xm_raw[c][o], in_=xm_v[o, :, :, c * P : (c + 1) * P])
+                nc.sync.dma_start(out=raw[pair][o], in_=xm_v[o, :, :, pair * HALF : (pair + 1) * HALF])
 
-        def dealt(h):
-            return slice(h * (P // 2), (h + 1) * (P // 2))
-
-        def round_xT(o, h, copy):
+        def round_xT(o, h, copy, places=slice(0, PACK)):
+            dealt = late_xT[:, h] if o else xT_bf[0][:, :, h * P // 2 : (h + 1) * P // 2, :]
             copy(
-                xT_bf[o][:, :, dealt(h), :].rearrange("p t m j -> p m j t"),
-                xT_raw[o][h][:].rearrange("p j (m t) -> p m j t", t=PACK),
+                dealt[:, places].rearrange("p t m j -> p m j t"),
+                xT_raw[o][h][:].rearrange("p j (m t) -> p m j t", t=PACK)[:, :, :, places],
             )
 
         def quantize(codes, scales, values):
             nc.vector.quantize_mx(out=codes, scales=scales, in_=values)
 
-        def score(o, h, t, scores):
-            rows = slice(t * P, (t + 1) * P)
-            nc.tensor.matmul_mx(
-                out=scores,
-                lhsT=xT_codes[o][:, rows].bitcast(E4M3),
-                lhsT_scale=xT_sc[o][:, rows],
-                rhs=w_codes[:, halves[h]].bitcast(E4M3),
-                rhs_scale=w_sc[:, halves[h]],
-                start=True,
-                stop=True,
-            )
-
-        def means(o, h, pair, b):
-            scores = bank[b][:].rearrange("p (e i) -> p e i", e=2)
-            for e in range(2):
-                score(o, h, 2 * pair + e, scores[:, e, :])
-            nc.scalar.activation(out=mean[o][h][:, 2 * pair : 2 * pair + 2, :], in_=scores, func=EXP)
+        def means(o, h, places, b):
+            count = places.stop - places.start
+            scores = bank[b][:, : count * HALF].rearrange("p (e i) -> p e i", e=count)
+            for e in range(count):
+                rows = slice((places.start + e) * P, (places.start + e + 1) * P)
+                nc.tensor.matmul_mx(
+                    out=scores[:, e, :],
+                    lhsT=xT_codes[o][:, rows].bitcast(E4M3),
+                    lhsT_scale=xT_sc[o][:, rows],
+                    rhs=w_codes[:, halves[h]].bitcast(E4M3),
+                    rhs_scale=w_sc[:, halves[h]],
+                    start=True,
+                    stop=True,
+                )
+            nc.scalar.activation(out=mean_of(o, h, places), in_=scores, func=EXP)
 
         def walk_words(ap):
             return ap.rearrange("p (c i) t -> p c t i", i=RUN)
@@ -198,97 +193,54 @@ def tile_attend_gpoi_w_kernel(tc, xT, w_words, w_scales, y, wt, xm, offs, out):
         def walk_places(ap):
             return ap.rearrange("p t (c i) -> p c t i", i=RUN)
 
-        def subtract(o, h, e, engine):
-            cols = parts[o][h][e]
-            engine.tensor_tensor(residual[o][h][e], mean[o][h][:, :, cols], y_sb[o][h][:, :, cols], SUB)
+        def subtract(o, h, places, engine):
+            engine.tensor_tensor(
+                residual[o][h][:, places, :],
+                mean_of(o, h, places),
+                y_sb[o][places.start // 2][:, places.start % 2 : (places.stop - 1) % 2 + 1, halves[h]],
+                SUB,
+            )
 
-        def weigh_and_interleave(o, h, e):
-            cols = parts[o][h][e]
+        def weigh(o, h, cols):
             nc.vector.tensor_tensor(
                 walk_words(by_word(g_flat[o][h])[:, cols, :]),
-                walk_places(residual[o][h][e]),
+                walk_places(residual[o][h][:, :, cols]),
                 wt_psum[:, o, :].unsqueeze(1).unsqueeze(3).to_broadcast([P, (cols.stop - cols.start) // RUN, PACK, RUN]),
                 MUL,
             )
 
-        weighed = [side_work(1, 1, 0)[:, t, :] for t in range(PACK)]
-
-        turned_means = side_work(1, 1, 1)
-
-        def last_means():
-            slots = slice(HALF, HALF + SIDE)
-            nc.tensor.matmul_mx(
-                out=bank[5][:],
-                lhsT=w_codes[:, slots].bitcast(E4M3),
-                lhsT_scale=w_sc[:, slots],
-                rhs=xT_codes[1][:].bitcast(E4M3),
-                rhs_scale=xT_sc[1][:],
-                start=True,
-                stop=True,
-            )
-            nc.scalar.activation(out=turned_means, in_=by_place(bank[5][:]), func=EXP)
-            slots = slice(HALF + SIDE, N)
-            for t in range(PACK):
-                rows = slice(t * P, (t + 1) * P)
-                nc.tensor.matmul_mx(
-                    out=bank[2][:, rows],
-                    lhsT=xT_codes[1][:, rows].bitcast(E4M3),
-                    lhsT_scale=xT_sc[1][:, rows],
-                    rhs=w_codes[:, slots].bitcast(E4M3),
-                    rhs_scale=w_sc[:, slots],
-                    start=True,
-                    stop=True,
-                )
-            nc.scalar.activation(out=mean[1][1][:, :, sides[1]], in_=by_place(bank[2][:]), func=EXP)
-            for t in range(PACK):
-                nc.tensor.transpose(bank[4][:, t * P : (t + 1) * P], turned_means[:, t, :], identity[:])
-
-        def weigh_last_y():
-            for t in reversed(range(PACK)):
-                nc.scalar.activation(
-                    out=weighed[t], in_=y_sb[1][1][:, t, sides[0]], func=COPY, scale=wt_sb[:, 1, t : t + 1]
-                )
-
-        def finish_last_rows():
-            for t in reversed(range(PACK)):
-                nc.vector.scalar_tensor_tensor(
-                    last_rows[:, t, :], bank[4][:, t * P : (t + 1) * P], wt_sb[:, 1, t : t + 1], weighed[t], MUL, SUB
-                )
-
-        def interleave_last_rows(cols):
-            on_scalar(walk_words(by_word(g_flat[1][1])[:, cols, :]), walk_places(last_rows[:, :, cols]))
-
         def round_xm(c, o, copy):
-            copy(walk_words(by_word(xm_bf[c][o])), walk_places(xm_raw[c][o]))
+            copy(
+                walk_words(by_word(xm_bf[c][:, o * K_PASS : (o + 1) * K_PASS])),
+                walk_places(raw[c // 2][o][:, :, sides[c % 2]]),
+            )
+
+        def quantize_xm(c, values):
+            quantize(xm_codes[c][:].bitcast(E4M3), xm_sc[c][:], values)
+
+        def quantize_side(o, h, e):
+            quantize(
+                g_codes[o][h][:, sides[e]].bitcast(E5M2),
+                g_sc[o][h][:, sides[e]],
+                g_flat[o][h][:, e * K_PASS : (e + 1) * K_PASS],
+            )
 
         def quantize_g(o, h):
-            quantize(g_codes[o][h][:].bitcast(E5M2), g_sc[o][h][:], g_flat[o][h])
+            for e in range(2):
+                quantize_side(o, h, e)
 
-        def quantize_xm(c, o):
-            cols = slice(o * P, (o + 1) * P)
-            quantize(xm_codes[c][:, cols].bitcast(E4M3), xm_sc[c][:, cols], xm_bf[c][o])
-
-        def quantize_late_xm(c):
-            quantize(xm_codes[c][:].bitcast(E4M3), xm_sc[c][:], late_bf)
-
-        def quantize_last_side(e):
-            quantize(
-                g_codes[1][1][:, sides[e]].bitcast(E5M2),
-                g_sc[1][1][:, sides[e]],
-                g_flat[1][1][:, e * K_PASS : (e + 1) * K_PASS],
-            )
-
-        def multiply(c, h, b, order=(0, 1), cols=lo):
+        def multiply(c, h, b, order=(0, 1), cols=lo, only=(0, 1)):
             for o in order:
-                nc.tensor.matmul_mx(
-                    out=bank[b][:, cols],
-                    lhsT=xm_codes[c][:, o * P : (o + 1) * P].bitcast(E4M3),
-                    lhsT_scale=xm_sc[c][:, o * P : (o + 1) * P],
-                    rhs=g_codes[o][h][:, cols].bitcast(E5M2),
-                    rhs_scale=g_sc[o][h][:, cols],
-                    start=o == order[0],
-                    stop=o == order[1],
-                )
+                if o in only:
+                    nc.tensor.matmul_mx(
+                        out=bank[b][:, cols],
+                        lhsT=xm_codes[c][:, o * P : (o + 1) * P].bitcast(E4M3),
+                        lhsT_scale=xm_sc[c][:, o * P : (o + 1) * P],
+                        rhs=g_codes[o][h][:, cols].bitcast(E5M2),
+                        rhs_scale=g_sc[o][h][:, cols],
+                        start=o == order[0],
+                        stop=o == order[1],
+                    )
 
         def drain_on_scalar(c, h, b, cols=lo):
             on_scalar(dw_sb[c][h][:, cols], bank[b][:, cols])
@@ -305,100 +257,92 @@ def tile_attend_gpoi_w_kernel(tc, xT, w_words, w_scales, y, wt, xm, offs, out):
         nc.gpsimd.memset(table_scales[:, : T // 8], 0)
         zero_on_vector(table_scales[:, T // 8 :])
 
-        load_xT(0, 0)
+        zero_on_vector(wt_rows[:])
         nc.sync.dma_start(offsets[:], offs)
+        load_xT(0, 0)
         scale_rows = w_scales[0].bitcast(I32)
         for q in range(4):
             nc.sync.dma_start(out=table_scales[32 * q : 32 * q + 4, :], in_=scale_rows[4 * q : 4 * q + 4, :])
+        nc.sync.dma_start(out=wt_rows[:PASSES, :], in_=wt[0].rearrange("(o k) one -> o (k one)", o=PASSES))
         load_xT(0, 1)
         nc.sync.dma_start(out=table_words[:], in_=w_words[0].rearrange("p n t -> p (n t)").bitcast(I32))
-        nc.vector.memset(wt_square[:], 0.0)
-        nc.sync.dma_start(out=wt_sb, in_=wt[0].rearrange("(o p t) one -> p o (t one)", o=PASSES, t=PACK))
         load_xT(1, 0)
         load_xT(1, 1)
-        load_y(0, 0)
-        load_y(0, 1)
-        load_y(1, 0)
-        load_y(1, 1)
+        for o in range(PASSES):
+            for places in pairs:
+                load_y(o, places)
         load_xm(0)
         load_xm(1)
-        load_xm(2)
-        load_xm(3)
 
-        for window in windows[:2]:
-            zero_on_vector(window[:].bitcast(I32))
+        make_identity(nc, identity[:])
+        zero_on_vector(windows[0][:].bitcast(I32))
+        zero_on_vector(windows[1][:, K_PASS:].bitcast(I32))
+        nc.gpsimd.memset(windows[1][:, :K_PASS].bitcast(I32), 0)
         for window in windows[2:]:
             nc.gpsimd.memset(window[:].bitcast(I32), 0)
-        make_identity(nc, identity[:])
 
         nc.vector.tensor_copy(w_sc[:], table_scales[:].bitcast(U8).indirect(offsets[:]))
         round_xT(0, 0, on_scalar_activation)
+        for t in range(PACK):
+            nc.tensor.transpose(bank[6][:, t * P : (t + 1) * P], wt_rows[:, t::PACK], identity[:])
         round_xT(0, 1, on_scalar)
-        quantize(xT_codes[0][:].bitcast(E4M3), xT_sc[0][:], xT_bf[0][:].rearrange("p t m j -> p (t m j)"))
+        quantize(xT_codes[0][:].bitcast(E4M3), xT_sc[0][:], xT_words[0][:].bitcast(BF16))
         for cols in halves:
             nc.vector.tensor_copy(w_codes[:, cols], table_words[:].bitcast(U32).indirect(entries(cols)))
 
-        for t, b in ((0, 3), (1, 0)):
-            score(0, 0, t, bank[b][:, lo])
-            nc.scalar.activation(out=mean[0][0][:, t, :], in_=bank[b][:, lo], func=EXP)
-        means(0, 0, 1, 1)
-        means(0, 1, 0, 2)
-        means(0, 1, 1, 7)
+        means(0, 0, slice(0, 1), 3)
+        means(0, 0, slice(1, 2), 0)
+        means(0, 1, pairs[0], 1)
+        means(0, 0, pairs[1], 2)
+        means(0, 1, pairs[1], 7)
 
-        nc.tensor.transpose(bank[4][:, :P], wt_square[:], identity[:])
-        on_scalar(wt_turned[:], bank[4][:, :P])
-        nc.tensor.transpose(bank[6][:, :P], wt_turned[:], identity[:])
-
-        round_xT(1, 0, on_vector)
-        round_xT(1, 1, on_vector)
         for h in range(2):
+            round_xT(1, h, on_vector)
             for t in range(PACK):
-                cols = slice(t * P + dealt(h).start, t * P + dealt(h).stop)
+                cols = slice(t * P + h * P // 2, t * P + (h + 1) * P // 2)
                 quantize(
-                    xT_codes[1][:, cols].bitcast(E4M3),
-                    xT_sc[1][:, cols],
-                    xT_bf[1][:, t, dealt(h), :].rearrange("p m j -> p (m j)"),
+                    xT_codes[1][:, cols].bitcast(E4M3), xT_sc[1][:, cols], late_xT[:, h, t].rearrange("p m j -> p (m j)")
                 )
 
+        subtract(0, 0, pairs[0], nc.vector)
+        subtract(0, 1, pairs[0], nc.vector)
+        subtract(0, 0, pairs[1], nc.vector)
+        subtract(0, 1, pairs[1], nc.gpsimd)
         for e in range(2):
-            subtract(0, 0, e, nc.vector)
-        subtract(0, 1, 0, nc.gpsimd)
-        for e in range(2):
-            weigh_and_interleave(0, 0, e)
-        means(1, 0, 0, 0)
-        means(1, 0, 1, 1)
-        last_means()
-        subtract(1, 0, 0, nc.vector)
+            weigh(0, 0, sides[e])
         quantize_g(0, 0)
-        subtract(1, 0, 1, nc.vector)
-        subtract(0, 1, 1, nc.gpsimd)
+
+        for h, q, b in ((0, 0, 3), (0, 1, 0), (1, 0, 1), (1, 1, 2)):
+            means(1, h, pairs[q], b)
+        subtract(1, 0, pairs[0], nc.vector)
+        subtract(1, 0, pairs[1], nc.vector)
+        subtract(1, 1, pairs[0], nc.gpsimd)
         for e in range(2):
-            weigh_and_interleave(1, 0, e)
-        weigh_last_y()
+            weigh(1, 0, sides[e])
         quantize_g(1, 0)
         for o in range(PASSES):
             round_xm(0, o, on_scalar)
-        quantize(xm_codes[0][:].bitcast(E4M3), xm_sc[0][:], first_bf)
-        finish_last_rows()
-        for o in range(PASSES):
-            round_xm(1, o, on_scalar)
-        multiply(0, 0, 7)
-        interleave_last_rows(slice(0, SIDE // 2))
-        drain_on_scalar(0, 0, 7)
-        interleave_last_rows(slice(SIDE // 2, SIDE))
+        quantize_xm(0, xm_bf[0])
+        subtract(1, 1, pairs[1], nc.gpsimd)
+        multiply(0, 0, 5)
+        on_scalar(
+            xm_bf[1].rearrange("p (o c i t) -> p o c t i", o=PASSES, i=RUN, t=PACK),
+            early_placed[:, :, :, sides[1]].rearrange("p o t (c i) -> p o c t i", i=RUN),
+        )
+        drain_on_scalar(0, 0, 5)
         scatter_on_scalar(0, 0)
 
-        subtract(1, 1, 1, nc.gpsimd)
-        for e in range(2):
-            weigh_and_interleave(0, 1, e)
-        quantize(xm_codes[1][:].bitcast(E4M3), xm_sc[1][:], flat(mean[0][1][:, 2:, :]).bitcast(BF16))
-        quantize_last_side(0)
-        weigh_and_interleave(1, 1, 1)
-        quantize_g(0, 1)
-        quantize_last_side(1)
+        weigh(0, 1, lo)
+        quantize_xm(1, xm_bf[1])
+        weigh(1, 1, sides[1])
+        quantize(g_codes[0][1][:].bitcast(E5M2), g_sc[0][1][:], g_flat[0][1])
+        weigh(1, 1, sides[0])
+        for e, b in ((1, 3), (0, 0)):
+            multiply(0, 1, b, cols=sides[e], only=(0,))
         multiply(1, 0, 2)
-        for e, b in ((0, 0), (1, 3)):
-            multiply(0, 1, b, order=(1, 0) if e == 0 else (0, 1), cols=sides[e])
+        for e, b in ((1, 3), (0, 0)):
+            quantize_side(1, 1, e)
+            multiply(0, 1, b, cols=sides[e], only=(1,))
             drain_on_scalar(0, 1, b, sides[e])
         scatter_on_scalar(0, 1)
         store(0)
@@ -407,11 +351,11 @@ def tile_attend_gpoi_w_kernel(tc, xT, w_words, w_scales, y, wt, xm, offs, out):
         for o in range(PASSES):
             round_xm(2, o, on_vector)
         drain_on_vector(1, 0, 2)
-        quantize_late_xm(2)
+        quantize_xm(2, late_bf)
         drain_on_vector(1, 1, 7)
         nc.gpsimd.tensor_scalar(
             late_bf.rearrange("p (o i t) -> p o i t", o=PASSES, t=PACK),
-            raw3.rearrange("p (o t i) -> p o i t", o=PASSES, t=PACK),
+            late_placed[:, :, :, sides[1]].rearrange("p o t i -> p o i t"),
             1.0,
             0.0,
             MUL,
@@ -424,8 +368,8 @@ def tile_attend_gpoi_w_kernel(tc, xT, w_words, w_scales, y, wt, xm, offs, out):
         scatter_on_scalar(1, 1)
         store(1)
         drain_on_vector(2, 1, 1)
-        quantize_late_xm(3)
-        nc.vector.tensor_copy(windows[2][:].indirect(offsets[:]), dw2_and_raw3[:, :N])
+        quantize_xm(3, late_bf)
+        nc.vector.tensor_copy(windows[2][:].indirect(offsets[:]), dw2)
         store(2)
         for h, b in ((0, 4), (1, 5)):
             multiply(3, h, b)

@@ -66,7 +66,8 @@ def tile_attend_gpoi_w_kernel(tc, xT, w_words, w_scales, y, wt, xm, offs, out):
         wt_rows = tile("wt_rows", [P, K_PASS], F32)
         wt_psum = bank[6][:].rearrange("p (t o) -> p o t", t=PACK)
         xT_raw = units("xT_raw", placed, F32)
-        y_sb = units("y_sb", [P, 2, N], F32)
+        wt_sb = tile("wt_sb", [P, PACK], F32)
+        y_sb = units("y_sb", placed, F32)
         windows = [tile(f"window{c}", [P, T], F32) for c in range(D_BLOCKS)]
 
         w_codes = tile("w_codes", [P, N], U32)
@@ -81,49 +82,43 @@ def tile_attend_gpoi_w_kernel(tc, xT, w_words, w_scales, y, wt, xm, offs, out):
         g_codes = units("g_codes", [P, HALF], U32)
         g_sc = units("g_sc", [P, HALF], U8)
 
-        def mean_pair(name):
-            return tile(name, [P, 2, HALF], F32)[:]
 
-        raw_step = 2 * UNIT - SIDE
-        strip = tile("strip", [P, 2 * raw_step], F32)
-        early_placed = strip[:].rearrange("p (o w) -> p o w", o=PASSES)[:, :, :UNIT].rearrange("p o (t i) -> p o t i", t=PACK)
-        last_residual = tile("last_residual", [P, UNIT], F32)
-        high_g = strip[:, raw_step + SIDE - K_PASS : raw_step + SIDE]
-        last_g = strip[:, raw_step + UNIT - SIDE : raw_step + UNIT - SIDE + K_PASS]
-        high_residual = tile("high_residual", [P, UNIT], F32)
+        low_strip = tile("low_strip", [P, K_PASS - SIDE + UNIT], F32)
+        low_residual = low_strip[:, :UNIT]
         mean = [
-            [
-                [mean_pair(f"mean00{q}") for q in range(2)],
-                [high_residual[:, K_PASS:].rearrange("p (t i) -> p t i", t=2), mean_pair("mean011")],
-            ],
-            [
-                [last_residual[:, :K_PASS].rearrange("p (t i) -> p t i", t=2), mean_pair("mean101")],
-                [mean_pair(f"mean11{q}") for q in range(2)],
-            ],
+            [by_place(low_strip[:, K_PASS - SIDE :]), tile("mean01", placed, F32)[:]],
+            [tile(f"mean1{h}", placed, F32)[:] for h in range(2)],
         ]
 
-        def mean_of(o, h, places):
-            q = places.start // 2
-            return mean[o][h][q][:, places.start - 2 * q : places.stop - 2 * q, :]
-
+        strip = tile("strip", [P, UNIT + K_PASS], F32)
+        high_residual = strip[:, :UNIT]
+        first_bf = strip[:, UNIT - HALF : UNIT + HALF].bitcast(BF16)
+        last_residual = strip[:, UNIT:]
+        second_raw = tile("second_raw", [P, 2 * K_PASS], F32)
         g_words = [
-            [tile("g_words00", [P, K_PASS], F32)[:], high_g],
-            [tile("g_words10", [P, K_PASS], F32)[:], last_g],
+            [strip[:, :K_PASS], tile("g_words01", [P, K_PASS], F32)[:]],
+            [tile("g_words10", [P, K_PASS], F32)[:], second_raw[:, HALF : HALF + K_PASS]],
         ]
         g_flat = [[g_words[o][h].bitcast(BF16) for h in range(2)] for o in range(PASSES)]
         residual = [
-            [tile("residual00", placed, F32)[:], by_place(high_residual[:])],
-            [tile("residual10", placed, F32)[:], by_place(last_residual[:])],
+            [tile("residual00", placed, F32)[:], by_place(high_residual)],
+            [by_place(low_residual), None],
         ]
-
+        turned_means = tile("turned_means", [P, PACK, P], F32)
+        weighed = tile("weighed", [P, PACK, SIDE], F32)
+        last_rows = tile("last_rows", [P, PACK, SIDE], BF16)
+        early_raw = [
+            [tile(f"raw0{o}", [P, PACK, P], F32)[:] for o in range(PASSES)],
+            [tile("raw10", [P, PACK, P], F32)[:], by_place(second_raw[:, :K_PASS])],
+        ]
         late_raw = tile("late_raw", [P, PASSES, HALF + UNIT], F32)
         late_placed = late_raw[:, :, HALF:].rearrange("p o (t i) -> p o t i", t=PACK)
-        raw = [[early_placed[:, o] for o in range(PASSES)], [late_placed[:, o] for o in range(PASSES)]]
-        late_bf = last_residual[:, K_PASS:].bitcast(BF16)
-        xm_bf = [late_bf, tile("xm_bf1", [P, UNIT], BF16)[:], late_bf]
+        raw = early_raw + [[late_placed[:, o, :, cols] for o in range(PASSES)] for cols in sides]
+        late_bf = g_flat[1][1]
+        xm_bf = [first_bf, tile("xm_bf1", [P, UNIT], BF16)[:], late_bf]
         dw2 = late_raw[:, 1, :N]
         dw_sb = [
-            [tile("dw00", [P, HALF], F32)[:], tile("dw01", [P, HALF], F32)[:]],
+            [second_raw[:, :HALF], tile("dw01", [P, HALF], F32)[:]],
             [late_raw[:, 0, SIDE : SIDE + HALF], tile("dw11", [P, HALF], F32)[:]],
             [dw2[:, lo], dw2[:, hi]],
             [tile("dw30", [P, HALF], F32)[:], tile("dw31", [P, HALF], F32)[:]],
@@ -154,12 +149,15 @@ def tile_attend_gpoi_w_kernel(tc, xT, w_words, w_scales, y, wt, xm, offs, out):
             r0 = o * K_PASS + h * HALF
             nc.sync.dma_start(out=xT_raw[o][h][:], in_=xT_v[:, :, r0 : r0 + HALF])
 
-        def load_y(o, places):
-            nc.sync.dma_start(out=y_sb[o][places.start // 2][:], in_=y_v[o, :, places, :])
+        def load_y(o, h, cols=lo):
+            nc.sync.dma_start(out=y_sb[o][h][:, :, cols], in_=y_v[o, :, :, halves[h]][:, :, cols])
 
-        def load_xm(pair):
+        def load_xm(c, o):
+            nc.sync.dma_start(out=raw[c][o], in_=xm_v[o, :, :, c * P : (c + 1) * P])
+
+        def load_late_xm():
             for o in range(PASSES):
-                nc.sync.dma_start(out=raw[pair][o], in_=xm_v[o, :, :, pair * HALF : (pair + 1) * HALF])
+                nc.sync.dma_start(out=late_placed[:, o], in_=xm_v[o, :, :, hi])
 
         def round_xT(o, h, copy, places=slice(0, PACK)):
             dealt = late_xT[:, h] if o else xT_bf[0][:, :, h * P // 2 : (h + 1) * P // 2, :]
@@ -185,7 +183,7 @@ def tile_attend_gpoi_w_kernel(tc, xT, w_words, w_scales, y, wt, xm, offs, out):
                     start=True,
                     stop=True,
                 )
-            nc.scalar.activation(out=mean_of(o, h, places), in_=scores, func=EXP)
+            nc.scalar.activation(out=mean[o][h][:, places, :], in_=scores, func=EXP)
 
         def walk_words(ap):
             return ap.rearrange("p (c i) t -> p c t i", i=RUN)
@@ -196,15 +194,15 @@ def tile_attend_gpoi_w_kernel(tc, xT, w_words, w_scales, y, wt, xm, offs, out):
         def subtract(o, h, places, engine):
             engine.tensor_tensor(
                 residual[o][h][:, places, :],
-                mean_of(o, h, places),
-                y_sb[o][places.start // 2][:, places.start % 2 : (places.stop - 1) % 2 + 1, halves[h]],
+                mean[o][h][:, places, :],
+                y_sb[o][h][:, places, :],
                 SUB,
             )
 
-        def weigh(o, h, cols):
+        def weigh(o, h, cols, values):
             nc.vector.tensor_tensor(
                 walk_words(by_word(g_flat[o][h])[:, cols, :]),
-                walk_places(residual[o][h][:, :, cols]),
+                walk_places(values),
                 wt_psum[:, o, :].unsqueeze(1).unsqueeze(3).to_broadcast([P, (cols.stop - cols.start) // RUN, PACK, RUN]),
                 MUL,
             )
@@ -212,7 +210,7 @@ def tile_attend_gpoi_w_kernel(tc, xT, w_words, w_scales, y, wt, xm, offs, out):
         def round_xm(c, o, copy):
             copy(
                 walk_words(by_word(xm_bf[c][:, o * K_PASS : (o + 1) * K_PASS])),
-                walk_places(raw[c // 2][o][:, :, sides[c % 2]]),
+                walk_places(raw[c][o]),
             )
 
         def quantize_xm(c, values):
@@ -229,18 +227,45 @@ def tile_attend_gpoi_w_kernel(tc, xT, w_words, w_scales, y, wt, xm, offs, out):
             for e in range(2):
                 quantize_side(o, h, e)
 
-        def multiply(c, h, b, order=(0, 1), cols=lo, only=(0, 1)):
+        def multiply(c, h, b, order=(0, 1), cols=lo):
             for o in order:
-                if o in only:
-                    nc.tensor.matmul_mx(
-                        out=bank[b][:, cols],
-                        lhsT=xm_codes[c][:, o * P : (o + 1) * P].bitcast(E4M3),
-                        lhsT_scale=xm_sc[c][:, o * P : (o + 1) * P],
-                        rhs=g_codes[o][h][:, cols].bitcast(E5M2),
-                        rhs_scale=g_sc[o][h][:, cols],
-                        start=o == order[0],
-                        stop=o == order[1],
-                    )
+                nc.tensor.matmul_mx(
+                    out=bank[b][:, cols],
+                    lhsT=xm_codes[c][:, o * P : (o + 1) * P].bitcast(E4M3),
+                    lhsT_scale=xm_sc[c][:, o * P : (o + 1) * P],
+                    rhs=g_codes[o][h][:, cols].bitcast(E5M2),
+                    rhs_scale=g_sc[o][h][:, cols],
+                    start=o == order[0],
+                    stop=o == order[1],
+                )
+
+        def last_means():
+            slots = slice(HALF, HALF + SIDE)
+            nc.tensor.matmul_mx(
+                out=bank[5][:],
+                lhsT=w_codes[:, slots].bitcast(E4M3),
+                lhsT_scale=w_sc[:, slots],
+                rhs=xT_codes[1][:].bitcast(E4M3),
+                rhs_scale=xT_sc[1][:],
+                start=True,
+                stop=True,
+            )
+            nc.scalar.activation(out=turned_means[:], in_=by_place(bank[5][:]), func=EXP)
+            slots = slice(HALF + SIDE, N)
+            for t in range(PACK):
+                rows = slice(t * P, (t + 1) * P)
+                nc.tensor.matmul_mx(
+                    out=bank[1][:, rows],
+                    lhsT=xT_codes[1][:, rows].bitcast(E4M3),
+                    lhsT_scale=xT_sc[1][:, rows],
+                    rhs=w_codes[:, slots].bitcast(E4M3),
+                    rhs_scale=w_sc[:, slots],
+                    start=True,
+                    stop=True,
+                )
+            nc.scalar.activation(out=mean[1][1][:, :, sides[1]], in_=by_place(bank[1][:]), func=EXP)
+            for t in range(PACK):
+                nc.tensor.transpose(bank[4][:, t * P : (t + 1) * P], turned_means[:, t, :], identity[:])
 
         def drain_on_scalar(c, h, b, cols=lo):
             on_scalar(dw_sb[c][h][:, cols], bank[b][:, cols])
@@ -268,11 +293,15 @@ def tile_attend_gpoi_w_kernel(tc, xT, w_words, w_scales, y, wt, xm, offs, out):
         nc.sync.dma_start(out=table_words[:], in_=w_words[0].rearrange("p n t -> p (n t)").bitcast(I32))
         load_xT(1, 0)
         load_xT(1, 1)
-        for o in range(PASSES):
-            for places in pairs:
-                load_y(o, places)
-        load_xm(0)
-        load_xm(1)
+        load_y(0, 0)
+        load_y(1, 0)
+        load_y(0, 1)
+        load_xm(0, 0)
+        load_xm(0, 1)
+        for e in range(2):
+            load_y(1, 1, sides[e])
+            load_xm(1, e)
+        load_late_xm()
 
         make_identity(nc, identity[:])
         zero_on_vector(windows[0][:].bitcast(I32))
@@ -285,6 +314,7 @@ def tile_attend_gpoi_w_kernel(tc, xT, w_words, w_scales, y, wt, xm, offs, out):
         round_xT(0, 0, on_scalar_activation)
         for t in range(PACK):
             nc.tensor.transpose(bank[6][:, t * P : (t + 1) * P], wt_rows[:, t::PACK], identity[:])
+        on_scalar(wt_sb[:], wt_psum[:, 1, :])
         round_xT(0, 1, on_scalar)
         quantize(xT_codes[0][:].bitcast(E4M3), xT_sc[0][:], xT_words[0][:].bitcast(BF16))
         for cols in halves:
@@ -292,57 +322,63 @@ def tile_attend_gpoi_w_kernel(tc, xT, w_words, w_scales, y, wt, xm, offs, out):
 
         means(0, 0, slice(0, 1), 3)
         means(0, 0, slice(1, 2), 0)
-        means(0, 1, pairs[0], 1)
-        means(0, 0, pairs[1], 2)
+        means(0, 0, pairs[1], 1)
+        means(0, 1, pairs[0], 2)
         means(0, 1, pairs[1], 7)
 
         for h in range(2):
-            round_xT(1, h, on_vector)
+            for places in pairs:
+                round_xT(1, h, on_vector, places)
             for t in range(PACK):
                 cols = slice(t * P + h * P // 2, t * P + (h + 1) * P // 2)
                 quantize(
                     xT_codes[1][:, cols].bitcast(E4M3), xT_sc[1][:, cols], late_xT[:, h, t].rearrange("p m j -> p (m j)")
                 )
 
-        subtract(0, 0, pairs[0], nc.vector)
-        subtract(0, 1, pairs[0], nc.vector)
-        subtract(0, 0, pairs[1], nc.vector)
-        subtract(0, 1, pairs[1], nc.gpsimd)
-        for e in range(2):
-            weigh(0, 0, sides[e])
-        quantize_g(0, 0)
-
-        for h, q, b in ((0, 0, 3), (0, 1, 0), (1, 0, 1), (1, 1, 2)):
-            means(1, h, pairs[q], b)
-        subtract(1, 0, pairs[0], nc.vector)
+        for q, b in ((0, 3), (1, 0)):
+            means(1, 0, pairs[q], b)
+        last_means()
+        for cols in sides:
+            nc.vector.tensor_tensor(residual[0][0][:, :, cols], mean[0][0][:, :, cols], y_sb[0][0][:, :, cols], SUB)
+        subtract(1, 0, pairs[0], nc.gpsimd)
+        for cols in sides:
+            weigh(0, 0, cols, residual[0][0][:, :, cols])
         subtract(1, 0, pairs[1], nc.vector)
-        subtract(1, 1, pairs[0], nc.gpsimd)
-        for e in range(2):
-            weigh(1, 0, sides[e])
+        quantize(g_codes[0][0][:].bitcast(E5M2), g_sc[0][0][:], g_flat[0][0])
+        subtract(0, 1, pairs[0], nc.gpsimd)
+        for cols in sides:
+            weigh(1, 0, cols, residual[1][0][:, :, cols])
         quantize_g(1, 0)
+        subtract(0, 1, slice(2, 3), nc.vector)
         for o in range(PASSES):
             round_xm(0, o, on_scalar)
         quantize_xm(0, xm_bf[0])
-        subtract(1, 1, pairs[1], nc.gpsimd)
-        multiply(0, 0, 5)
-        on_scalar(
-            xm_bf[1].rearrange("p (o c i t) -> p o c t i", o=PASSES, i=RUN, t=PACK),
-            early_placed[:, :, :, sides[1]].rearrange("p o t (c i) -> p o c t i", i=RUN),
-        )
-        drain_on_scalar(0, 0, 5)
+        subtract(0, 1, slice(3, 4), nc.gpsimd)
+        nc.gpsimd.tensor_tensor(by_place(last_residual), mean[1][1][:, :, sides[1]], y_sb[1][1][:, :, sides[1]], SUB)
+        multiply(0, 0, 7)
+        for t in range(PACK):
+            nc.scalar.activation(
+                out=weighed[:, t, :], in_=y_sb[1][1][:, t, sides[0]], func=COPY, scale=wt_sb[:, t : t + 1]
+            )
+        for t in range(PACK):
+            nc.vector.scalar_tensor_tensor(
+                last_rows[:, t, :], bank[4][:, t * P : (t + 1) * P], wt_sb[:, t : t + 1], weighed[:, t, :], MUL, SUB
+            )
+        for o in range(PASSES):
+            round_xm(1, o, on_scalar)
+        drain_on_scalar(0, 0, 7)
+        on_scalar(walk_words(by_word(g_flat[1][1])[:, sides[0], :]), walk_places(last_rows[:]))
         scatter_on_scalar(0, 0)
 
-        weigh(0, 1, lo)
+        for cols in sides:
+            weigh(0, 1, cols, residual[0][1][:, :, cols])
         quantize_xm(1, xm_bf[1])
-        weigh(1, 1, sides[1])
+        weigh(1, 1, sides[1], by_place(last_residual))
         quantize(g_codes[0][1][:].bitcast(E5M2), g_sc[0][1][:], g_flat[0][1])
-        weigh(1, 1, sides[0])
-        for e, b in ((1, 3), (0, 0)):
-            multiply(0, 1, b, cols=sides[e], only=(0,))
         multiply(1, 0, 2)
-        for e, b in ((1, 3), (0, 0)):
+        for e, b in ((0, 0), (1, 3)):
             quantize_side(1, 1, e)
-            multiply(0, 1, b, cols=sides[e], only=(1,))
+            multiply(0, 1, b, cols=sides[e])
             drain_on_scalar(0, 1, b, sides[e])
         scatter_on_scalar(0, 1)
         store(0)

@@ -28,6 +28,8 @@ D_BLOCKS = D // P
 HALF = 256
 SIDE = HALF // 2
 UNIT = PACK * HALF
+EARLY = 108
+LAP = 64
 RUN = 4
 
 
@@ -83,33 +85,31 @@ def tile_attend_gpoi_w_kernel(tc, xT, w_words, w_scales, y, wt, xm, offs, out):
         g_sc = units("g_sc", [P, HALF], U8)
 
 
-        low_strip = tile("low_strip", [P, K_PASS - SIDE + UNIT], F32)
-        low_residual = low_strip[:, :UNIT]
+        late = HALF - EARLY
+        first_strip = tile("first_strip", [P, PACK * EARLY - LAP + UNIT], F32)
+        strip = tile("strip", [P, 3 * UNIT], F32)
+        late_start = UNIT - LAP
+        bf_start = late_start + PACK * late - LAP // 2
+        high_residual = [by_place(first_strip[:, : PACK * EARLY]), by_place(strip[:, late_start : late_start + PACK * late])]
+        first_bf = strip[:, bf_start : bf_start + K_PASS].bitcast(BF16)
+        last_residual = strip[:, bf_start + HALF : bf_start + HALF + K_PASS]
         mean = [
-            [by_place(low_strip[:, K_PASS - SIDE :]), tile("mean01", placed, F32)[:]],
-            [tile(f"mean1{h}", placed, F32)[:] for h in range(2)],
+            [by_place(first_strip[:, PACK * EARLY - LAP :]), tile("mean01", placed, F32)[:]],
+            [by_place(strip[:, :UNIT]), tile("mean11", placed, F32)[:]],
         ]
-
-        strip = tile("strip", [P, UNIT + K_PASS], F32)
-        high_residual = strip[:, :UNIT]
-        first_bf = strip[:, UNIT - HALF : UNIT + HALF].bitcast(BF16)
-        last_residual = strip[:, UNIT:]
         second_raw = tile("second_raw", [P, 2 * K_PASS], F32)
         g_words = [
-            [strip[:, :K_PASS], tile("g_words01", [P, K_PASS], F32)[:]],
-            [tile("g_words10", [P, K_PASS], F32)[:], second_raw[:, HALF : HALF + K_PASS]],
+            [tile(f"g_words0{h}", [P, K_PASS], F32)[:] for h in range(2)],
+            [tile("g_words10", [P, K_PASS], F32)[:], second_raw[:, K_PASS:]],
         ]
         g_flat = [[g_words[o][h].bitcast(BF16) for h in range(2)] for o in range(PASSES)]
-        residual = [
-            [tile("residual00", placed, F32)[:], by_place(high_residual)],
-            [by_place(low_residual), None],
-        ]
+        residual = passes("residual", placed, F32)
         turned_means = tile("turned_means", [P, PACK, P], F32)
         weighed = tile("weighed", [P, PACK, SIDE], F32)
         last_rows = tile("last_rows", [P, PACK, SIDE], BF16)
         early_raw = [
-            [tile(f"raw0{o}", [P, PACK, P], F32)[:] for o in range(PASSES)],
-            [tile("raw10", [P, PACK, P], F32)[:], by_place(second_raw[:, :K_PASS])],
+            [tile("raw00", [P, PACK, P], F32)[:], by_place(g_words[0][1])],
+            [tile("raw10", [P, PACK, P], F32)[:], by_place(second_raw[:, K_PASS - LAP :][:, :K_PASS])],
         ]
         late_raw = tile("late_raw", [P, PASSES, HALF + UNIT], F32)
         late_placed = late_raw[:, :, HALF:].rearrange("p o (t i) -> p o t i", t=PACK)
@@ -118,7 +118,7 @@ def tile_attend_gpoi_w_kernel(tc, xT, w_words, w_scales, y, wt, xm, offs, out):
         xm_bf = [first_bf, tile("xm_bf1", [P, UNIT], BF16)[:], late_bf]
         dw2 = late_raw[:, 1, :N]
         dw_sb = [
-            [second_raw[:, :HALF], tile("dw01", [P, HALF], F32)[:]],
+            [second_raw[:, HALF:K_PASS], tile("dw01", [P, HALF], F32)[:]],
             [late_raw[:, 0, SIDE : SIDE + HALF], tile("dw11", [P, HALF], F32)[:]],
             [dw2[:, lo], dw2[:, hi]],
             [tile("dw30", [P, HALF], F32)[:], tile("dw31", [P, HALF], F32)[:]],
@@ -191,13 +191,8 @@ def tile_attend_gpoi_w_kernel(tc, xT, w_words, w_scales, y, wt, xm, offs, out):
         def walk_places(ap):
             return ap.rearrange("p t (c i) -> p c t i", i=RUN)
 
-        def subtract(o, h, places, engine):
-            engine.tensor_tensor(
-                residual[o][h][:, places, :],
-                mean[o][h][:, places, :],
-                y_sb[o][h][:, places, :],
-                SUB,
-            )
+        def subtract(dst, o, h, cols, engine):
+            engine.tensor_tensor(dst, mean[o][h][:, :, cols], y_sb[o][h][:, :, cols], SUB)
 
         def weigh(o, h, cols, values):
             nc.vector.tensor_tensor(
@@ -207,10 +202,10 @@ def tile_attend_gpoi_w_kernel(tc, xT, w_words, w_scales, y, wt, xm, offs, out):
                 MUL,
             )
 
-        def round_xm(c, o, copy):
+        def round_xm(c, o, copy, cols=slice(0, P)):
             copy(
-                walk_words(by_word(xm_bf[c][:, o * K_PASS : (o + 1) * K_PASS])),
-                walk_places(raw[c][o]),
+                walk_words(by_word(xm_bf[c][:, o * K_PASS : (o + 1) * K_PASS])[:, cols, :]),
+                walk_places(raw[c][o][:, :, cols]),
             )
 
         def quantize_xm(c, values):
@@ -294,8 +289,8 @@ def tile_attend_gpoi_w_kernel(tc, xT, w_words, w_scales, y, wt, xm, offs, out):
         load_xT(1, 0)
         load_xT(1, 1)
         load_y(0, 0)
-        load_y(1, 0)
         load_y(0, 1)
+        load_y(1, 0)
         load_xm(0, 0)
         load_xm(0, 1)
         for e in range(2):
@@ -339,22 +334,23 @@ def tile_attend_gpoi_w_kernel(tc, xT, w_words, w_scales, y, wt, xm, offs, out):
             means(1, 0, pairs[q], b)
         last_means()
         for cols in sides:
-            nc.vector.tensor_tensor(residual[0][0][:, :, cols], mean[0][0][:, :, cols], y_sb[0][0][:, :, cols], SUB)
-        subtract(1, 0, pairs[0], nc.gpsimd)
+            subtract(residual[0][:, :, cols], 0, 0, cols, nc.vector)
+        subtract(high_residual[0], 0, 1, slice(0, EARLY), nc.gpsimd)
         for cols in sides:
-            weigh(0, 0, cols, residual[0][0][:, :, cols])
-        subtract(1, 0, pairs[1], nc.vector)
-        quantize(g_codes[0][0][:].bitcast(E5M2), g_sc[0][0][:], g_flat[0][0])
-        subtract(0, 1, pairs[0], nc.gpsimd)
-        for cols in sides:
-            weigh(1, 0, cols, residual[1][0][:, :, cols])
-        quantize_g(1, 0)
-        subtract(0, 1, slice(2, 3), nc.vector)
+            weigh(0, 0, cols, residual[0][:, :, cols])
+        quantize_g(0, 0)
+        for cols in reversed(sides):
+            subtract(residual[1][:, :, cols], 1, 0, cols, nc.vector)
+        subtract(high_residual[1][:, :, :EARLY], 0, 1, slice(EARLY, 2 * EARLY), nc.gpsimd)
+        for cols in reversed(sides):
+            weigh(1, 0, cols, residual[1][:, :, cols])
+        for e in reversed(range(2)):
+            quantize_side(1, 0, e)
         for o in range(PASSES):
             round_xm(0, o, on_scalar)
         quantize_xm(0, xm_bf[0])
-        subtract(0, 1, slice(3, 4), nc.gpsimd)
-        nc.gpsimd.tensor_tensor(by_place(last_residual), mean[1][1][:, :, sides[1]], y_sb[1][1][:, :, sides[1]], SUB)
+        subtract(high_residual[1][:, :, EARLY:], 0, 1, slice(2 * EARLY, HALF), nc.gpsimd)
+        subtract(by_place(last_residual), 1, 1, sides[1], nc.gpsimd)
         multiply(0, 0, 7)
         for t in range(PACK):
             nc.scalar.activation(
@@ -364,14 +360,15 @@ def tile_attend_gpoi_w_kernel(tc, xT, w_words, w_scales, y, wt, xm, offs, out):
             nc.vector.scalar_tensor_tensor(
                 last_rows[:, t, :], bank[4][:, t * P : (t + 1) * P], wt_sb[:, t : t + 1], weighed[:, t, :], MUL, SUB
             )
-        for o in range(PASSES):
-            round_xm(1, o, on_scalar)
+        round_xm(1, 0, on_scalar)
+        for cols in (slice(0, P // 2), slice(P // 2, P)):
+            round_xm(1, 1, on_scalar, cols)
         drain_on_scalar(0, 0, 7)
         on_scalar(walk_words(by_word(g_flat[1][1])[:, sides[0], :]), walk_places(last_rows[:]))
         scatter_on_scalar(0, 0)
 
-        for cols in sides:
-            weigh(0, 1, cols, residual[0][1][:, :, cols])
+        weigh(0, 1, slice(0, EARLY), high_residual[0])
+        weigh(0, 1, slice(EARLY, HALF), high_residual[1])
         quantize_xm(1, xm_bf[1])
         weigh(1, 1, sides[1], by_place(last_residual))
         quantize(g_codes[0][1][:].bitcast(E5M2), g_sc[0][1][:], g_flat[0][1])

@@ -89,10 +89,12 @@ def tile_attend_gpoi_w_kernel(tc, xT, w_words, w_scales, y, wt, xm, offs, out):
         first_strip = tile("first_strip", [P, PACK * EARLY - LAP + UNIT], F32)
         strip = tile("strip", [P, 3 * UNIT], F32)
         late_start = UNIT - LAP
-        bf_start = late_start + PACK * late - LAP // 2
+        last_start = late_start + PACK * late
+        bf_start = last_start + K_PASS - LAP
         high_residual = [by_place(first_strip[:, : PACK * EARLY]), by_place(strip[:, late_start : late_start + PACK * late])]
         first_bf = strip[:, bf_start : bf_start + K_PASS].bitcast(BF16)
-        last_residual = strip[:, bf_start + HALF : bf_start + HALF + K_PASS]
+        last_residual = strip[:, last_start : last_start + K_PASS]
+        last_rows = by_place(strip[:, bf_start + K_PASS - SIDE : bf_start + K_PASS + SIDE].bitcast(BF16))
         mean = [
             [by_place(first_strip[:, PACK * EARLY - LAP :]), tile("mean01", placed, F32)[:]],
             [by_place(strip[:, :UNIT]), tile("mean11", placed, F32)[:]],
@@ -106,7 +108,6 @@ def tile_attend_gpoi_w_kernel(tc, xT, w_words, w_scales, y, wt, xm, offs, out):
         residual = passes("residual", placed, F32)
         turned_means = tile("turned_means", [P, PACK, P], F32)
         weighed = tile("weighed", [P, PACK, SIDE], F32)
-        last_rows = tile("last_rows", [P, PACK, SIDE], BF16)
         early_raw = [
             [tile("raw00", [P, PACK, P], F32)[:], by_place(g_words[0][1])],
             [tile("raw10", [P, PACK, P], F32)[:], by_place(second_raw[:, K_PASS - LAP :][:, :K_PASS])],
@@ -202,6 +203,12 @@ def tile_attend_gpoi_w_kernel(tc, xT, w_words, w_scales, y, wt, xm, offs, out):
                 MUL,
             )
 
+        def finish_rows(places):
+            for t in reversed(range(places.start, places.stop)):
+                nc.vector.scalar_tensor_tensor(
+                    last_rows[:, t, :], bank[4][:, t * P : (t + 1) * P], wt_sb[:, t : t + 1], weighed[:, t, :], MUL, SUB
+                )
+
         def round_xm(c, o, copy, cols=slice(0, P)):
             copy(
                 walk_words(by_word(xm_bf[c][:, o * K_PASS : (o + 1) * K_PASS])[:, cols, :]),
@@ -292,10 +299,11 @@ def tile_attend_gpoi_w_kernel(tc, xT, w_words, w_scales, y, wt, xm, offs, out):
         load_y(0, 1)
         load_y(1, 0)
         load_xm(0, 0)
+        load_y(1, 1, sides[0])
         load_xm(0, 1)
-        for e in range(2):
-            load_y(1, 1, sides[e])
-            load_xm(1, e)
+        load_xm(1, 0)
+        load_y(1, 1, sides[1])
+        load_xm(1, 1)
         load_late_xm()
 
         make_identity(nc, identity[:])
@@ -341,30 +349,27 @@ def tile_attend_gpoi_w_kernel(tc, xT, w_words, w_scales, y, wt, xm, offs, out):
         quantize_g(0, 0)
         for cols in reversed(sides):
             subtract(residual[1][:, :, cols], 1, 0, cols, nc.vector)
-        subtract(high_residual[1][:, :, :EARLY], 0, 1, slice(EARLY, 2 * EARLY), nc.gpsimd)
+        subtract(high_residual[1], 0, 1, slice(EARLY, HALF), nc.gpsimd)
         for cols in reversed(sides):
             weigh(1, 0, cols, residual[1][:, :, cols])
-        for e in reversed(range(2)):
-            quantize_side(1, 0, e)
-        for o in range(PASSES):
-            round_xm(0, o, on_scalar)
-        quantize_xm(0, xm_bf[0])
-        subtract(high_residual[1][:, :, EARLY:], 0, 1, slice(2 * EARLY, HALF), nc.gpsimd)
-        subtract(by_place(last_residual), 1, 1, sides[1], nc.gpsimd)
-        multiply(0, 0, 7)
-        for t in range(PACK):
+        round_xm(0, 0, on_scalar)
+        for t in reversed(range(PACK)):
             nc.scalar.activation(
                 out=weighed[:, t, :], in_=y_sb[1][1][:, t, sides[0]], func=COPY, scale=wt_sb[:, t : t + 1]
             )
-        for t in range(PACK):
-            nc.vector.scalar_tensor_tensor(
-                last_rows[:, t, :], bank[4][:, t * P : (t + 1) * P], wt_sb[:, t : t + 1], weighed[:, t, :], MUL, SUB
-            )
+        finish_rows(pairs[1])
+        for e in reversed(range(2)):
+            quantize_side(1, 0, e)
+        round_xm(0, 1, on_scalar)
+        quantize_xm(0, xm_bf[0])
+        subtract(by_place(last_residual), 1, 1, sides[1], nc.gpsimd)
+        multiply(0, 0, 7)
+        finish_rows(pairs[0])
         round_xm(1, 0, on_scalar)
         for cols in (slice(0, P // 2), slice(P // 2, P)):
             round_xm(1, 1, on_scalar, cols)
         drain_on_scalar(0, 0, 7)
-        on_scalar(walk_words(by_word(g_flat[1][1])[:, sides[0], :]), walk_places(last_rows[:]))
+        on_scalar(walk_words(by_word(g_flat[1][1])[:, sides[0], :]), walk_places(last_rows))
         scatter_on_scalar(0, 0)
 
         weigh(0, 1, slice(0, EARLY), high_residual[0])

@@ -30,6 +30,7 @@ SIDE = HALF // 2
 UNIT = PACK * HALF
 EARLY = 108
 LAP = 64
+TAIL = 16
 RUN = 4
 
 
@@ -99,10 +100,10 @@ def tile_attend_gpoi_w_kernel(tc, xT, w_words, w_scales, y, wt, xm, offs, out):
             [by_place(first_strip[:, PACK * EARLY - LAP :]), tile("mean01", placed, F32)[:]],
             [by_place(strip[:, :UNIT]), tile("mean11", placed, F32)[:]],
         ]
-        second_raw = tile("second_raw", [P, 2 * K_PASS], F32)
+        second_raw = tile("second_raw", [P, 2 * K_PASS + SIDE], F32)
         g_words = [
             [tile(f"g_words0{h}", [P, K_PASS], F32)[:] for h in range(2)],
-            [tile("g_words10", [P, K_PASS], F32)[:], second_raw[:, K_PASS:]],
+            [tile("g_words10", [P, K_PASS], F32)[:], second_raw[:, K_PASS - SIDE : UNIT - SIDE]],
         ]
         g_flat = [[g_words[o][h].bitcast(BF16) for h in range(2)] for o in range(PASSES)]
         residual = passes("residual", placed, F32)
@@ -112,15 +113,18 @@ def tile_attend_gpoi_w_kernel(tc, xT, w_words, w_scales, y, wt, xm, offs, out):
             [tile("raw00", [P, PACK, P], F32)[:], by_place(g_words[0][1])],
             [tile("raw10", [P, PACK, P], F32)[:], by_place(second_raw[:, K_PASS - LAP :][:, :K_PASS])],
         ]
-        late_raw = tile("late_raw", [P, PASSES, HALF + UNIT], F32)
-        late_placed = late_raw[:, :, HALF:].rearrange("p o (t i) -> p o t i", t=PACK)
+        late_raw = tile("late_raw", [P, PASSES, 2 * UNIT], F32)
+        late_placed = late_raw[:].rearrange("p o (t i) -> p o t i", t=PACK)[:, :, :, hi]
+        high1 = K_PASS + SIDE
         raw = early_raw + [[late_placed[:, o, :, cols] for o in range(PASSES)] for cols in sides]
         late_bf = g_flat[1][1]
         xm_bf = [first_bf, tile("xm_bf1", [P, UNIT], BF16)[:], late_bf]
-        dw2 = late_raw[:, 1, :N]
+        dw2 = late_raw[:, 1, UNIT : UNIT + N]
+        apart = UNIT - high1
+        tails = late_raw[:, 1, high1 + HALF - TAIL :][:, : 2 * apart].rearrange("p (e w) -> p e w", e=2)[:, :, :TAIL]
         dw_sb = [
-            [second_raw[:, HALF:K_PASS], tile("dw01", [P, HALF], F32)[:]],
-            [late_raw[:, 0, SIDE : SIDE + HALF], tile("dw11", [P, HALF], F32)[:]],
+            [second_raw[:, UNIT - SIDE :], tile("dw01", [P, HALF], F32)[:]],
+            [late_raw[:, 1, LAP : HALF + LAP], late_raw[:, 1, high1 : high1 + HALF]],
             [dw2[:, lo], dw2[:, hi]],
             [tile("dw30", [P, HALF], F32)[:], tile("dw31", [P, HALF], F32)[:]],
         ]
@@ -209,6 +213,9 @@ def tile_attend_gpoi_w_kernel(tc, xT, w_words, w_scales, y, wt, xm, offs, out):
                     last_rows[:, t, :], bank[4][:, t * P : (t + 1) * P], wt_sb[:, t : t + 1], weighed[:, t, :], MUL, SUB
                 )
 
+        def interleave_last_rows(cols):
+            on_scalar(walk_words(by_word(g_flat[1][1])[:, cols, :]), walk_places(last_rows[:, :, cols]))
+
         def round_xm(c, o, copy, cols=slice(0, P)):
             copy(
                 walk_words(by_word(xm_bf[c][:, o * K_PASS : (o + 1) * K_PASS])[:, cols, :]),
@@ -229,10 +236,10 @@ def tile_attend_gpoi_w_kernel(tc, xT, w_words, w_scales, y, wt, xm, offs, out):
             for e in range(2):
                 quantize_side(o, h, e)
 
-        def multiply(c, h, b, order=(0, 1), cols=lo):
+        def multiply(c, h, b, order=(0, 1), cols=lo, at=None):
             for o in order:
                 nc.tensor.matmul_mx(
-                    out=bank[b][:, cols],
+                    out=bank[b][:, at or cols],
                     lhsT=xm_codes[c][:, o * P : (o + 1) * P].bitcast(E4M3),
                     lhsT_scale=xm_sc[c][:, o * P : (o + 1) * P],
                     rhs=g_codes[o][h][:, cols].bitcast(E5M2),
@@ -302,8 +309,8 @@ def tile_attend_gpoi_w_kernel(tc, xT, w_words, w_scales, y, wt, xm, offs, out):
         load_y(1, 1, sides[0])
         load_xm(0, 1)
         load_xm(1, 0)
-        load_y(1, 1, sides[1])
         load_xm(1, 1)
+        load_y(1, 1, sides[1])
         load_late_xm()
 
         make_identity(nc, identity[:])
@@ -368,8 +375,9 @@ def tile_attend_gpoi_w_kernel(tc, xT, w_words, w_scales, y, wt, xm, offs, out):
         round_xm(1, 0, on_scalar)
         for cols in (slice(0, P // 2), slice(P // 2, P)):
             round_xm(1, 1, on_scalar, cols)
+        interleave_last_rows(slice(0, SIDE // 2))
         drain_on_scalar(0, 0, 7)
-        on_scalar(walk_words(by_word(g_flat[1][1])[:, sides[0], :]), walk_places(last_rows))
+        interleave_last_rows(slice(SIDE // 2, SIDE))
         scatter_on_scalar(0, 0)
 
         weigh(0, 1, slice(0, EARLY), high_residual[0])
@@ -386,11 +394,12 @@ def tile_attend_gpoi_w_kernel(tc, xT, w_words, w_scales, y, wt, xm, offs, out):
         store(0)
 
         multiply(1, 1, 7, order=(1, 0))
-        for o in range(PASSES):
-            round_xm(2, o, on_vector)
+        round_xm(2, 0, on_vector)
+        for cols in (slice(0, P // 2), slice(P // 2, P)):
+            round_xm(2, 1, on_vector, cols)
         drain_on_vector(1, 0, 2)
         quantize_xm(2, late_bf)
-        drain_on_vector(1, 1, 7)
+        on_vector(dw_sb[1][1][:, : HALF - TAIL], bank[7][:, : HALF - TAIL])
         nc.gpsimd.tensor_scalar(
             late_bf.rearrange("p (o i t) -> p o i t", o=PASSES, t=PACK),
             late_placed[:, :, :, sides[1]].rearrange("p o t i -> p o i t"),
@@ -400,9 +409,10 @@ def tile_attend_gpoi_w_kernel(tc, xT, w_words, w_scales, y, wt, xm, offs, out):
             ADD,
         )
         nc.vector.tensor_copy(windows[1][:].indirect(entries(lo)), dw_sb[1][0])
-        multiply(2, 0, 0)
+        multiply(2, 0, 7, at=hi)
         multiply(2, 1, 1)
-        drain_on_scalar(2, 0, 0)
+        on_scalar(dw2[:, : HALF - TAIL], bank[7][:, HALF : N - TAIL])
+        on_scalar(tails, bank[7][:].rearrange("p (e w) -> p e w", e=2)[:, :, HALF - TAIL :])
         scatter_on_scalar(1, 1)
         store(1)
         drain_on_vector(2, 1, 1)

@@ -303,8 +303,9 @@ def tile_attend_gpoi_w_kernel(tc, xT, w_words, w_scales, y, wt, xm, offs, out):
         load_xT(1, 0)
         load_xT(1, 1)
         load_y(0, 0)
-        load_y(0, 1)
+        load_y(0, 1, slice(0, SIDE))
         load_y(1, 0)
+        load_y(0, 1, slice(SIDE, HALF))
         load_xm(0, 0)
         load_y(1, 1, sides[0])
         load_xm(0, 1)

from contextlib import ExitStack

import concourse.mybir as mybir
from concourse.masks import make_identity

D, R, N, T = 512, 1024, 512, 2048
FLOPS = 2 * 2 * D * R * N

F32 = mybir.dt.float32
BF16 = mybir.dt.bfloat16
I32 = mybir.dt.int32
U32 = mybir.dt.uint32
U16 = mybir.dt.uint16
U8 = mybir.dt.uint8
E4M3 = mybir.dt.float8_e4m3fn_x4
E5M2 = mybir.dt.float8_e5m2_x4
COPY = mybir.ActivationFunctionType.Copy
EXP = mybir.ActivationFunctionType.Exp
ADD = mybir.AluOpType.add
SUB = mybir.AluOpType.subtract
MUL = mybir.AluOpType.mult

P = 128
PACK = 4
K_PASS = P * PACK
PASSES = R // K_PASS
D_BLOCKS = D // P
HALF = 256
SIDE = HALF // 2
UNIT = PACK * HALF
EARLY = 108
LAP = 64
TAIL = 16
RUN = 4


def tile_attend_gpoi_w_kernel(tc, xT, w_words, w_scales, y, wt, xm, offs, out):
    nc = tc.nc
    with ExitStack() as ctx:
        keep = ctx.enter_context(tc.tile_pool(name="keep", bufs=1))
        psum = ctx.enter_context(tc.psum_pool(name="psum", bufs=1))
        bank = [psum.tile([P, N], F32, name=f"bank{b}") for b in range(8)]

        def tile(name, shape, dtype):
            return keep.tile(shape, dtype, align_bytes=256, name=name)

        def units(name, shape, dtype):
            return [[tile(f"{name}{o}{h}", shape, dtype) for h in range(2)] for o in range(PASSES)]

        def passes(name, shape, dtype):
            return [tile(f"{name}{o}", shape, dtype) for o in range(PASSES)]

        def by_place(ap):
            return ap.rearrange("p (t i) -> p t i", t=PACK)

        def by_word(ap):
            return ap.rearrange("p (i t) -> p i t", t=PACK)

        lo, hi = slice(0, HALF), slice(HALF, N)
        halves = (lo, hi)
        sides = (slice(0, SIDE), slice(SIDE, HALF))
        pairs = (slice(0, 2), slice(2, 4))
        placed = [P, PACK, HALF]

        offsets = keep.tile([P, N // 16], U16)
        table_words = tile("table_words", [P, T], I32)
        table_scales = tile("table_scales", [P, T // 4], I32)
        identity = tile("identity", [P, P], F32)
        wt_rows = tile("wt_rows", [P, K_PASS], F32)
        wt_psum = bank[6][:].rearrange("p (t o) -> p o t", t=PACK)
        xT_raw = units("xT_raw", placed, F32)
        wt_sb = tile("wt_sb", [P, PACK], F32)
        y_sb = units("y_sb", placed, F32)
        windows = [tile(f"window{c}", [P, T], F32) for c in range(D_BLOCKS)]

        w_codes = tile("w_codes", [P, N], U32)
        w_sc = tile("w_sc", [P, N], U8)
        xT_words = passes("xT_words", [P, UNIT], F32)
        xT_bf = [words[:].bitcast(BF16).rearrange("p (t m j) -> p t m j", t=PACK, j=PACK) for words in xT_words[:1]]
        late_xT = xT_words[1][:].bitcast(BF16).rearrange("p (h t m j) -> p h t m j", h=2, t=PACK, j=PACK)
        xT_codes = passes("xT_codes", [P, K_PASS], U32)
        xT_sc = passes("xT_sc", [P, K_PASS], U8)
        xm_codes = [tile(f"xm_codes{c}", [P, PASSES * P], U32) for c in range(D_BLOCKS)]
        xm_sc = [tile(f"xm_sc{c}", [P, PASSES * P], U8) for c in range(D_BLOCKS)]
        g_codes = units("g_codes", [P, HALF], U32)
        g_sc = units("g_sc", [P, HALF], U8)


        late = HALF - EARLY
        first_strip = tile("first_strip", [P, PACK * EARLY - LAP + UNIT], F32)
        strip = tile("strip", [P, 3 * UNIT], F32)
        late_start = UNIT - LAP
        last_start = late_start + PACK * late
        bf_start = last_start + K_PASS - LAP
        high_residual = [by_place(first_strip[:, : PACK * EARLY]), by_place(strip[:, late_start : late_start + PACK * late])]
        first_bf = strip[:, bf_start : bf_start + K_PASS].bitcast(BF16)
        last_residual = strip[:, last_start : last_start + K_PASS]
        last_rows = by_place(strip[:, bf_start + K_PASS - SIDE : bf_start + K_PASS + SIDE].bitcast(BF16))
        mean = [
            [by_place(first_strip[:, PACK * EARLY - LAP :]), tile("mean01", placed, F32)[:]],
            [by_place(strip[:, :UNIT]), tile("mean11", placed, F32)[:]],
        ]
        second_raw = tile("second_raw", [P, 2 * K_PASS + SIDE], F32)
        g_words = [
            [tile(f"g_words0{h}", [P, K_PASS], F32)[:] for h in range(2)],
            [tile("g_words10", [P, K_PASS], F32)[:], second_raw[:, K_PASS - SIDE : UNIT - SIDE]],
        ]
        g_flat = [[g_words[o][h].bitcast(BF16) for h in range(2)] for o in range(PASSES)]
        residual = passes("residual", placed, F32)
        turned_means = tile("turned_means", [P, PACK, P], F32)
        weighed = tile("weighed", [P, PACK, SIDE], F32)
        early_raw = [
            [tile("raw00", [P, PACK, P], F32)[:], by_place(g_words[0][1])],
            [tile("raw10", [P, PACK, P], F32)[:], by_place(second_raw[:, K_PASS - LAP :][:, :K_PASS])],
        ]
        late_raw = tile("late_raw", [P, PASSES, 2 * UNIT], F32)
        late_placed = late_raw[:].rearrange("p o (t i) -> p o t i", t=PACK)[:, :, :, hi]
        high1 = K_PASS + SIDE
        raw = early_raw + [[late_placed[:, o, :, cols] for o in range(PASSES)] for cols in sides]
        late_bf = g_flat[1][1]
        xm_bf = [first_bf, tile("xm_bf1", [P, UNIT], BF16)[:], late_bf]
        dw2 = late_raw[:, 1, UNIT : UNIT + N]
        apart = UNIT - high1
        tails = late_raw[:, 1, high1 + HALF - TAIL :][:, : 2 * apart].rearrange("p (e w) -> p e w", e=2)[:, :, :TAIL]
        dw_sb = [
            [second_raw[:, UNIT - SIDE :], tile("dw01", [P, HALF], F32)[:]],
            [late_raw[:, 1, LAP : HALF + LAP], late_raw[:, 1, high1 : high1 + HALF]],
            [dw2[:, lo], dw2[:, hi]],
            [tile("dw30", [P, HALF], F32)[:], tile("dw31", [P, HALF], F32)[:]],
        ]

        xT_v = xT[0].rearrange("(p j) r -> p j r", j=PACK)
        y_v = y[0].rearrange("(o p t) i -> o p t i", o=PASSES, t=PACK)
        xm_v = xm[0].rearrange("(o p t) d -> o p t d", o=PASSES, t=PACK)

        def on_vector(dst, src):
            nc.vector.tensor_copy(out=dst, in_=src)

        def on_scalar(dst, src):
            nc.scalar.copy(out=dst, in_=src)

        def on_scalar_activation(dst, src):
            nc.scalar.activation(out=dst, in_=src, func=COPY)

        def zero_on_vector(words):
            cut = words.shape[1] // 2 - 1
            nc.vector.memset(words[:, :cut], 0)
            nc.vector.memset(words[:, cut:], 0)

        def entries(cols):
            return offsets[:, cols.start // 16 : cols.stop // 16]

        def load_xT(o, h):
            r0 = o * K_PASS + h * HALF
            nc.sync.dma_start(out=xT_raw[o][h][:], in_=xT_v[:, :, r0 : r0 + HALF])

        def load_y(o, h, cols=lo):
            nc.sync.dma_start(out=y_sb[o][h][:, :, cols], in_=y_v[o, :, :, halves[h]][:, :, cols])

        def load_xm(c, o):
            nc.sync.dma_start(out=raw[c][o], in_=xm_v[o, :, :, c * P : (c + 1) * P])

        def load_late_xm():
            for o in range(PASSES):
                nc.sync.dma_start(out=late_placed[:, o], in_=xm_v[o, :, :, hi])

        def round_xT(o, h, copy, places=slice(0, PACK)):
            dealt = late_xT[:, h] if o else xT_bf[0][:, :, h * P // 2 : (h + 1) * P // 2, :]
            copy(
                dealt[:, places].rearrange("p t m j -> p m j t"),
                xT_raw[o][h][:].rearrange("p j (m t) -> p m j t", t=PACK)[:, :, :, places],
            )

        def quantize(codes, scales, values):
            nc.vector.quantize_mx(out=codes, scales=scales, in_=values)

        def means(o, h, places, b):
            count = places.stop - places.start
            scores = bank[b][:, : count * HALF].rearrange("p (e i) -> p e i", e=count)
            for e in range(count):
                rows = slice((places.start + e) * P, (places.start + e + 1) * P)
                nc.tensor.matmul_mx(
                    out=scores[:, e, :],
                    lhsT=xT_codes[o][:, rows].bitcast(E4M3),
                    lhsT_scale=xT_sc[o][:, rows],
                    rhs=w_codes[:, halves[h]].bitcast(E4M3),
                    rhs_scale=w_sc[:, halves[h]],
                    start=True,
                    stop=True,
                )
            nc.scalar.activation(out=mean[o][h][:, places, :], in_=scores, func=EXP)

        def walk_words(ap):
            return ap.rearrange("p (c i) t -> p c t i", i=RUN)

        def walk_places(ap):
            return ap.rearrange("p t (c i) -> p c t i", i=RUN)

        def subtract(dst, o, h, cols, engine):
            engine.tensor_tensor(dst, mean[o][h][:, :, cols], y_sb[o][h][:, :, cols], SUB)

        def weigh(o, h, cols, values):
            nc.vector.tensor_tensor(
                walk_words(by_word(g_flat[o][h])[:, cols, :]),
                walk_places(values),
                wt_psum[:, o, :].unsqueeze(1).unsqueeze(3).to_broadcast([P, (cols.stop - cols.start) // RUN, PACK, RUN]),
                MUL,
            )

        def finish_rows(places):
            for t in reversed(range(places.start, places.stop)):
                nc.vector.scalar_tensor_tensor(
                    last_rows[:, t, :], bank[4][:, t * P : (t + 1) * P], wt_sb[:, t : t + 1], weighed[:, t, :], MUL, SUB
                )

        def interleave_last_rows(cols):
            on_scalar(walk_words(by_word(g_flat[1][1])[:, cols, :]), walk_places(last_rows[:, :, cols]))

        def round_xm(c, o, copy, cols=slice(0, P)):
            copy(
                walk_words(by_word(xm_bf[c][:, o * K_PASS : (o + 1) * K_PASS])[:, cols, :]),
                walk_places(raw[c][o][:, :, cols]),
            )

        def quantize_xm(c, values):
            quantize(xm_codes[c][:].bitcast(E4M3), xm_sc[c][:], values)

        def quantize_side(o, h, e):
            quantize(
                g_codes[o][h][:, sides[e]].bitcast(E5M2),
                g_sc[o][h][:, sides[e]],
                g_flat[o][h][:, e * K_PASS : (e + 1) * K_PASS],
            )

        def quantize_g(o, h):
            for e in range(2):
                quantize_side(o, h, e)

        def multiply(c, h, b, order=(0, 1), cols=lo, at=None):
            for o in order:
                nc.tensor.matmul_mx(
                    out=bank[b][:, at or cols],
                    lhsT=xm_codes[c][:, o * P : (o + 1) * P].bitcast(E4M3),
                    lhsT_scale=xm_sc[c][:, o * P : (o + 1) * P],
                    rhs=g_codes[o][h][:, cols].bitcast(E5M2),
                    rhs_scale=g_sc[o][h][:, cols],
                    start=o == order[0],
                    stop=o == order[1],
                )

        def last_means():
            slots = slice(HALF, HALF + SIDE)
            nc.tensor.matmul_mx(
                out=bank[5][:],
                lhsT=w_codes[:, slots].bitcast(E4M3),
                lhsT_scale=w_sc[:, slots],
                rhs=xT_codes[1][:].bitcast(E4M3),
                rhs_scale=xT_sc[1][:],
                start=True,
                stop=True,
            )
            nc.scalar.activation(out=turned_means[:], in_=by_place(bank[5][:]), func=EXP)
            slots = slice(HALF + SIDE, N)
            for t in range(PACK):
                rows = slice(t * P, (t + 1) * P)
                nc.tensor.matmul_mx(
                    out=bank[1][:, rows],
                    lhsT=xT_codes[1][:, rows].bitcast(E4M3),
                    lhsT_scale=xT_sc[1][:, rows],
                    rhs=w_codes[:, slots].bitcast(E4M3),
                    rhs_scale=w_sc[:, slots],
                    start=True,
                    stop=True,
                )
            nc.scalar.activation(out=mean[1][1][:, :, sides[1]], in_=by_place(bank[1][:]), func=EXP)
            for t in range(PACK):
                nc.tensor.transpose(bank[4][:, t * P : (t + 1) * P], turned_means[:, t, :], identity[:])

        def drain_on_scalar(c, h, b, cols=lo):
            on_scalar(dw_sb[c][h][:, cols], bank[b][:, cols])

        def drain_on_vector(c, h, b):
            on_vector(dw_sb[c][h], bank[b][:, lo])

        def scatter_on_scalar(c, h):
            nc.scalar.activation(out=windows[c][:].indirect(entries(halves[h])), in_=dw_sb[c][h], func=COPY)

        def store(c):
            nc.sync.dma_start(out=out[c * P : (c + 1) * P, :], in_=windows[c][:])

        nc.gpsimd.memset(table_scales[:, : T // 8], 0)
        zero_on_vector(table_scales[:, T // 8 :])

        zero_on_vector(wt_rows[:])
        nc.sync.dma_start(offsets[:], offs)
        load_xT(0, 0)
        scale_rows = w_scales[0].bitcast(I32)
        for q in range(4):
            nc.sync.dma_start(out=table_scales[32 * q : 32 * q + 4, :], in_=scale_rows[4 * q : 4 * q + 4, :])
        nc.sync.dma_start(out=wt_rows[:PASSES, :], in_=wt[0].rearrange("(o k) one -> o (k one)", o=PASSES))
        load_xT(0, 1)
        nc.sync.dma_start(out=table_words[:], in_=w_words[0].rearrange("p n t -> p (n t)").bitcast(I32))
        load_xT(1, 0)
        load_xT(1, 1)
        load_y(0, 0)
        load_y(0, 1, slice(0, SIDE))
        load_y(1, 0)
        load_y(0, 1, slice(SIDE, HALF))
        load_xm(0, 0)
        load_y(1, 1, sides[0])
        load_xm(0, 1)
        load_xm(1, 0)
        load_xm(1, 1)
        load_y(1, 1, sides[1])
        load_late_xm()

        make_identity(nc, identity[:])
        zero_on_vector(windows[0][:].bitcast(I32))
        zero_on_vector(windows[1][:, K_PASS:].bitcast(I32))
        nc.gpsimd.memset(windows[1][:, :K_PASS].bitcast(I32), 0)
        for window in windows[2:]:
            nc.gpsimd.memset(window[:].bitcast(I32), 0)

        nc.vector.tensor_copy(w_sc[:], table_scales[:].bitcast(U8).indirect(offsets[:]))
        round_xT(0, 0, on_scalar_activation)
        for t in range(PACK):
            nc.tensor.transpose(bank[6][:, t * P : (t + 1) * P], wt_rows[:, t::PACK], identity[:])
        on_scalar(wt_sb[:], wt_psum[:, 1, :])
        round_xT(0, 1, on_scalar)
        quantize(xT_codes[0][:].bitcast(E4M3), xT_sc[0][:], xT_words[0][:].bitcast(BF16))
        for cols in halves:
            nc.vector.tensor_copy(w_codes[:, cols], table_words[:].bitcast(U32).indirect(entries(cols)))

        means(0, 0, slice(0, 1), 3)
        means(0, 0, slice(1, 2), 0)
        means(0, 0, pairs[1], 1)
        means(0, 1, pairs[0], 2)
        means(0, 1, pairs[1], 7)

        for h in range(2):
            for places in pairs:
                round_xT(1, h, on_vector, places)
            for t in range(PACK):
                cols = slice(t * P + h * P // 2, t * P + (h + 1) * P // 2)
                quantize(
                    xT_codes[1][:, cols].bitcast(E4M3), xT_sc[1][:, cols], late_xT[:, h, t].rearrange("p m j -> p (m j)")
                )

        for q, b in ((0, 3), (1, 0)):
            means(1, 0, pairs[q], b)
        last_means()
        for cols in sides:
            subtract(residual[0][:, :, cols], 0, 0, cols, nc.vector)
        subtract(high_residual[0], 0, 1, slice(0, EARLY), nc.gpsimd)
        for cols in sides:
            weigh(0, 0, cols, residual[0][:, :, cols])
        quantize_g(0, 0)
        for cols in reversed(sides):
            subtract(residual[1][:, :, cols], 1, 0, cols, nc.vector)
        subtract(high_residual[1], 0, 1, slice(EARLY, HALF), nc.gpsimd)
        for cols in reversed(sides):
            weigh(1, 0, cols, residual[1][:, :, cols])
        round_xm(0, 0, on_scalar)
        for t in reversed(range(PACK)):
            nc.scalar.activation(
                out=weighed[:, t, :], in_=y_sb[1][1][:, t, sides[0]], func=COPY, scale=wt_sb[:, t : t + 1]
            )
        finish_rows(pairs[1])
        for e in reversed(range(2)):
            quantize_side(1, 0, e)
        round_xm(0, 1, on_scalar)
        quantize_xm(0, xm_bf[0])
        subtract(by_place(last_residual), 1, 1, sides[1], nc.gpsimd)
        multiply(0, 0, 7)
        finish_rows(pairs[0])
        round_xm(1, 0, on_scalar)
        for cols in (slice(0, P // 2), slice(P // 2, P)):
            round_xm(1, 1, on_scalar, cols)
        interleave_last_rows(slice(0, SIDE // 2))
        drain_on_scalar(0, 0, 7)
        interleave_last_rows(slice(SIDE // 2, SIDE))
        scatter_on_scalar(0, 0)

        weigh(0, 1, slice(0, EARLY), high_residual[0])
        weigh(0, 1, slice(EARLY, HALF), high_residual[1])
        quantize_xm(1, xm_bf[1])
        weigh(1, 1, sides[1], by_place(last_residual))
        quantize(g_codes[0][1][:].bitcast(E5M2), g_sc[0][1][:], g_flat[0][1])
        multiply(1, 0, 2)
        for e, b in ((0, 0), (1, 3)):
            quantize_side(1, 1, e)
            multiply(0, 1, b, cols=sides[e])
            drain_on_scalar(0, 1, b, sides[e])
        scatter_on_scalar(0, 1)
        store(0)

        multiply(1, 1, 7, order=(1, 0))
        round_xm(2, 0, on_vector)
        for cols in (slice(0, P // 2), slice(P // 2, P)):
            round_xm(2, 1, on_vector, cols)
        drain_on_vector(1, 0, 2)
        quantize_xm(2, late_bf)
        on_vector(dw_sb[1][1][:, : HALF - TAIL], bank[7][:, : HALF - TAIL])
        nc.gpsimd.tensor_scalar(
            late_bf.rearrange("p (o i t) -> p o i t", o=PASSES, t=PACK),
            late_placed[:, :, :, sides[1]].rearrange("p o t i -> p o i t"),
            1.0,
            0.0,
            MUL,
            ADD,
        )
        nc.vector.tensor_copy(windows[1][:].indirect(entries(lo)), dw_sb[1][0])
        multiply(2, 0, 7, at=hi)
        multiply(2, 1, 1)
        on_scalar(dw2[:, : HALF - TAIL], bank[7][:, HALF : N - TAIL])
        on_scalar(tails, bank[7][:].rearrange("p (e w) -> p e w", e=2)[:, :, HALF - TAIL :])
        scatter_on_scalar(1, 1)
        store(1)
        drain_on_vector(2, 1, 1)
        quantize_xm(3, late_bf)
        nc.vector.tensor_copy(windows[2][:].indirect(offsets[:]), dw2)
        store(2)
        for h, b in ((0, 4), (1, 5)):
            multiply(3, h, b)
            drain_on_scalar(3, h, b)
        for h in range(2):
            scatter_on_scalar(3, h)
        store(3)
